import numpy as np
import ml_dtypes


def mxq(x, axis, fmt="e4m3"):
    dtype, down = {"e4m3": (ml_dtypes.float8_e4m3fn, 7), "e5m2": (ml_dtypes.float8_e5m2, 14)}[fmt]
    v = np.moveaxis(np.asarray(x, np.float32).astype(ml_dtypes.bfloat16).astype(np.float64), axis, -1)
    blocks = v.reshape(v.shape[:-1] + (-1, 32))
    amax = np.abs(blocks).max(-1, keepdims=True)
    byte = np.maximum(np.where(amax > 0, np.frexp(amax)[1] - 1 + 127, 0) - down, 1)
    scale = np.exp2(byte - 127.0)
    codes = (blocks / scale).astype(np.float32).astype(dtype).astype(np.float64)
    return np.moveaxis((codes * scale).reshape(v.shape), -1, axis)


WIDE = False


def mx_kscale(k):
    if not WIDE:
        return np.ones(k)
    levels = np.array([10, -10, 5, -5, 0])
    if k % 512:
        return np.exp2(np.random.permutation(np.resize(levels, k // 32))).repeat(32)
    a = np.empty((k // 512, 16))
    for p in range(k // 512):
        a[p, :8] = np.random.permutation(np.resize(levels, 8))
        for g in range(8):
            far = levels[np.abs(levels - a[p, g]) >= 10]
            a[p, g + 8] = far[np.random.randint(len(far))]
    return np.exp2(a.ravel()).repeat(32)


def f64(x):
    return np.asarray(x).astype(np.float64)


def striped(idx):
    return np.tile(idx.reshape(-1, 16).T, (8, 1)).astype(np.uint16)


def unstriped(offs):
    return offs[:16].T.reshape(-1).astype(np.int64)


E2M1 = np.array([0.0, 0.5, 1.0, 1.5, 2.0, 3.0, 4.0, 6.0, -0.0, -0.5, -1.0, -1.5, -2.0, -3.0, -4.0, -6.0])


def pack_weight(w, fmt):
    k, n = w.shape
    w = f64(np.asarray(w, np.float32).astype(ml_dtypes.bfloat16)).reshape(k // 32, 32, n)
    amax = np.abs(w).max(1)
    if fmt == "e4m3":
        byte = np.frexp(amax)[1] - 1 + 127 - 7
    else:
        mant, ex = np.frexp(amax / 6.0)
        byte = np.where(mant > 0.5, ex, ex - 1) + 127
    byte = np.clip(np.where(amax > 0, byte, 1), 1, 254)
    scaled = (w * np.exp2(127.0 - byte)[:, None, :]).reshape(k, n).astype(np.float32)
    by_word = np.ascontiguousarray(scaled.reshape(k // 512, 128, 4, n).transpose(0, 1, 3, 2))
    if fmt == "e4m3":
        words = by_word.astype(ml_dtypes.float8_e4m3fn).view(np.uint8)
    else:
        c = by_word.astype(ml_dtypes.float4_e2m1fn).view(np.uint8) & 0xF
        words = (c[..., 0::2] | (c[..., 1::2] << 4)).reshape(k // 512, 128, 2 * n)
    return np.ascontiguousarray(words), np.ascontiguousarray(byte.astype(np.uint8).reshape(k // 512, 16, n))


def unpack_weight(words, scales, fmt):
    g, _, n = scales.shape
    words = np.ascontiguousarray(words).reshape(g, 128, n, -1)
    if fmt == "e4m3":
        vals = words.view(ml_dtypes.float8_e4m3fn).astype(np.float64)
    else:
        nib = np.empty((g, 128, n, 4), np.uint8)
        nib[..., 0::2] = words & 0xF
        nib[..., 1::2] = words >> 4
        vals = E2M1[nib]
    vals = vals * np.repeat(np.exp2(scales.astype(np.float64) - 127.0), 8, axis=1)[..., None]
    return vals.transpose(0, 1, 3, 2).reshape(g * 512, n)


def gelu(v):
    return 0.5 * v * (1.0 + np.tanh(np.sqrt(2.0 / np.pi) * (v + 0.044715 * v**3)))


K, K3, H, N, T, T3, S = 512, 1024, 1024, 1024, 2048, 4096, 1024

def setup_inputs():
    n = np.random.standard_normal
    s1 = mx_kscale(K)[:, None]
    s3 = mx_kscale(K3)[:, None]
    u = mx_kscale(H)[:, None]
    tab_words, tab_scales = pack_weight(n((K, T)) * s1, "e4m3")
    tab2_words, tab2_scales = pack_weight(n((K, T)) * s1, "e4m3")
    tab3_words, tab3_scales = pack_weight(n((K3, T3)) * s3, "e2m1")
    w1_words, w1_scales = pack_weight(n((K, H)) / np.sqrt(K) / s1, "e2m1")
    w2 = (0.8 * n((K, H)) / np.sqrt(K) / s1).astype(np.float32)
    w3 = (n((K3, H)) / np.sqrt(K3) / s3 * u.T).astype(np.float32)
    w4_words, w4_scales = pack_weight(1.8 * n((H, N)) / np.sqrt(H) / u, "e4m3")
    return {"tab_words": tab_words, "tab_scales": tab_scales,
            "tab2_words": tab2_words, "tab2_scales": tab2_scales,
            "tab3_words": tab3_words, "tab3_scales": tab3_scales,
            "offs": striped(np.random.permutation(T)[:S]),
            "offs2": striped(np.random.permutation(T)[:S]),
            "offs3": striped(np.random.permutation(T3)[:S]),
            "w1_words": w1_words, "w1_scales": w1_scales, "w2": w2, "w3": w3,
            "w4_words": w4_words, "w4_scales": w4_scales,
            "gain": np.exp(0.3 * n(N)).astype(np.float32)}

def reference(tab_words, tab_scales, tab2_words, tab2_scales, tab3_words, tab3_scales,
              offs, offs2, offs3, w1_words, w1_scales, w2, w3, w4_words, w4_scales, gain):
    v = unpack_weight(tab_words, tab_scales, "e4m3")[:, unstriped(offs)]
    v2 = unpack_weight(tab2_words, tab2_scales, "e4m3")[:, unstriped(offs2)]
    v3 = unpack_weight(tab3_words, tab3_scales, "e2m1")[:, unstriped(offs3)]
    buyer = unpack_weight(w1_words, w1_scales, "e2m1").T @ v
    seller = mxq(f64(w2), 0, "e4m3").T @ v2
    house = mxq(f64(w3), 0, "e4m3").T @ v3
    h = house / (1.0 + np.exp(-(buyer + seller)))
    y = unpack_weight(w4_words, w4_scales, "e4m3").T @ mxq(h, 0, "e4m3")
    return f64(gain)[:, None] * np.tanh(y + seller)

@@ -1,0 +1,309 @@
+from contextlib import ExitStack
+
+import concourse.mybir as mybir
+
+K, K3, H, N, T, T3, S = 512, 1024, 1024, 1024, 2048, 4096, 1024
+FLOPS = 2 * S * (K * H + K * H + K3 * H + H * N)
+
+F32 = mybir.dt.float32
+BF16 = mybir.dt.bfloat16
+I32 = mybir.dt.int32
+U32 = mybir.dt.uint32
+U16 = mybir.dt.uint16
+U8 = mybir.dt.uint8
+FP8X4 = mybir.dt.float8_e4m3fn_x4
+FP4X4 = mybir.dt.float4_e2m1fn_x4
+ACT = mybir.ActivationFunctionType
+ALU = mybir.AluOpType
+
+P = 128
+HALF = 512
+UNIT = 128
+
+
+def tile_list_haggling_features_kernel(
+    tc, tab_words, tab_scales, tab2_words, tab2_scales, tab3_words, tab3_scales,
+    offs, offs2, offs3, w1_words, w1_scales, w2, w3, w4_words, w4_scales, gain, out,
+):
+    nc = tc.nc
+    with ExitStack() as ctx:
+        keep = ctx.enter_context(tc.tile_pool(name="keep", bufs=1))
+        ring = ctx.enter_context(tc.tile_pool(name="ring", bufs=1))
+        psum = ctx.enter_context(tc.psum_pool(name="psum", bufs=1))
+
+        def held(name, cols, dtype):
+            return keep.tile([P, cols], dtype, name=name, align_bytes=64)
+
+        turns = {}
+
+        def in_turn(pool, name, shape, dtype, slots):
+            turns[name] = turns.get(name, -1) + 1
+            tag = "%s%d" % (name, turns[name] % slots)
+            if pool is psum:
+                return pool.tile(shape, dtype, name=tag)
+            return pool.tile(shape, dtype, name=tag, align_bytes=64)
+
+        warm = held("warm", 8, F32)
+        nc.vector.memset(warm[:], 0.0)
+        nc.scalar.activation(warm[:, 1:2], warm[:, 0:1], ACT.Sigmoid)
+
+        seller_plane = held("seller_plane", T // 4, I32)
+        buyer_plane = held("buyer_plane", T // 4, I32)
+        house_plane = held("house_plane", T3 // 4, I32)
+        weight_plane_raw = held("weight_plane_raw", H // 4, I32)
+        for plane in (seller_plane, buyer_plane, house_plane, weight_plane_raw):
+            nc.vector.memset(plane[:], 0)
+
+        def load_plane(queue, plane, scales, row0):
+            rows = 4 * scales.shape[0]
+            for q in range(4):
+                src = scales[:, 4 * q:4 * q + 4, :] if rows > 4 else scales[0, 4 * q:4 * q + 4, :]
+                queue.dma_start(out=plane[32 * q + row0:32 * q + row0 + rows, :], in_=src.bitcast(I32))
+
+        def load_weight(w, a, b):
+            raw = in_turn(ring, "raw", [P, 4, HALF], F32, 4)
+            rows = w[512 * a:512 * (a + 1), HALF * b:HALF * (b + 1)]
+            nc.sync.dma_start(out=raw[:], in_=rows.rearrange("(p j) c -> p j c", j=4))
+            return raw
+
+        list2 = keep.tile([P, S // 16], U16, name="list2")
+        list1 = keep.tile([P, S // 16], U16, name="list1")
+        list3 = keep.tile([P, S // 16], U16, name="list3")
+        seller_tab = held("seller_tab", T, I32)
+        buyer_tab = held("buyer_tab", T, I32)
+        house_tab = [held("house_tab%d" % a, T3 // 2, I32) for a in range(2)]
+        w1_raw = held("w1_raw", H // 2, I32)
+        w4_raw = held("w4_raw", 2 * N, I32)
+        gains = held("gains", 8, F32)
+
+        nc.sync.dma_start(list2[:], offs2)
+        nc.sync.dma_start(list1[:], offs)
+        load_plane(nc.sync, seller_plane, tab2_scales, 0)
+        load_plane(nc.sync, buyer_plane, tab_scales, 0)
+        w2_raw = [load_weight(w2, 0, 0)]
+        nc.sync.dma_start(list3[:], offs3)
+        load_plane(nc.sync, house_plane, tab3_scales, 0)
+        nc.sync.dma_start(out=seller_tab[:], in_=tab2_words[0].rearrange("p t i -> p (t i)").bitcast(I32))
+        w2_raw.append(load_weight(w2, 0, 1))
+        nc.sync.dma_start(out=w1_raw[:], in_=w1_words[0].bitcast(I32))
+        load_plane(nc.sync, weight_plane_raw, w1_scales, 0)
+        nc.sync.dma_start(out=buyer_tab[:], in_=tab_words[0].rearrange("p t i -> p (t i)").bitcast(I32))
+        load_plane(nc.sync, weight_plane_raw, w4_scales, 4)
+        w3_raw = {}
+        w3_raw[0, 0] = load_weight(w3, 0, 0)
+
+        def gather(name, window, dtype, lst, j0, count):
+            picked = held(name, count, dtype)
+            nc.vector.tensor_copy(picked[:], window[:].bitcast(dtype).indirect(lst[:, j0 // 16:(j0 + count) // 16]))
+            return picked
+
+        def quantise_weight(name, raw):
+            rounded = in_turn(ring, "rounded", [P, 4 * HALF], BF16, 3)
+            nc.scalar.copy(
+                out=rounded[:].rearrange("p (t m j) -> p m j t", t=4, j=4),
+                in_=raw[:].rearrange("p j (m t) -> p m j t", t=4))
+            codes = held(name + "_codes", HALF, U32)
+            scales = held(name + "_scales", HALF, U8)
+            nc.vector.quantize_mx(out=codes[:].bitcast(FP8X4), scales=scales[:], in_=rounded[:])
+            return codes, scales
+
+        def permute(name, raw, dtype, cols):
+            ordered = held(name, cols, dtype)
+            nc.vector.tensor_copy(
+                out=ordered[:].rearrange("p (b t m) -> p b m t", t=4, m=P),
+                in_=raw[:].bitcast(dtype).rearrange("p (b m t) -> p b m t", t=4, m=P))
+            return ordered
+
+        seller_w, buyer_w = {}, {}
+        house_w = {}
+        w2q, w3q = {}, {}
+
+        seller_sc = gather("seller_sc", seller_plane, U8, list2, 0, S)
+        buyer_sc = gather("buyer_sc", buyer_plane, U8, list1, 0, S)
+        house_sc0 = gather("house_sc0", house_plane, U8, list3, 0, S)
+        w2q[0] = quantise_weight("w2_0", w2_raw[0])
+        for half in range(2):
+            seller_w[half] = gather("seller_w%d" % half, seller_tab, U32, list2, HALF * half, HALF)
+        w2q[1] = quantise_weight("w2_1", w2_raw[1])
+        w1_codes = permute("w1_codes", w1_raw, U16, H)
+        weight_plane = permute("weight_plane", weight_plane_raw, U8, H)
+        nc.sync.dma_start(out=weight_plane_raw[0:P - 4, :], in_=house_sc0[4:P, :].bitcast(I32))
+        house_sc = [house_sc0[:], weight_plane_raw[:].bitcast(U8)]
+        nc.sync.dma_start(out=house_tab[0][:], in_=tab3_words[0].bitcast(I32))
+        w3_raw[1, 0] = load_weight(w3, 1, 0)
+        nc.sync.dma_start(out=house_tab[1][:], in_=tab3_words[1].bitcast(I32))
+        nc.sync.dma_start(
+            out=w4_raw[:].rearrange("p (a c) -> p a c", a=2),
+            in_=w4_words.rearrange("a p c i -> p a (c i)").bitcast(I32))
+        nc.sync.dma_start(
+            out=gains[:].rearrange("p (b t) -> p b t", t=4),
+            in_=gain.rearrange("(b p t) -> p b t", b=2, t=4))
+        for a in range(2):
+            w3_raw[a, 1] = load_weight(w3, a, 1)
+
+        def seller_pass(dst, b, t, j0, n, start, stop):
+            codes, scales = w2q[b]
+            half, c0 = divmod(j0, HALF)
+            nc.tensor.matmul_mx(
+                out=dst, lhsT=codes[:, P * t:P * (t + 1)].bitcast(FP8X4), lhsT_scale=scales[:, P * t:P * (t + 1)],
+                rhs=seller_w[half][:, c0:c0 + n].bitcast(FP8X4), rhs_scale=seller_sc[:, j0:j0 + n],
+                start=start, stop=stop)
+
+        def buyer_pass(dst, b, t, j0, n, start, stop):
+            half, c0 = divmod(j0, HALF)
+            m0 = HALF * b + P * t
+            nc.tensor.matmul_mx(
+                out=dst, lhsT=w1_codes[:, m0:m0 + P].bitcast(FP4X4), lhsT_scale=weight_plane[:, m0:m0 + P],
+                rhs=buyer_w[half][:, c0:c0 + n].bitcast(FP8X4), rhs_scale=buyer_sc[:, j0:j0 + n],
+                start=start, stop=stop)
+
+        gate = {(b, half): held("gate%d%d" % (b, half), 4 * HALF, F32) for b in range(2) for half in range(2)}
+        kept = {}
+
+        def keep_seller():
+            for b in range(2):
+                for t in range(4):
+                    if (b, t) != (1, 3):
+                        bank = in_turn(psum, "bank", [P, HALF], F32, 4)
+                        seller_pass(bank[:], b, t, 0, HALF, True, True)
+                        kept[b, t] = held("kept%d%d" % (b, t), HALF, F32)
+                        nc.scalar.copy(out=kept[b, t][:], in_=bank[:])
+
+        def gate_first_half(b):
+            logits = held("logits%d" % b, 4 * HALF, F32)
+            for t in range(4):
+                row = logits[:, HALF * t:HALF * (t + 1)]
+                bank = in_turn(psum, "bank", [P, HALF], F32, 4)
+                if (b, t) in kept:
+                    buyer_pass(bank[:], b, t, 0, HALF, True, True)
+                    nc.vector.tensor_tensor(row, bank[:], kept[b, t][:], ALU.add)
+                else:
+                    seller_pass(bank[:], b, t, 0, HALF, True, False)
+                    buyer_pass(bank[:], b, t, 0, HALF, False, True)
+                    nc.scalar.copy(out=row, in_=bank[:])
+            nc.scalar.activation(
+                gate[b, 0][:].rearrange("p (c i t) -> p c t i", i=4, t=4),
+                logits[:].rearrange("p (t c i) -> p c t i", i=4, t=4), ACT.Sigmoid)
+
+        def gate_second_half(b):
+            for u in range(4):
+                bank = in_turn(psum, "bank", [P, HALF], F32, 4)
+                for t in range(4):
+                    dst = bank[:, UNIT * t:UNIT * (t + 1)]
+                    seller_pass(dst, b, t, HALF + UNIT * u, UNIT, True, False)
+                    buyer_pass(dst, b, t, HALF + UNIT * u, UNIT, False, True)
+                nc.scalar.activation(
+                    gate[b, 1][:, HALF * u:HALF * (u + 1)].rearrange("p (j t) -> p j t", t=4),
+                    bank[:].rearrange("p (t j) -> p j t", t=4), ACT.Sigmoid)
+
+        keep_seller()
+        w3q[0, 0] = quantise_weight("w3_00", w3_raw[0, 0])
+        for half in range(2):
+            buyer_w[half] = gather("buyer_w%d" % half, buyer_tab, U32, list1, HALF * half, HALF)
+        gate_first_half(0)
+        for half in range(2):
+            house_w[0, half] = gather("house_w0%d" % half, house_tab[0], U16, list3, HALF * half, HALF)
+        w3q[1, 0] = quantise_weight("w3_10", w3_raw[1, 0])
+        gate_first_half(1)
+        for half in range(2):
+            house_w[1, half] = gather("house_w1%d" % half, house_tab[1], U16, list3, HALF * half, HALF)
+        for a in range(2):
+            w3q[a, 1] = quantise_weight("w3_%d1" % a, w3_raw[a, 1])
+        gate_second_half(0)
+        gate_second_half(1)
+
+        h_codes = {(b, half): held("h_codes%d%d" % (b, half), HALF, U32) for b in range(2) for half in range(2)}
+        h_scales = {(b, half): held("h_scales%d%d" % (b, half), HALF, U8) for b in range(2) for half in range(2)}
+
+        def gated_pair(b, pair):
+            half, v = divmod(pair, 2)
+            rounded = in_turn(ring, "h_rounded", [P, 2 * HALF], BF16, 3)
+            for e in range(2):
+                u = 2 * v + e
+                bank = in_turn(psum, "house_bank", [P, HALF], F32, 4)
+                for t in range(4):
+                    for a in range(2):
+                        codes, scales = w3q[a, b]
+                        j0 = HALF * half + UNIT * u
+                        nc.tensor.matmul_mx(
+                            out=bank[:, UNIT * t:UNIT * (t + 1)],
+                            lhsT=codes[:, P * t:P * (t + 1)].bitcast(FP8X4), lhsT_scale=scales[:, P * t:P * (t + 1)],
+                            rhs=house_w[a, half][:, UNIT * u:UNIT * (u + 1)].bitcast(FP4X4),
+                            rhs_scale=house_sc[a][:, j0:j0 + UNIT],
+                            start=(a == 0), stop=(a == 1))
+                nc.vector.tensor_tensor(
+                    rounded[:, HALF * e:HALF * (e + 1)].rearrange("p (j t) -> p j t", t=4),
+                    bank[:].rearrange("p (t j) -> p j t", t=4),
+                    gate[b, half][:, HALF * u:HALF * (u + 1)].rearrange("p (j t) -> p j t", t=4), ALU.mult)
+            return rounded
+
+        def quantise_pair(b, pair, rounded):
+            half, v = divmod(pair, 2)
+            cols = slice(2 * UNIT * v, 2 * UNIT * (v + 1))
+            nc.vector.quantize_mx(
+                out=h_codes[b, half][:, cols].bitcast(FP8X4), scales=h_scales[b, half][:, cols], in_=rounded[:])
+
+        def mix_pass(dst, a, b, t, j0, n, start, stop):
+            half, c0 = divmod(j0, HALF)
+            m0 = HALF * b + P * t
+            nc.tensor.matmul_mx(
+                out=dst, lhsT=w4_codes[:, N * a + m0:N * a + m0 + P].bitcast(FP8X4),
+                lhsT_scale=weight_plane[4 + 4 * a:P, m0:m0 + P],
+                rhs=h_codes[a, half][:, c0:c0 + n].bitcast(FP8X4), rhs_scale=h_scales[a, half][:, c0:c0 + n],
+                start=start, stop=stop)
+
+        out_rows = out.rearrange("(b p t) j -> b p t j", b=2, t=4)
+
+        def apply_gain(dst, b, t):
+            nc.vector.tensor_scalar(dst, dst, gains[:, 4 * b + t:4 * b + t + 1], None, ALU.mult)
+
+        def output_first_half():
+            for b in range(2):
+                for t in range(4):
+                    bank = in_turn(psum, "bank", [P, HALF], F32, 4)
+                    res = in_turn(ring, "res", [P, HALF], F32, 6)
+                    again = (b, t) not in kept
+                    if again:
+                        seller_pass(bank[:], b, t, 0, HALF, True, False)
+                    for a in range(2):
+                        mix_pass(bank[:], a, b, t, 0, HALF, a == 0 and not again, a == 1)
+                    if again:
+                        nc.scalar.activation(res[:], bank[:], ACT.Tanh)
+                    else:
+                        nc.vector.tensor_tensor(res[:], bank[:], kept[b, t][:], ALU.add)
+                        nc.scalar.activation(res[:], res[:], ACT.Tanh)
+                    apply_gain(res[:], b, t)
+                    nc.sync.dma_start(out=out_rows[b, :, t, 0:HALF], in_=res[:])
+
+        def output_quarter(j0):
+            n = 2 * UNIT
+            for b in range(2):
+                for t0 in (0, 2):
+                    bank = in_turn(psum, "bank", [P, HALF], F32, 4)
+                    res = in_turn(ring, "res", [P, HALF], F32, 6)
+                    for e in range(2):
+                        seller_pass(bank[:, n * e:n * (e + 1)], b, t0 + e, j0, n, e == 0, False)
+                    for a in range(2):
+                        for e in range(2):
+                            mix_pass(bank[:, n * e:n * (e + 1)], a, b, t0 + e, j0, n, False, a == 1 and e == 1)
+                    nc.scalar.activation(res[:], bank[:], ACT.Tanh)
+                    for e in range(2):
+                        apply_gain(res[:, n * e:n * (e + 1)], b, t0 + e)
+                    nc.sync.dma_start(
+                        out=out_rows[b, :, t0:t0 + 2, j0:j0 + n], in_=res[:].rearrange("p (e j) -> p e j", e=2))
+
+        steps = [(0, 0), (0, 1), (1, 0), (1, 1), (0, 2), (1, 2), (0, 3), (1, 3)]
+        waiting = None
+        for b, pair in steps:
+            rounded = gated_pair(b, pair)
+            if waiting is not None:
+                quantise_pair(*waiting)
+            waiting = (b, pair, rounded)
+            if (b, pair) == (0, 1):
+                w4_codes = permute("w4_codes", w4_raw, I32, 2 * N)
+            if (b, pair) == (0, 2):
+                output_first_half()
+            if (b, pair) == (0, 3):
+                output_quarter(HALF)
+        quantise_pair(*waiting)
+        output_quarter(HALF + 2 * UNIT)

@@ -18,6 +18,7 @@ ALU = mybir.AluOpType
 
 P = 128
 HALF = 512
+QUARTER = 256
 UNIT = 128
 
 
@@ -31,17 +32,20 @@ def tile_list_haggling_features_kernel(
         ring = ctx.enter_context(tc.tile_pool(name="ring", bufs=1))
         psum = ctx.enter_context(tc.psum_pool(name="psum", bufs=1))
 
-        def held(name, cols, dtype):
-            return keep.tile([P, cols], dtype, name=name, align_bytes=64)
+        def held(name, cols, dtype, after=None):
+            return keep.tile([P, cols], dtype, name=name, tag=after or name, align_bytes=64)
 
         turns = {}
 
-        def in_turn(pool, name, shape, dtype, slots):
+        def slot_name(name, slots):
             turns[name] = turns.get(name, -1) + 1
-            tag = "%s%d" % (name, turns[name] % slots)
-            if pool is psum:
-                return pool.tile(shape, dtype, name=tag)
-            return pool.tile(shape, dtype, name=tag, align_bytes=64)
+            return "%s%d" % (name, turns[name] % slots)
+
+        def in_turn(name, cols, dtype, slots):
+            return ring.tile([P, cols], dtype, name=slot_name(name, slots), align_bytes=64)
+
+        def next_bank(name):
+            return psum.tile([P, HALF], F32, name=slot_name(name, 4))
 
         warm = held("warm", 8, F32)
         nc.vector.memset(warm[:], 0.0)
@@ -51,58 +55,68 @@ def tile_list_haggling_features_kernel(
         buyer_plane = held("buyer_plane", T // 4, I32)
         house_plane = held("house_plane", T3 // 4, I32)
         weight_plane_raw = held("weight_plane_raw", H // 4, I32)
-        for plane in (seller_plane, buyer_plane, house_plane, weight_plane_raw):
+        house_sc1 = held("house_sc1", S // 4, I32)
+        for plane in (seller_plane, buyer_plane, house_plane, weight_plane_raw, house_sc1):
             nc.vector.memset(plane[:], 0)
 
-        def load_plane(queue, plane, scales, row0):
+        def load_plane(plane, scales, row0, quads=range(4)):
             rows = 4 * scales.shape[0]
-            for q in range(4):
+            for q in quads:
                 src = scales[:, 4 * q:4 * q + 4, :] if rows > 4 else scales[0, 4 * q:4 * q + 4, :]
-                queue.dma_start(out=plane[32 * q + row0:32 * q + row0 + rows, :], in_=src.bitcast(I32))
+                nc.sync.dma_start(out=plane[32 * q + row0:32 * q + row0 + rows, :], in_=src.bitcast(I32))
 
-        def load_weight(w, a, b):
-            raw = in_turn(ring, "raw", [P, 4, HALF], F32, 4)
+        def load_weight(name, w, a, b, after=None):
+            raw = held(name, 4 * HALF, F32, after)
             rows = w[512 * a:512 * (a + 1), HALF * b:HALF * (b + 1)]
-            nc.sync.dma_start(out=raw[:], in_=rows.rearrange("(p j) c -> p j c", j=4))
+            nc.sync.dma_start(
+                out=raw[:].rearrange("p (j c) -> p j c", j=4), in_=rows.rearrange("(p j) c -> p j c", j=4))
             return raw
+
+        def load_words(name, words):
+            table = held(name, T, I32)
+            nc.sync.dma_start(out=table[:], in_=words.bitcast(I32))
+            return table
 
         list2 = keep.tile([P, S // 16], U16, name="list2")
         list1 = keep.tile([P, S // 16], U16, name="list1")
         list3 = keep.tile([P, S // 16], U16, name="list3")
-        seller_tab = held("seller_tab", T, I32)
-        buyer_tab = held("buyer_tab", T, I32)
-        house_tab = [held("house_tab%d" % a, T3 // 2, I32) for a in range(2)]
         w1_raw = held("w1_raw", H // 2, I32)
         w4_raw = held("w4_raw", 2 * N, I32)
         gains = held("gains", 8, F32)
+        w2_raw, w3_raw, house_tab = {}, {}, {}
 
         nc.sync.dma_start(list2[:], offs2)
         nc.sync.dma_start(list1[:], offs)
-        load_plane(nc.sync, seller_plane, tab2_scales, 0)
-        load_plane(nc.sync, buyer_plane, tab_scales, 0)
-        w2_raw = [load_weight(w2, 0, 0)]
+        load_plane(seller_plane, tab2_scales, 0)
+        load_plane(buyer_plane, tab_scales, 0, (0, 1))
+        w2_raw[0] = load_weight("w2_raw0", w2, 0, 0)
+        load_plane(buyer_plane, tab_scales, 0, (2, 3))
         nc.sync.dma_start(list3[:], offs3)
-        load_plane(nc.sync, house_plane, tab3_scales, 0)
-        nc.sync.dma_start(out=seller_tab[:], in_=tab2_words[0].rearrange("p t i -> p (t i)").bitcast(I32))
-        w2_raw.append(load_weight(w2, 0, 1))
+        load_plane(house_plane, tab3_scales, 0, (0, 1))
+        w2_raw[1] = load_weight("w2_raw1", w2, 0, 1)
+        load_plane(house_plane, tab3_scales, 0, (2, 3))
+        seller_tab = load_words("seller_tab", tab2_words[0].rearrange("p t i -> p (t i)"))
         nc.sync.dma_start(out=w1_raw[:], in_=w1_words[0].bitcast(I32))
-        load_plane(nc.sync, weight_plane_raw, w1_scales, 0)
-        nc.sync.dma_start(out=buyer_tab[:], in_=tab_words[0].rearrange("p t i -> p (t i)").bitcast(I32))
-        load_plane(nc.sync, weight_plane_raw, w4_scales, 4)
-        w3_raw = {}
-        w3_raw[0, 0] = load_weight(w3, 0, 0)
+        load_plane(weight_plane_raw, w1_scales, 0)
+        w3_raw[0, 0] = load_weight("w3_raw00", w3, 0, 0)
+        load_plane(weight_plane_raw, w4_scales, 4)
+        buyer_tab = load_words("buyer_tab", tab_words[0].rearrange("p t i -> p (t i)"))
+        w3_raw[1, 0] = load_weight("w3_raw10", w3, 1, 0)
+        house_tab[0] = load_words("house_tab0", tab3_words[0])
+        w3_raw[0, 1] = load_weight("w3_raw01", w3, 0, 1, "w2_raw0")
+        house_tab[1] = load_words("house_tab1", tab3_words[1])
 
         def gather(name, window, dtype, lst, j0, count):
             picked = held(name, count, dtype)
             nc.vector.tensor_copy(picked[:], window[:].bitcast(dtype).indirect(lst[:, j0 // 16:(j0 + count) // 16]))
             return picked
 
-        def quantise_weight(name, raw):
-            rounded = in_turn(ring, "rounded", [P, 4 * HALF], BF16, 3)
+        def quantise_weight(name, raw, after=None):
+            rounded = in_turn("rounded", 4 * HALF, BF16, 3)
             nc.scalar.copy(
                 out=rounded[:].rearrange("p (t m j) -> p m j t", t=4, j=4),
-                in_=raw[:].rearrange("p j (m t) -> p m j t", t=4))
-            codes = held(name + "_codes", HALF, U32)
+                in_=raw[:].rearrange("p (j m t) -> p m j t", t=4, j=4))
+            codes = held(name + "_codes", HALF, U32, after)
             scales = held(name + "_scales", HALF, U8)
             nc.vector.quantize_mx(out=codes[:].bitcast(FP8X4), scales=scales[:], in_=rounded[:])
             return codes, scales
@@ -114,32 +128,7 @@ def tile_list_haggling_features_kernel(
                 in_=raw[:].bitcast(dtype).rearrange("p (b m t) -> p b m t", t=4, m=P))
             return ordered
 
-        seller_w, buyer_w = {}, {}
-        house_w = {}
-        w2q, w3q = {}, {}
-
-        seller_sc = gather("seller_sc", seller_plane, U8, list2, 0, S)
-        buyer_sc = gather("buyer_sc", buyer_plane, U8, list1, 0, S)
-        house_sc0 = gather("house_sc0", house_plane, U8, list3, 0, S)
-        w2q[0] = quantise_weight("w2_0", w2_raw[0])
-        for half in range(2):
-            seller_w[half] = gather("seller_w%d" % half, seller_tab, U32, list2, HALF * half, HALF)
-        w2q[1] = quantise_weight("w2_1", w2_raw[1])
-        w1_codes = permute("w1_codes", w1_raw, U16, H)
-        weight_plane = permute("weight_plane", weight_plane_raw, U8, H)
-        nc.sync.dma_start(out=weight_plane_raw[0:P - 4, :], in_=house_sc0[4:P, :].bitcast(I32))
-        house_sc = [house_sc0[:], weight_plane_raw[:].bitcast(U8)]
-        nc.sync.dma_start(out=house_tab[0][:], in_=tab3_words[0].bitcast(I32))
-        w3_raw[1, 0] = load_weight(w3, 1, 0)
-        nc.sync.dma_start(out=house_tab[1][:], in_=tab3_words[1].bitcast(I32))
-        nc.sync.dma_start(
-            out=w4_raw[:].rearrange("p (a c) -> p a c", a=2),
-            in_=w4_words.rearrange("a p c i -> p a (c i)").bitcast(I32))
-        nc.sync.dma_start(
-            out=gains[:].rearrange("p (b t) -> p b t", t=4),
-            in_=gain.rearrange("(b p t) -> p b t", b=2, t=4))
-        for a in range(2):
-            w3_raw[a, 1] = load_weight(w3, a, 1)
+        seller_w, buyer_w, house_w, w2q, w3q, gate, kept = {}, {}, {}, {}, {}, {}, {}
 
         def seller_pass(dst, b, t, j0, n, start, stop):
             codes, scales = w2q[b]
@@ -157,26 +146,26 @@ def tile_list_haggling_features_kernel(
                 rhs=buyer_w[half][:, c0:c0 + n].bitcast(FP8X4), rhs_scale=buyer_sc[:, j0:j0 + n],
                 start=start, stop=stop)
 
-        gate = {(b, half): held("gate%d%d" % (b, half), 4 * HALF, F32) for b in range(2) for half in range(2)}
-        kept = {}
+        def is_kept(b, t):
+            return (b, t) != (1, 3)
 
-        def keep_seller():
-            for b in range(2):
-                for t in range(4):
-                    if (b, t) != (1, 3):
-                        bank = in_turn(psum, "bank", [P, HALF], F32, 4)
-                        seller_pass(bank[:], b, t, 0, HALF, True, True)
-                        kept[b, t] = held("kept%d%d" % (b, t), HALF, F32)
-                        nc.scalar.copy(out=kept[b, t][:], in_=bank[:])
+        def keep_seller(b):
+            kept[b] = held("kept%d" % b, 4 * HALF, F32, ("w3_raw00", None)[b])
+            for t in range(4):
+                if is_kept(b, t):
+                    bank = next_bank("bank")
+                    seller_pass(bank[:], b, t, 0, HALF, True, True)
+                    nc.scalar.copy(out=kept[b][:, HALF * t:HALF * (t + 1)], in_=bank[:])
 
         def gate_first_half(b):
             logits = held("logits%d" % b, 4 * HALF, F32)
+            gate[b, 0] = held("gate%d0" % b, 4 * HALF, F32, ("w3_raw10", "w2_raw0")[b])
             for t in range(4):
                 row = logits[:, HALF * t:HALF * (t + 1)]
-                bank = in_turn(psum, "bank", [P, HALF], F32, 4)
-                if (b, t) in kept:
+                bank = next_bank("bank")
+                if is_kept(b, t):
                     buyer_pass(bank[:], b, t, 0, HALF, True, True)
-                    nc.vector.tensor_tensor(row, bank[:], kept[b, t][:], ALU.add)
+                    nc.vector.tensor_tensor(row, bank[:], kept[b][:, HALF * t:HALF * (t + 1)], ALU.add)
                 else:
                     seller_pass(bank[:], b, t, 0, HALF, True, False)
                     buyer_pass(bank[:], b, t, 0, HALF, False, True)
@@ -186,8 +175,9 @@ def tile_list_haggling_features_kernel(
                 logits[:].rearrange("p (t c i) -> p c t i", i=4, t=4), ACT.Sigmoid)
 
         def gate_second_half(b):
+            gate[b, 1] = held("gate%d1" % b, 4 * HALF, F32, ("w2_raw1", None)[b])
             for u in range(4):
-                bank = in_turn(psum, "bank", [P, HALF], F32, 4)
+                bank = next_bank("bank")
                 for t in range(4):
                     dst = bank[:, UNIT * t:UNIT * (t + 1)]
                     seller_pass(dst, b, t, HALF + UNIT * u, UNIT, True, False)
@@ -196,31 +186,48 @@ def tile_list_haggling_features_kernel(
                     gate[b, 1][:, HALF * u:HALF * (u + 1)].rearrange("p (j t) -> p j t", t=4),
                     bank[:].rearrange("p (t j) -> p j t", t=4), ACT.Sigmoid)
 
-        keep_seller()
-        w3q[0, 0] = quantise_weight("w3_00", w3_raw[0, 0])
+        seller_sc = gather("seller_sc", seller_plane, U8, list2, 0, S)
+        buyer_sc = gather("buyer_sc", buyer_plane, U8, list1, 0, S)
+        w2q[0] = quantise_weight("w2_0", w2_raw[0])
+        house_sc0 = gather("house_sc0", house_plane, U8, list3, 0, S)
+        nc.sync.dma_start(out=house_sc1[0:P - 4, :], in_=house_sc0[4:P, :].bitcast(I32))
+        house_sc = [house_sc0[:], house_sc1[:].bitcast(U8)]
+        w3_raw[1, 1] = load_weight("w3_raw11", w3, 1, 1, "w2_raw1")
+        nc.sync.dma_start(
+            out=w4_raw[:].rearrange("p (a c) -> p a c", a=2),
+            in_=w4_words.rearrange("a p c i -> p a (c i)").bitcast(I32))
+        nc.sync.dma_start(
+            out=gains[:].rearrange("p (b t) -> p b t", t=4),
+            in_=gain.rearrange("(b p t) -> p b t", b=2, t=4))
+        for half in range(2):
+            seller_w[half] = gather("seller_w%d" % half, seller_tab, U32, list2, HALF * half, HALF)
+        w2q[1] = quantise_weight("w2_1", w2_raw[1], "house_plane")
+        w1_codes = permute("w1_codes", w1_raw, U16, H)
+        weight_plane = permute("weight_plane", weight_plane_raw, U8, H)
         for half in range(2):
             buyer_w[half] = gather("buyer_w%d" % half, buyer_tab, U32, list1, HALF * half, HALF)
-        gate_first_half(0)
+        w3q[0, 0] = quantise_weight("w3_00", w3_raw[0, 0], "buyer_tab")
+        keep_seller(0)
+        keep_seller(1)
         for half in range(2):
             house_w[0, half] = gather("house_w0%d" % half, house_tab[0], U16, list3, HALF * half, HALF)
-        w3q[1, 0] = quantise_weight("w3_10", w3_raw[1, 0])
-        gate_first_half(1)
+        w3q[1, 0] = quantise_weight("w3_10", w3_raw[1, 0], "house_tab0")
+        gate_first_half(0)
         for half in range(2):
             house_w[1, half] = gather("house_w1%d" % half, house_tab[1], U16, list3, HALF * half, HALF)
-        for a in range(2):
-            w3q[a, 1] = quantise_weight("w3_%d1" % a, w3_raw[a, 1])
-        gate_second_half(0)
-        gate_second_half(1)
+        w3q[0, 1] = quantise_weight("w3_01", w3_raw[0, 1], "house_tab1")
+        gate_first_half(1)
+        w3q[1, 1] = quantise_weight("w3_11", w3_raw[1, 1])
 
-        h_codes = {(b, half): held("h_codes%d%d" % (b, half), HALF, U32) for b in range(2) for half in range(2)}
-        h_scales = {(b, half): held("h_scales%d%d" % (b, half), HALF, U8) for b in range(2) for half in range(2)}
+        h_codes = {(b, q): held("h_codes%d%d" % (b, q), QUARTER, U32) for b in range(2) for q in range(4)}
+        h_scales = {(b, q): held("h_scales%d%d" % (b, q), QUARTER, U8) for b in range(2) for q in range(4)}
 
-        def gated_pair(b, pair):
-            half, v = divmod(pair, 2)
-            rounded = in_turn(ring, "h_rounded", [P, 2 * HALF], BF16, 3)
+        def gated_house(b, q):
+            half, v = divmod(q, 2)
+            rounded = in_turn("h_rounded", 2 * HALF, BF16, 3)
             for e in range(2):
                 u = 2 * v + e
-                bank = in_turn(psum, "house_bank", [P, HALF], F32, 4)
+                bank = next_bank("house_bank")
                 for t in range(4):
                     for a in range(2):
                         codes, scales = w3q[a, b]
@@ -237,73 +244,70 @@ def tile_list_haggling_features_kernel(
                     gate[b, half][:, HALF * u:HALF * (u + 1)].rearrange("p (j t) -> p j t", t=4), ALU.mult)
             return rounded
 
-        def quantise_pair(b, pair, rounded):
-            half, v = divmod(pair, 2)
-            cols = slice(2 * UNIT * v, 2 * UNIT * (v + 1))
-            nc.vector.quantize_mx(
-                out=h_codes[b, half][:, cols].bitcast(FP8X4), scales=h_scales[b, half][:, cols], in_=rounded[:])
+        def quantise_h(b, q, rounded):
+            nc.vector.quantize_mx(out=h_codes[b, q][:].bitcast(FP8X4), scales=h_scales[b, q][:], in_=rounded[:])
 
-        def mix_pass(dst, a, b, t, j0, n, start, stop):
-            half, c0 = divmod(j0, HALF)
+        def mix_pass(dst, a, b, t, q, start, stop):
             m0 = HALF * b + P * t
             nc.tensor.matmul_mx(
                 out=dst, lhsT=w4_codes[:, N * a + m0:N * a + m0 + P].bitcast(FP8X4),
                 lhsT_scale=weight_plane[4 + 4 * a:P, m0:m0 + P],
-                rhs=h_codes[a, half][:, c0:c0 + n].bitcast(FP8X4), rhs_scale=h_scales[a, half][:, c0:c0 + n],
+                rhs=h_codes[a, q][:].bitcast(FP8X4), rhs_scale=h_scales[a, q][:],
                 start=start, stop=stop)
 
         out_rows = out.rearrange("(b p t) j -> b p t j", b=2, t=4)
 
-        def apply_gain(dst, b, t):
-            nc.vector.tensor_scalar(dst, dst, gains[:, 4 * b + t:4 * b + t + 1], None, ALU.mult)
-
-        def output_first_half():
-            for b in range(2):
-                for t in range(4):
-                    bank = in_turn(psum, "bank", [P, HALF], F32, 4)
-                    res = in_turn(ring, "res", [P, HALF], F32, 6)
-                    again = (b, t) not in kept
-                    if again:
-                        seller_pass(bank[:], b, t, 0, HALF, True, False)
-                    for a in range(2):
-                        mix_pass(bank[:], a, b, t, 0, HALF, a == 0 and not again, a == 1)
-                    if again:
-                        nc.scalar.activation(res[:], bank[:], ACT.Tanh)
-                    else:
-                        nc.vector.tensor_tensor(res[:], bank[:], kept[b, t][:], ALU.add)
-                        nc.scalar.activation(res[:], res[:], ACT.Tanh)
-                    apply_gain(res[:], b, t)
-                    nc.sync.dma_start(out=out_rows[b, :, t, 0:HALF], in_=res[:])
-
-        def output_quarter(j0):
-            n = 2 * UNIT
+        def output_quarter(q):
+            n = QUARTER
+            j0 = n * q
             for b in range(2):
                 for t0 in (0, 2):
-                    bank = in_turn(psum, "bank", [P, HALF], F32, 4)
-                    res = in_turn(ring, "res", [P, HALF], F32, 6)
+                    bank = next_bank("bank")
+                    res = in_turn("res", HALF, F32, 6)
+                    again = [e for e in range(2) if q >= 2 or not is_kept(b, t0 + e)]
+                    passes = [(None, e) for e in again] + [(a, e) for a in range(2) for e in range(2)]
+                    for i, (a, e) in enumerate(passes):
+                        dst = bank[:, n * e:n * (e + 1)]
+                        if a is None:
+                            seller_pass(dst, b, t0 + e, j0, n, i == 0, False)
+                        else:
+                            mix_pass(dst, a, b, t0 + e, q, i == 0, i == len(passes) - 1)
+                    added = 2 - len(again)
+                    if added == 2:
+                        nc.vector.tensor_tensor(
+                            res[:].rearrange("p (e j) -> p e j", e=2), bank[:].rearrange("p (e j) -> p e j", e=2),
+                            kept[b][:].rearrange("p (t j) -> p t j", j=HALF)[:, t0:t0 + 2, j0:j0 + n], ALU.add)
+                        nc.scalar.activation(res[:], res[:], ACT.Tanh)
+                    elif added == 1:
+                        c0 = HALF * t0 + j0
+                        nc.vector.tensor_tensor(res[:, 0:n], bank[:, 0:n], kept[b][:, c0:c0 + n], ALU.add)
+                        nc.scalar.activation(res[:, n:2 * n], bank[:, n:2 * n], ACT.Tanh)
+                        nc.scalar.activation(res[:, 0:n], res[:, 0:n], ACT.Tanh)
+                    else:
+                        nc.scalar.activation(res[:], bank[:], ACT.Tanh)
                     for e in range(2):
-                        seller_pass(bank[:, n * e:n * (e + 1)], b, t0 + e, j0, n, e == 0, False)
-                    for a in range(2):
-                        for e in range(2):
-                            mix_pass(bank[:, n * e:n * (e + 1)], a, b, t0 + e, j0, n, False, a == 1 and e == 1)
-                    nc.scalar.activation(res[:], bank[:], ACT.Tanh)
-                    for e in range(2):
-                        apply_gain(res[:, n * e:n * (e + 1)], b, t0 + e)
+                        part = res[:, n * e:n * (e + 1)]
+                        col = gains[:, 4 * b + t0 + e:4 * b + t0 + e + 1]
+                        if q < 1:
+                            nc.scalar.activation(part, part, ACT.Copy, scale=col)
+                        else:
+                            nc.vector.tensor_scalar(part, part, col, None, ALU.mult)
                     nc.sync.dma_start(
                         out=out_rows[b, :, t0:t0 + 2, j0:j0 + n], in_=res[:].rearrange("p (e j) -> p e j", e=2))
 
-        steps = [(0, 0), (0, 1), (1, 0), (1, 1), (0, 2), (1, 2), (0, 3), (1, 3)]
         waiting = None
-        for b, pair in steps:
-            rounded = gated_pair(b, pair)
-            if waiting is not None:
-                quantise_pair(*waiting)
-            waiting = (b, pair, rounded)
-            if (b, pair) == (0, 1):
-                w4_codes = permute("w4_codes", w4_raw, I32, 2 * N)
-            if (b, pair) == (0, 2):
-                output_first_half()
-            if (b, pair) == (0, 3):
-                output_quarter(HALF)
-        quantise_pair(*waiting)
-        output_quarter(HALF + 2 * UNIT)
+        for q in range(4):
+            for b in range(2):
+                rounded = gated_house(b, q)
+                if waiting is not None:
+                    quantise_h(*waiting)
+                waiting = (b, q, rounded)
+                if (b, q) == (0, 0):
+                    w4_codes = permute("w4_codes", w4_raw, I32, 2 * N)
+                if (b, q) == (1, 0):
+                    gate_second_half(0)
+                    gate_second_half(1)
+            if q > 0:
+                output_quarter(q - 1)
+        quantise_h(*waiting)
+        output_quarter(3)

@@ -45,7 +45,7 @@ def tile_list_haggling_features_kernel(
             return ring.tile([P, cols], dtype, name=slot_name(name, slots), align_bytes=64)
 
         def next_bank(name):
-            return psum.tile([P, HALF], F32, name=slot_name(name, 4))
+            return psum.tile([P, HALF], F32, name=slot_name("bank", 8))
 
         warm = held("warm", 8, F32)
         nc.vector.memset(warm[:], 0.0)
@@ -55,8 +55,8 @@ def tile_list_haggling_features_kernel(
         buyer_plane = held("buyer_plane", T // 4, I32)
         house_plane = held("house_plane", T3 // 4, I32)
         weight_plane_raw = held("weight_plane_raw", H // 4, I32)
-        house_sc1 = held("house_sc1", S // 4, I32)
-        for plane in (seller_plane, buyer_plane, house_plane, weight_plane_raw, house_sc1):
+        table_planes = held("table_planes", S, I32)
+        for plane in (seller_plane, buyer_plane, house_plane, table_planes, weight_plane_raw):
             nc.vector.memset(plane[:], 0)
 
         def load_plane(plane, scales, row0, quads=range(4)):
@@ -64,6 +64,9 @@ def tile_list_haggling_features_kernel(
             for q in quads:
                 src = scales[:, 4 * q:4 * q + 4, :] if rows > 4 else scales[0, 4 * q:4 * q + 4, :]
                 nc.sync.dma_start(out=plane[32 * q + row0:32 * q + row0 + rows, :], in_=src.bitcast(I32))
+
+        def load_spread(plane, rows, first):
+            nc.sync.dma_start(out=plane[first:P:8, :], in_=rows.bitcast(I32))
 
         def load_weight(name, w, a, b, after=None):
             raw = held(name, 4 * HALF, F32, after)
@@ -87,29 +90,23 @@ def tile_list_haggling_features_kernel(
 
         nc.sync.dma_start(list2[:], offs2)
         nc.sync.dma_start(list1[:], offs)
-        load_plane(seller_plane, tab2_scales, 0)
-        load_plane(buyer_plane, tab_scales, 0, (0, 1))
-        w2_raw[0] = load_weight("w2_raw0", w2, 0, 0)
-        load_plane(buyer_plane, tab_scales, 0, (2, 3))
-        nc.sync.dma_start(list3[:], offs3)
-        load_plane(house_plane, tab3_scales, 0, (0, 1))
-        w2_raw[1] = load_weight("w2_raw1", w2, 0, 1)
-        load_plane(house_plane, tab3_scales, 0, (2, 3))
-        seller_tab = load_words("seller_tab", tab2_words[0].rearrange("p t i -> p (t i)"))
         nc.sync.dma_start(out=w1_raw[:], in_=w1_words[0].bitcast(I32))
-        load_plane(weight_plane_raw, w1_scales, 0)
-        w3_raw[0, 0] = load_weight("w3_raw00", w3, 0, 0)
-        load_plane(weight_plane_raw, w4_scales, 4)
-        buyer_tab = load_words("buyer_tab", tab_words[0].rearrange("p t i -> p (t i)"))
-        w3_raw[1, 0] = load_weight("w3_raw10", w3, 1, 0)
-        house_tab[0] = load_words("house_tab0", tab3_words[0])
-        w3_raw[0, 1] = load_weight("w3_raw01", w3, 0, 1, "w2_raw0")
-        house_tab[1] = load_words("house_tab1", tab3_words[1])
+        load_spread(seller_plane, tab2_scales[0], 0)
+        load_spread(buyer_plane, tab_scales[0], 0)
+        w2_raw[0] = load_weight("w2_raw0", w2, 0, 0)
+        nc.sync.dma_start(list3[:], offs3)
+        load_spread(house_plane, tab3_scales[0], 0)
+        load_spread(house_plane, tab3_scales[1], 4)
+        w2_raw[1] = load_weight("w2_raw1", w2, 0, 1)
+        seller_tab = load_words("seller_tab", tab2_words[0].rearrange("p t i -> p (t i)"))
 
         def gather(name, window, dtype, lst, j0, count):
             picked = held(name, count, dtype)
             nc.vector.tensor_copy(picked[:], window[:].bitcast(dtype).indirect(lst[:, j0 // 16:(j0 + count) // 16]))
             return picked
+
+        def gather_scales(dst, window, lst):
+            nc.vector.tensor_copy(dst, window[:].bitcast(U8).indirect(lst[:]))
 
         def quantise_weight(name, raw, after=None):
             rounded = in_turn("rounded", 4 * HALF, BF16, 3)
@@ -150,7 +147,7 @@ def tile_list_haggling_features_kernel(
             return (b, t) != (1, 3)
 
         def keep_seller(b):
-            kept[b] = held("kept%d" % b, 4 * HALF, F32, ("w3_raw00", None)[b])
+            kept[b] = held("kept%d" % b, 4 * HALF, F32, None)
             for t in range(4):
                 if is_kept(b, t):
                     bank = next_bank("bank")
@@ -159,7 +156,7 @@ def tile_list_haggling_features_kernel(
 
         def gate_first_half(b):
             logits = held("logits%d" % b, 4 * HALF, F32)
-            gate[b, 0] = held("gate%d0" % b, 4 * HALF, F32, ("w3_raw10", "w2_raw0")[b])
+            gate[b, 0] = held("gate%d0" % b, 4 * HALF, F32, ("w3_raw10", "w2_raw1")[b])
             for t in range(4):
                 row = logits[:, HALF * t:HALF * (t + 1)]
                 bank = next_bank("bank")
@@ -169,13 +166,13 @@ def tile_list_haggling_features_kernel(
                 else:
                     seller_pass(bank[:], b, t, 0, HALF, True, False)
                     buyer_pass(bank[:], b, t, 0, HALF, False, True)
-                    nc.scalar.copy(out=row, in_=bank[:])
+                    nc.vector.tensor_copy(row, bank[:])
             nc.scalar.activation(
                 gate[b, 0][:].rearrange("p (c i t) -> p c t i", i=4, t=4),
                 logits[:].rearrange("p (t c i) -> p c t i", i=4, t=4), ACT.Sigmoid)
 
         def gate_second_half(b):
-            gate[b, 1] = held("gate%d1" % b, 4 * HALF, F32, ("w2_raw1", None)[b])
+            gate[b, 1] = held("gate%d1" % b, 4 * HALF, F32, "logits%d" % b)
             for u in range(4):
                 bank = next_bank("bank")
                 for t in range(4):
@@ -186,12 +183,26 @@ def tile_list_haggling_features_kernel(
                     gate[b, 1][:, HALF * u:HALF * (u + 1)].rearrange("p (j t) -> p j t", t=4),
                     bank[:].rearrange("p (t j) -> p j t", t=4), ACT.Sigmoid)
 
-        seller_sc = gather("seller_sc", seller_plane, U8, list2, 0, S)
-        buyer_sc = gather("buyer_sc", buyer_plane, U8, list1, 0, S)
+        w1_codes = permute("w1_codes", w1_raw, U16, H)
+        pair_scales = held("pair_scales", 2 * S, U8)
+        gather_scales(pair_scales[:, 0:S], seller_plane, list2)
+        gather_scales(pair_scales[:, S:2 * S], buyer_plane, list1)
         w2q[0] = quantise_weight("w2_0", w2_raw[0])
-        house_sc0 = gather("house_sc0", house_plane, U8, list3, 0, S)
-        nc.sync.dma_start(out=house_sc1[0:P - 4, :], in_=house_sc0[4:P, :].bitcast(I32))
-        house_sc = [house_sc0[:], house_sc1[:].bitcast(U8)]
+        house_scales = gather("house_scales", house_plane, U8, list3, 0, S)
+        for i in range(4):
+            nc.sync.dma_start(out=table_planes[i:P:32, 0:S // 2], in_=pair_scales[8 * i:P:32, :].bitcast(I32))
+        load_plane(weight_plane_raw, w1_scales, 0)
+        load_plane(weight_plane_raw, w4_scales, 4)
+        buyer_tab = load_words("buyer_tab", tab_words[0].rearrange("p t i -> p (t i)"))
+        w3_raw[0, 0] = load_weight("w3_raw00", w3, 0, 0)
+        w3_raw[1, 0] = load_weight("w3_raw10", w3, 1, 0)
+        for a in range(2):
+            for i in range(4):
+                c0 = (2 + a) * S // 4
+                nc.sync.dma_start(
+                    out=table_planes[i:P:32, c0:c0 + S // 4], in_=house_scales[8 * i + 4 * a:P:32, :].bitcast(I32))
+            house_tab[a] = load_words("house_tab%d" % a, tab3_words[a])
+        w3_raw[0, 1] = load_weight("w3_raw01", w3, 0, 1, "w2_raw0")
         w3_raw[1, 1] = load_weight("w3_raw11", w3, 1, 1, "w2_raw1")
         nc.sync.dma_start(
             out=w4_raw[:].rearrange("p (a c) -> p a c", a=2),
@@ -199,25 +210,29 @@ def tile_list_haggling_features_kernel(
         nc.sync.dma_start(
             out=gains[:].rearrange("p (b t) -> p b t", t=4),
             in_=gain.rearrange("(b p t) -> p b t", b=2, t=4))
+        plane_bytes = table_planes[:].bitcast(U8)
+        seller_sc = plane_bytes[:, 0:S]
+        buyer_sc = plane_bytes[:, S:2 * S]
+        house_sc = [plane_bytes[:, 2 * S:3 * S], plane_bytes[:, 3 * S:4 * S]]
         for half in range(2):
             seller_w[half] = gather("seller_w%d" % half, seller_tab, U32, list2, HALF * half, HALF)
         w2q[1] = quantise_weight("w2_1", w2_raw[1], "house_plane")
-        w1_codes = permute("w1_codes", w1_raw, U16, H)
-        weight_plane = permute("weight_plane", weight_plane_raw, U8, H)
         for half in range(2):
             buyer_w[half] = gather("buyer_w%d" % half, buyer_tab, U32, list1, HALF * half, HALF)
-        w3q[0, 0] = quantise_weight("w3_00", w3_raw[0, 0], "buyer_tab")
+        weight_plane = permute("weight_plane", weight_plane_raw, U8, H)
         keep_seller(0)
         keep_seller(1)
+        w3q[0, 0] = quantise_weight("w3_00", w3_raw[0, 0])
         for half in range(2):
             house_w[0, half] = gather("house_w0%d" % half, house_tab[0], U16, list3, HALF * half, HALF)
         w3q[1, 0] = quantise_weight("w3_10", w3_raw[1, 0], "house_tab0")
-        gate_first_half(0)
         for half in range(2):
             house_w[1, half] = gather("house_w1%d" % half, house_tab[1], U16, list3, HALF * half, HALF)
-        w3q[0, 1] = quantise_weight("w3_01", w3_raw[0, 1], "house_tab1")
-        gate_first_half(1)
+        w3q[0, 1] = quantise_weight("w3_01", w3_raw[0, 1])
         w3q[1, 1] = quantise_weight("w3_11", w3_raw[1, 1])
+        gate_first_half(0)
+        gate_first_half(1)
+        gate_second_half(0)
 
         h_codes = {(b, q): held("h_codes%d%d" % (b, q), QUARTER, U32) for b in range(2) for q in range(4)}
         h_scales = {(b, q): held("h_scales%d%d" % (b, q), QUARTER, U8) for b in range(2) for q in range(4)}
@@ -263,7 +278,7 @@ def tile_list_haggling_features_kernel(
             for b in range(2):
                 for t0 in (0, 2):
                     bank = next_bank("bank")
-                    res = in_turn("res", HALF, F32, 6)
+                    res = in_turn("res", HALF, F32, 8)
                     again = [e for e in range(2) if q >= 2 or not is_kept(b, t0 + e)]
                     passes = [(None, e) for e in again] + [(a, e) for a in range(2) for e in range(2)]
                     for i, (a, e) in enumerate(passes):
@@ -295,19 +310,18 @@ def tile_list_haggling_features_kernel(
                     nc.sync.dma_start(
                         out=out_rows[b, :, t0:t0 + 2, j0:j0 + n], in_=res[:].rearrange("p (e j) -> p e j", e=2))
 
-        waiting = None
-        for q in range(4):
-            for b in range(2):
-                rounded = gated_house(b, q)
-                if waiting is not None:
-                    quantise_h(*waiting)
-                waiting = (b, q, rounded)
-                if (b, q) == (0, 0):
-                    w4_codes = permute("w4_codes", w4_raw, I32, 2 * N)
-                if (b, q) == (1, 0):
-                    gate_second_half(0)
-                    gate_second_half(1)
-            if q > 0:
-                output_quarter(q - 1)
-        quantise_h(*waiting)
+        def gated_pair(steps):
+            made = [(b, q, gated_house(b, q)) for b, q in steps]
+            for one in made:
+                quantise_h(*one)
+
+        gated_pair([(0, 0), (0, 1)])
+        w4_codes = permute("w4_codes", w4_raw, I32, 2 * N)
+        gated_pair([(1, 0), (1, 1)])
+        gate_second_half(1)
+        output_quarter(0)
+        gated_pair([(0, 2), (1, 2)])
+        output_quarter(1)
+        gated_pair([(0, 3), (1, 3)])
+        output_quarter(2)
         output_quarter(3)

@@ -55,8 +55,9 @@ def tile_list_haggling_features_kernel(
         buyer_plane = held("buyer_plane", T // 4, I32)
         house_plane = held("house_plane", T3 // 4, I32)
         weight_plane_raw = held("weight_plane_raw", H // 4, I32)
-        table_planes = held("table_planes", S, I32)
-        for plane in (seller_plane, buyer_plane, house_plane, table_planes, weight_plane_raw):
+        pair_planes = held("pair_planes", S // 2, I32)
+        house_planes = [held("house_planes%d" % a, S // 4, I32) for a in range(2)]
+        for plane in (seller_plane, buyer_plane, house_plane, pair_planes, weight_plane_raw, *house_planes):
             nc.vector.memset(plane[:], 0)
 
         def load_plane(plane, scales, row0, quads=range(4)):
@@ -164,9 +165,9 @@ def tile_list_haggling_features_kernel(
                     buyer_pass(bank[:], b, t, 0, HALF, True, True)
                     nc.vector.tensor_tensor(row, bank[:], kept[b][:, HALF * t:HALF * (t + 1)], ALU.add)
                 else:
-                    seller_pass(bank[:], b, t, 0, HALF, True, False)
-                    buyer_pass(bank[:], b, t, 0, HALF, False, True)
-                    nc.vector.tensor_copy(row, bank[:])
+                    buyer_pass(bank[:], b, t, 0, HALF, True, False)
+                    seller_pass(bank[:], b, t, 0, HALF, False, True)
+                    nc.scalar.copy(out=row, in_=bank[:])
             nc.scalar.activation(
                 gate[b, 0][:].rearrange("p (c i t) -> p c t i", i=4, t=4),
                 logits[:].rearrange("p (t c i) -> p c t i", i=4, t=4), ACT.Sigmoid)
@@ -190,7 +191,7 @@ def tile_list_haggling_features_kernel(
         w2q[0] = quantise_weight("w2_0", w2_raw[0])
         house_scales = gather("house_scales", house_plane, U8, list3, 0, S)
         for i in range(4):
-            nc.sync.dma_start(out=table_planes[i:P:32, 0:S // 2], in_=pair_scales[8 * i:P:32, :].bitcast(I32))
+            nc.sync.dma_start(out=pair_planes[i:P:32, :], in_=pair_scales[8 * i:P:32, :].bitcast(I32))
         load_plane(weight_plane_raw, w1_scales, 0)
         load_plane(weight_plane_raw, w4_scales, 4)
         buyer_tab = load_words("buyer_tab", tab_words[0].rearrange("p t i -> p (t i)"))
@@ -198,9 +199,8 @@ def tile_list_haggling_features_kernel(
         w3_raw[1, 0] = load_weight("w3_raw10", w3, 1, 0)
         for a in range(2):
             for i in range(4):
-                c0 = (2 + a) * S // 4
                 nc.sync.dma_start(
-                    out=table_planes[i:P:32, c0:c0 + S // 4], in_=house_scales[8 * i + 4 * a:P:32, :].bitcast(I32))
+                    out=house_planes[a][i:P:32, :], in_=house_scales[8 * i + 4 * a:P:32, :].bitcast(I32))
             house_tab[a] = load_words("house_tab%d" % a, tab3_words[a])
         w3_raw[0, 1] = load_weight("w3_raw01", w3, 0, 1, "w2_raw0")
         w3_raw[1, 1] = load_weight("w3_raw11", w3, 1, 1, "w2_raw1")
@@ -210,10 +210,10 @@ def tile_list_haggling_features_kernel(
         nc.sync.dma_start(
             out=gains[:].rearrange("p (b t) -> p b t", t=4),
             in_=gain.rearrange("(b p t) -> p b t", b=2, t=4))
-        plane_bytes = table_planes[:].bitcast(U8)
+        plane_bytes = pair_planes[:].bitcast(U8)
         seller_sc = plane_bytes[:, 0:S]
         buyer_sc = plane_bytes[:, S:2 * S]
-        house_sc = [plane_bytes[:, 2 * S:3 * S], plane_bytes[:, 3 * S:4 * S]]
+        house_sc = [plane[:].bitcast(U8) for plane in house_planes]
         for half in range(2):
             seller_w[half] = gather("seller_w%d" % half, seller_tab, U32, list2, HALF * half, HALF)
         w2q[1] = quantise_weight("w2_1", w2_raw[1], "house_plane")
@@ -237,30 +237,37 @@ def tile_list_haggling_features_kernel(
         h_codes = {(b, q): held("h_codes%d%d" % (b, q), QUARTER, U32) for b in range(2) for q in range(4)}
         h_scales = {(b, q): held("h_scales%d%d" % (b, q), QUARTER, U8) for b in range(2) for q in range(4)}
 
-        def gated_house(b, q):
+        house_banks, h_rounded = {}, {}
+
+        def house_passes(b, q):
             half, v = divmod(q, 2)
-            rounded = in_turn("h_rounded", 2 * HALF, BF16, 3)
             for e in range(2):
                 u = 2 * v + e
-                bank = next_bank("house_bank")
-                for t in range(4):
-                    for a in range(2):
+                j0 = HALF * half + UNIT * u
+                bank = next_bank("bank")
+                house_banks[b, q, e] = bank
+                for a in range(2):
+                    for t in range(4):
                         codes, scales = w3q[a, b]
-                        j0 = HALF * half + UNIT * u
                         nc.tensor.matmul_mx(
                             out=bank[:, UNIT * t:UNIT * (t + 1)],
                             lhsT=codes[:, P * t:P * (t + 1)].bitcast(FP8X4), lhsT_scale=scales[:, P * t:P * (t + 1)],
                             rhs=house_w[a, half][:, UNIT * u:UNIT * (u + 1)].bitcast(FP4X4),
                             rhs_scale=house_sc[a][:, j0:j0 + UNIT],
-                            start=(a == 0), stop=(a == 1))
-                nc.vector.tensor_tensor(
-                    rounded[:, HALF * e:HALF * (e + 1)].rearrange("p (j t) -> p j t", t=4),
-                    bank[:].rearrange("p (t j) -> p j t", t=4),
-                    gate[b, half][:, HALF * u:HALF * (u + 1)].rearrange("p (j t) -> p j t", t=4), ALU.mult)
-            return rounded
+                            start=(a == 0 and t == 0), stop=(a == 1 and t == 3))
 
-        def quantise_h(b, q, rounded):
-            nc.vector.quantize_mx(out=h_codes[b, q][:].bitcast(FP8X4), scales=h_scales[b, q][:], in_=rounded[:])
+        def apply_gate(b, q, after=None):
+            half, v = divmod(q, 2)
+            h_rounded[b, q] = held("h_rounded%d%d" % (b, q), 2 * HALF, BF16, after)
+            for e in range(2):
+                u = 2 * v + e
+                nc.vector.tensor_tensor(
+                    h_rounded[b, q][:, HALF * e:HALF * (e + 1)].rearrange("p (j t) -> p j t", t=4),
+                    house_banks[b, q, e][:].rearrange("p (t j) -> p j t", t=4),
+                    gate[b, half][:, HALF * u:HALF * (u + 1)].rearrange("p (j t) -> p j t", t=4), ALU.mult)
+
+        def quantise_h(b, q):
+            nc.vector.quantize_mx(out=h_codes[b, q][:].bitcast(FP8X4), scales=h_scales[b, q][:], in_=h_rounded[b, q][:])
 
         def mix_pass(dst, a, b, t, q, start, stop):
             m0 = HALF * b + P * t
@@ -303,7 +310,7 @@ def tile_list_haggling_features_kernel(
                     for e in range(2):
                         part = res[:, n * e:n * (e + 1)]
                         col = gains[:, 4 * b + t0 + e:4 * b + t0 + e + 1]
-                        if q < 1:
+                        if q == 0 or (q == 1 and b == 0):
                             nc.scalar.activation(part, part, ACT.Copy, scale=col)
                         else:
                             nc.vector.tensor_scalar(part, part, col, None, ALU.mult)
@@ -311,9 +318,11 @@ def tile_list_haggling_features_kernel(
                         out=out_rows[b, :, t0:t0 + 2, j0:j0 + n], in_=res[:].rearrange("p (e j) -> p e j", e=2))
 
         def gated_pair(steps):
-            made = [(b, q, gated_house(b, q)) for b, q in steps]
-            for one in made:
-                quantise_h(*one)
+            for b, q in steps:
+                house_passes(b, q)
+                apply_gate(b, q)
+            for b, q in steps:
+                quantise_h(b, q)
 
         gated_pair([(0, 0), (0, 1)])
         w4_codes = permute("w4_codes", w4_raw, I32, 2 * N)

@@ -17,9 +17,16 @@ ACT = mybir.ActivationFunctionType
 ALU = mybir.AluOpType
 
 P = 128
-HALF = 512
-QUARTER = 256
-UNIT = 128
+BANK = 512
+GROUP = 512
+HALF = S // 2
+QUARTER = S // 4
+UNIT = S // 8
+BANKS = 8
+ROUNDED_SLOTS = 3
+RESULT_SLOTS = 8
+REPEATED_SLICE = (1, 3)
+SCALAR_GAIN_BANKS = 6
 
 
 def tile_list_haggling_features_kernel(
@@ -44,34 +51,39 @@ def tile_list_haggling_features_kernel(
         def in_turn(name, cols, dtype, slots):
             return ring.tile([P, cols], dtype, name=slot_name(name, slots), align_bytes=64)
 
-        def next_bank(name):
-            return psum.tile([P, HALF], F32, name=slot_name("bank", 8))
+        def next_bank():
+            return psum.tile([P, BANK], F32, name=slot_name("bank", BANKS))
 
         warm = held("warm", 8, F32)
         nc.vector.memset(warm[:], 0.0)
         nc.scalar.activation(warm[:, 1:2], warm[:, 0:1], ACT.Sigmoid)
 
-        seller_plane = held("seller_plane", T // 4, I32)
-        buyer_plane = held("buyer_plane", T // 4, I32)
-        house_plane = held("house_plane", T3 // 4, I32)
+        seller_rows = held("seller_rows", T // 4, I32)
+        buyer_rows = held("buyer_rows", T // 4, I32)
+        house_rows = held("house_rows", T3 // 4, I32)
         weight_plane_raw = held("weight_plane_raw", H // 4, I32)
-        pair_planes = held("pair_planes", S // 2, I32)
+        pair_planes = held("pair_planes", 2 * S // 4, I32)
         house_planes = [held("house_planes%d" % a, S // 4, I32) for a in range(2)]
-        for plane in (seller_plane, buyer_plane, house_plane, pair_planes, weight_plane_raw, *house_planes):
-            nc.vector.memset(plane[:], 0)
+        for tile in (seller_rows, buyer_rows, house_rows, pair_planes, weight_plane_raw, *house_planes):
+            nc.vector.memset(tile[:], 0)
 
-        def load_plane(plane, scales, row0, quads=range(4)):
+        def load_plane(scales, row0):
             rows = 4 * scales.shape[0]
-            for q in quads:
-                src = scales[:, 4 * q:4 * q + 4, :] if rows > 4 else scales[0, 4 * q:4 * q + 4, :]
-                nc.sync.dma_start(out=plane[32 * q + row0:32 * q + row0 + rows, :], in_=src.bitcast(I32))
+            for quad in range(4):
+                src = scales[:, 4 * quad:4 * quad + 4, :] if rows > 4 else scales[0, 4 * quad:4 * quad + 4, :]
+                first = 32 * quad + row0
+                nc.sync.dma_start(out=weight_plane_raw[first:first + rows, :], in_=src.bitcast(I32))
 
-        def load_spread(plane, rows, first):
-            nc.sync.dma_start(out=plane[first:P:8, :], in_=rows.bitcast(I32))
+        def load_rows(tile, rows, first):
+            nc.sync.dma_start(out=tile[first:P:8, :], in_=rows.bitcast(I32))
+
+        def place_rows(plane, picked, first):
+            for i in range(4):
+                nc.sync.dma_start(out=plane[i:P:32, :], in_=picked[first + 8 * i:P:32, :].bitcast(I32))
 
         def load_weight(name, w, a, b, after=None):
-            raw = held(name, 4 * HALF, F32, after)
-            rows = w[512 * a:512 * (a + 1), HALF * b:HALF * (b + 1)]
+            raw = held(name, 4 * GROUP, F32, after)
+            rows = w[512 * a:512 * (a + 1), GROUP * b:GROUP * (b + 1)]
             nc.sync.dma_start(
                 out=raw[:].rearrange("p (j c) -> p j c", j=4), in_=rows.rearrange("(p j) c -> p j c", j=4))
             return raw
@@ -81,87 +93,90 @@ def tile_list_haggling_features_kernel(
             nc.sync.dma_start(out=table[:], in_=words.bitcast(I32))
             return table
 
-        list2 = keep.tile([P, S // 16], U16, name="list2")
-        list1 = keep.tile([P, S // 16], U16, name="list1")
-        list3 = keep.tile([P, S // 16], U16, name="list3")
+        seller_list = keep.tile([P, S // 16], U16, name="seller_list")
+        buyer_list = keep.tile([P, S // 16], U16, name="buyer_list")
+        house_list = keep.tile([P, S // 16], U16, name="house_list")
         w1_raw = held("w1_raw", H // 2, I32)
         w4_raw = held("w4_raw", 2 * N, I32)
         gains = held("gains", 8, F32)
         w2_raw, w3_raw, house_tab = {}, {}, {}
 
-        nc.sync.dma_start(list2[:], offs2)
-        nc.sync.dma_start(list1[:], offs)
+        nc.sync.dma_start(seller_list[:], offs2)
+        nc.sync.dma_start(buyer_list[:], offs)
         nc.sync.dma_start(out=w1_raw[:], in_=w1_words[0].bitcast(I32))
-        load_spread(seller_plane, tab2_scales[0], 0)
-        load_spread(buyer_plane, tab_scales[0], 0)
+        load_rows(seller_rows, tab2_scales[0], 0)
+        load_rows(buyer_rows, tab_scales[0], 0)
         w2_raw[0] = load_weight("w2_raw0", w2, 0, 0)
-        nc.sync.dma_start(list3[:], offs3)
-        load_spread(house_plane, tab3_scales[0], 0)
-        load_spread(house_plane, tab3_scales[1], 4)
+        nc.sync.dma_start(house_list[:], offs3)
+        load_rows(house_rows, tab3_scales[0], 0)
+        load_rows(house_rows, tab3_scales[1], 4)
         w2_raw[1] = load_weight("w2_raw1", w2, 0, 1)
+        load_plane(w1_scales, 0)
+        w3_raw[0, 0] = load_weight("w3_raw00", w3, 0, 0)
+        load_plane(w4_scales, 4)
         seller_tab = load_words("seller_tab", tab2_words[0].rearrange("p t i -> p (t i)"))
 
-        def gather(name, window, dtype, lst, j0, count):
-            picked = held(name, count, dtype)
-            nc.vector.tensor_copy(picked[:], window[:].bitcast(dtype).indirect(lst[:, j0 // 16:(j0 + count) // 16]))
-            return picked
+        def gather_into(dst, window, dtype, entries):
+            nc.vector.tensor_copy(dst, window[:].bitcast(dtype).indirect(entries))
 
-        def gather_scales(dst, window, lst):
-            nc.vector.tensor_copy(dst, window[:].bitcast(U8).indirect(lst[:]))
+        def gather_halves(name, window, dtype, lst):
+            halves = []
+            for half in range(2):
+                picked = held("%s%d" % (name, half), HALF, dtype)
+                gather_into(picked[:], window, dtype, lst[:, HALF * half // 16:HALF * (half + 1) // 16])
+                halves.append(picked)
+            return halves
 
         def quantise_weight(name, raw, after=None):
-            rounded = in_turn("rounded", 4 * HALF, BF16, 3)
+            rounded = in_turn("rounded", 4 * GROUP, BF16, ROUNDED_SLOTS)
             nc.scalar.copy(
                 out=rounded[:].rearrange("p (t m j) -> p m j t", t=4, j=4),
                 in_=raw[:].rearrange("p (j m t) -> p m j t", t=4, j=4))
-            codes = held(name + "_codes", HALF, U32, after)
-            scales = held(name + "_scales", HALF, U8)
+            codes = held(name + "_codes", GROUP, U32, after)
+            scales = held(name + "_scales", GROUP, U8)
             nc.vector.quantize_mx(out=codes[:].bitcast(FP8X4), scales=scales[:], in_=rounded[:])
             return codes, scales
 
-        def permute(name, raw, dtype, cols):
+        def reorder(name, raw, dtype, cols, run):
             ordered = held(name, cols, dtype)
             nc.vector.tensor_copy(
-                out=ordered[:].rearrange("p (b t m) -> p b m t", t=4, m=P),
-                in_=raw[:].bitcast(dtype).rearrange("p (b m t) -> p b m t", t=4, m=P))
+                out=ordered[:].rearrange("p (b t c i) -> p b c t i", t=4, c=P // run, i=run),
+                in_=raw[:].bitcast(dtype).rearrange("p (b c i t) -> p b c t i", t=4, c=P // run, i=run))
             return ordered
 
-        seller_w, buyer_w, house_w, w2q, w3q, gate, kept = {}, {}, {}, {}, {}, {}, {}
+        w2q, w3q, house_w, gate, kept = {}, {}, {}, {}, {}
 
         def seller_pass(dst, b, t, j0, n, start, stop):
             codes, scales = w2q[b]
             half, c0 = divmod(j0, HALF)
             nc.tensor.matmul_mx(
                 out=dst, lhsT=codes[:, P * t:P * (t + 1)].bitcast(FP8X4), lhsT_scale=scales[:, P * t:P * (t + 1)],
-                rhs=seller_w[half][:, c0:c0 + n].bitcast(FP8X4), rhs_scale=seller_sc[:, j0:j0 + n],
+                rhs=seller_w[half][:, c0:c0 + n].bitcast(FP8X4), rhs_scale=seller_plane[:, j0:j0 + n],
                 start=start, stop=stop)
 
         def buyer_pass(dst, b, t, j0, n, start, stop):
             half, c0 = divmod(j0, HALF)
-            m0 = HALF * b + P * t
+            m0 = GROUP * b + P * t
             nc.tensor.matmul_mx(
                 out=dst, lhsT=w1_codes[:, m0:m0 + P].bitcast(FP4X4), lhsT_scale=weight_plane[:, m0:m0 + P],
-                rhs=buyer_w[half][:, c0:c0 + n].bitcast(FP8X4), rhs_scale=buyer_sc[:, j0:j0 + n],
+                rhs=buyer_w[half][:, c0:c0 + n].bitcast(FP8X4), rhs_scale=buyer_plane[:, j0:j0 + n],
                 start=start, stop=stop)
 
-        def is_kept(b, t):
-            return (b, t) != (1, 3)
-
         def keep_seller(b):
-            kept[b] = held("kept%d" % b, 4 * HALF, F32, None)
+            kept[b] = held("kept%d" % b, 4 * HALF, F32)
             for t in range(4):
-                if is_kept(b, t):
-                    bank = next_bank("bank")
+                if (b, t) != REPEATED_SLICE:
+                    bank = next_bank()
                     seller_pass(bank[:], b, t, 0, HALF, True, True)
                     nc.scalar.copy(out=kept[b][:, HALF * t:HALF * (t + 1)], in_=bank[:])
 
-        def gate_first_half(b):
+        def gate_first_half(b, after):
             logits = held("logits%d" % b, 4 * HALF, F32)
-            gate[b, 0] = held("gate%d0" % b, 4 * HALF, F32, ("w3_raw10", "w2_raw1")[b])
+            gate[b, 0] = held("gate%d0" % b, 4 * HALF, F32, after)
             for t in range(4):
                 row = logits[:, HALF * t:HALF * (t + 1)]
-                bank = next_bank("bank")
-                if is_kept(b, t):
+                bank = next_bank()
+                if (b, t) != REPEATED_SLICE:
                     buyer_pass(bank[:], b, t, 0, HALF, True, True)
                     nc.vector.tensor_tensor(row, bank[:], kept[b][:, HALF * t:HALF * (t + 1)], ALU.add)
                 else:
@@ -175,102 +190,91 @@ def tile_list_haggling_features_kernel(
         def gate_second_half(b):
             gate[b, 1] = held("gate%d1" % b, 4 * HALF, F32, "logits%d" % b)
             for u in range(4):
-                bank = next_bank("bank")
+                bank = next_bank()
                 for t in range(4):
                     dst = bank[:, UNIT * t:UNIT * (t + 1)]
                     seller_pass(dst, b, t, HALF + UNIT * u, UNIT, True, False)
                     buyer_pass(dst, b, t, HALF + UNIT * u, UNIT, False, True)
                 nc.scalar.activation(
-                    gate[b, 1][:, HALF * u:HALF * (u + 1)].rearrange("p (j t) -> p j t", t=4),
+                    gate[b, 1][:, BANK * u:BANK * (u + 1)].rearrange("p (j t) -> p j t", t=4),
                     bank[:].rearrange("p (t j) -> p j t", t=4), ACT.Sigmoid)
 
-        w1_codes = permute("w1_codes", w1_raw, U16, H)
-        pair_scales = held("pair_scales", 2 * S, U8)
-        gather_scales(pair_scales[:, 0:S], seller_plane, list2)
-        gather_scales(pair_scales[:, S:2 * S], buyer_plane, list1)
+        w1_codes = reorder("w1_codes", w1_raw, U16, H, 8)
+        pair_picked = held("pair_picked", 2 * S, U8)
+        gather_into(pair_picked[:, 0:S], seller_rows, U8, seller_list[:])
+        gather_into(pair_picked[:, S:2 * S], buyer_rows, U8, buyer_list[:])
         w2q[0] = quantise_weight("w2_0", w2_raw[0])
-        house_scales = gather("house_scales", house_plane, U8, list3, 0, S)
-        for i in range(4):
-            nc.sync.dma_start(out=pair_planes[i:P:32, :], in_=pair_scales[8 * i:P:32, :].bitcast(I32))
-        load_plane(weight_plane_raw, w1_scales, 0)
-        load_plane(weight_plane_raw, w4_scales, 4)
+        house_picked = held("house_picked", S, U8)
+        gather_into(house_picked[:], house_rows, U8, house_list[:])
+        place_rows(pair_planes, pair_picked, 0)
+
         buyer_tab = load_words("buyer_tab", tab_words[0].rearrange("p t i -> p (t i)"))
-        w3_raw[0, 0] = load_weight("w3_raw00", w3, 0, 0)
         w3_raw[1, 0] = load_weight("w3_raw10", w3, 1, 0)
         for a in range(2):
-            for i in range(4):
-                nc.sync.dma_start(
-                    out=house_planes[a][i:P:32, :], in_=house_scales[8 * i + 4 * a:P:32, :].bitcast(I32))
+            place_rows(house_planes[a], house_picked, 4 * a)
             house_tab[a] = load_words("house_tab%d" % a, tab3_words[a])
-        w3_raw[0, 1] = load_weight("w3_raw01", w3, 0, 1, "w2_raw0")
-        w3_raw[1, 1] = load_weight("w3_raw11", w3, 1, 1, "w2_raw1")
+        for a in range(2):
+            w3_raw[a, 1] = load_weight("w3_raw%d1" % a, w3, a, 1, "w2_raw%d" % a)
         nc.sync.dma_start(
             out=w4_raw[:].rearrange("p (a c) -> p a c", a=2),
             in_=w4_words.rearrange("a p c i -> p a (c i)").bitcast(I32))
         nc.sync.dma_start(
             out=gains[:].rearrange("p (b t) -> p b t", t=4),
             in_=gain.rearrange("(b p t) -> p b t", b=2, t=4))
-        plane_bytes = pair_planes[:].bitcast(U8)
-        seller_sc = plane_bytes[:, 0:S]
-        buyer_sc = plane_bytes[:, S:2 * S]
-        house_sc = [plane[:].bitcast(U8) for plane in house_planes]
-        for half in range(2):
-            seller_w[half] = gather("seller_w%d" % half, seller_tab, U32, list2, HALF * half, HALF)
-        w2q[1] = quantise_weight("w2_1", w2_raw[1], "house_plane")
-        for half in range(2):
-            buyer_w[half] = gather("buyer_w%d" % half, buyer_tab, U32, list1, HALF * half, HALF)
-        weight_plane = permute("weight_plane", weight_plane_raw, U8, H)
-        keep_seller(0)
-        keep_seller(1)
-        w3q[0, 0] = quantise_weight("w3_00", w3_raw[0, 0])
-        for half in range(2):
-            house_w[0, half] = gather("house_w0%d" % half, house_tab[0], U16, list3, HALF * half, HALF)
+        seller_plane = pair_planes[:].bitcast(U8)[:, 0:S]
+        buyer_plane = pair_planes[:].bitcast(U8)[:, S:2 * S]
+
+        seller_w = gather_halves("seller_w", seller_tab, U32, seller_list)
+        w2q[1] = quantise_weight("w2_1", w2_raw[1], "house_rows")
+        buyer_w = gather_halves("buyer_w", buyer_tab, U32, buyer_list)
+        weight_plane = reorder("weight_plane", weight_plane_raw, U8, H, 16)
+        for b in range(2):
+            keep_seller(b)
+        w3q[0, 0] = quantise_weight("w3_00", w3_raw[0, 0], "seller_tab")
+        house_w[0] = gather_halves("house_w0", house_tab[0], U16, house_list)
         w3q[1, 0] = quantise_weight("w3_10", w3_raw[1, 0], "house_tab0")
-        for half in range(2):
-            house_w[1, half] = gather("house_w1%d" % half, house_tab[1], U16, list3, HALF * half, HALF)
-        w3q[0, 1] = quantise_weight("w3_01", w3_raw[0, 1])
-        w3q[1, 1] = quantise_weight("w3_11", w3_raw[1, 1])
-        gate_first_half(0)
-        gate_first_half(1)
+        house_w[1] = gather_halves("house_w1", house_tab[1], U16, house_list)
+        for a in range(2):
+            w3q[a, 1] = quantise_weight("w3_%d1" % a, w3_raw[a, 1])
+        gate_first_half(0, "w3_raw10")
+        gate_first_half(1, "w2_raw1")
         gate_second_half(0)
 
         h_codes = {(b, q): held("h_codes%d%d" % (b, q), QUARTER, U32) for b in range(2) for q in range(4)}
         h_scales = {(b, q): held("h_scales%d%d" % (b, q), QUARTER, U8) for b in range(2) for q in range(4)}
 
-        house_banks, h_rounded = {}, {}
-
-        def house_passes(b, q):
-            half, v = divmod(q, 2)
-            for e in range(2):
-                u = 2 * v + e
+        def gated_house(b, q):
+            half, first_unit = q // 2, 2 * (q % 2)
+            banks = []
+            for u in (first_unit, first_unit + 1):
                 j0 = HALF * half + UNIT * u
-                bank = next_bank("bank")
-                house_banks[b, q, e] = bank
+                bank = next_bank()
+                banks.append(bank)
                 for a in range(2):
+                    codes, scales = w3q[a, b]
                     for t in range(4):
-                        codes, scales = w3q[a, b]
                         nc.tensor.matmul_mx(
                             out=bank[:, UNIT * t:UNIT * (t + 1)],
                             lhsT=codes[:, P * t:P * (t + 1)].bitcast(FP8X4), lhsT_scale=scales[:, P * t:P * (t + 1)],
-                            rhs=house_w[a, half][:, UNIT * u:UNIT * (u + 1)].bitcast(FP4X4),
-                            rhs_scale=house_sc[a][:, j0:j0 + UNIT],
+                            rhs=house_w[a][half][:, UNIT * u:UNIT * (u + 1)].bitcast(FP4X4),
+                            rhs_scale=house_planes[a][:].bitcast(U8)[:, j0:j0 + UNIT],
                             start=(a == 0 and t == 0), stop=(a == 1 and t == 3))
-
-        def apply_gate(b, q, after=None):
-            half, v = divmod(q, 2)
-            h_rounded[b, q] = held("h_rounded%d%d" % (b, q), 2 * HALF, BF16, after)
-            for e in range(2):
-                u = 2 * v + e
+            h = held("h%d%d" % (b, q), 2 * BANK, BF16)
+            for e, bank in enumerate(banks):
+                u = first_unit + e
                 nc.vector.tensor_tensor(
-                    h_rounded[b, q][:, HALF * e:HALF * (e + 1)].rearrange("p (j t) -> p j t", t=4),
-                    house_banks[b, q, e][:].rearrange("p (t j) -> p j t", t=4),
-                    gate[b, half][:, HALF * u:HALF * (u + 1)].rearrange("p (j t) -> p j t", t=4), ALU.mult)
+                    h[:, BANK * e:BANK * (e + 1)].rearrange("p (j t) -> p j t", t=4),
+                    bank[:].rearrange("p (t j) -> p j t", t=4),
+                    gate[b, half][:, BANK * u:BANK * (u + 1)].rearrange("p (j t) -> p j t", t=4), ALU.mult)
+            return h
 
-        def quantise_h(b, q):
-            nc.vector.quantize_mx(out=h_codes[b, q][:].bitcast(FP8X4), scales=h_scales[b, q][:], in_=h_rounded[b, q][:])
+        def gated_pair(steps):
+            pieces = [gated_house(b, q) for b, q in steps]
+            for step, h in zip(steps, pieces):
+                nc.vector.quantize_mx(out=h_codes[step][:].bitcast(FP8X4), scales=h_scales[step][:], in_=h[:])
 
         def mix_pass(dst, a, b, t, q, start, stop):
-            m0 = HALF * b + P * t
+            m0 = GROUP * b + P * t
             nc.tensor.matmul_mx(
                 out=dst, lhsT=w4_codes[:, N * a + m0:N * a + m0 + P].bitcast(FP8X4),
                 lhsT_scale=weight_plane[4 + 4 * a:P, m0:m0 + P],
@@ -284,23 +288,21 @@ def tile_list_haggling_features_kernel(
             j0 = n * q
             for b in range(2):
                 for t0 in (0, 2):
-                    bank = next_bank("bank")
-                    res = in_turn("res", HALF, F32, 8)
-                    again = [e for e in range(2) if q >= 2 or not is_kept(b, t0 + e)]
-                    passes = [(None, e) for e in again] + [(a, e) for a in range(2) for e in range(2)]
-                    for i, (a, e) in enumerate(passes):
-                        dst = bank[:, n * e:n * (e + 1)]
-                        if a is None:
-                            seller_pass(dst, b, t0 + e, j0, n, i == 0, False)
-                        else:
-                            mix_pass(dst, a, b, t0 + e, q, i == 0, i == len(passes) - 1)
-                    added = 2 - len(again)
-                    if added == 2:
+                    bank = next_bank()
+                    res = in_turn("res", BANK, F32, RESULT_SLOTS)
+                    repeated = [e for e in range(2) if j0 >= HALF or (b, t0 + e) == REPEATED_SLICE]
+                    for e in repeated:
+                        seller_pass(bank[:, n * e:n * (e + 1)], b, t0 + e, j0, n, e == repeated[0], False)
+                    for a in range(2):
+                        for e in range(2):
+                            opens = not repeated and (a, e) == (0, 0)
+                            mix_pass(bank[:, n * e:n * (e + 1)], a, b, t0 + e, q, opens, (a, e) == (1, 1))
+                    if not repeated:
                         nc.vector.tensor_tensor(
                             res[:].rearrange("p (e j) -> p e j", e=2), bank[:].rearrange("p (e j) -> p e j", e=2),
                             kept[b][:].rearrange("p (t j) -> p t j", j=HALF)[:, t0:t0 + 2, j0:j0 + n], ALU.add)
                         nc.scalar.activation(res[:], res[:], ACT.Tanh)
-                    elif added == 1:
+                    elif repeated == [1]:
                         c0 = HALF * t0 + j0
                         nc.vector.tensor_tensor(res[:, 0:n], bank[:, 0:n], kept[b][:, c0:c0 + n], ALU.add)
                         nc.scalar.activation(res[:, n:2 * n], bank[:, n:2 * n], ACT.Tanh)
@@ -310,22 +312,15 @@ def tile_list_haggling_features_kernel(
                     for e in range(2):
                         part = res[:, n * e:n * (e + 1)]
                         col = gains[:, 4 * b + t0 + e:4 * b + t0 + e + 1]
-                        if q == 0 or (q == 1 and b == 0):
+                        if 4 * q + 2 * b + t0 // 2 < SCALAR_GAIN_BANKS:
                             nc.scalar.activation(part, part, ACT.Copy, scale=col)
                         else:
                             nc.vector.tensor_scalar(part, part, col, None, ALU.mult)
                     nc.sync.dma_start(
                         out=out_rows[b, :, t0:t0 + 2, j0:j0 + n], in_=res[:].rearrange("p (e j) -> p e j", e=2))
 
-        def gated_pair(steps):
-            for b, q in steps:
-                house_passes(b, q)
-                apply_gate(b, q)
-            for b, q in steps:
-                quantise_h(b, q)
-
         gated_pair([(0, 0), (0, 1)])
-        w4_codes = permute("w4_codes", w4_raw, I32, 2 * N)
+        w4_codes = reorder("w4_codes", w4_raw, I32, 2 * N, 4)
         gated_pair([(1, 0), (1, 1)])
         gate_second_half(1)
         output_quarter(0)

@@ -127,11 +127,16 @@ def tile_list_haggling_features_kernel(
                 halves.append(picked)
             return halves
 
-        def quantise_weight(name, raw, after=None):
+        def quantise_weight(name, raw, after=None, on_gpsimd=False):
             rounded = in_turn("rounded", 4 * GROUP, BF16, ROUNDED_SLOTS)
-            nc.scalar.copy(
-                out=rounded[:].rearrange("p (t m j) -> p m j t", t=4, j=4),
-                in_=raw[:].rearrange("p (j m t) -> p m j t", t=4, j=4))
+            if on_gpsimd:
+                nc.gpsimd.tensor_copy(
+                    out=rounded[:].rearrange("p (t m j) -> p t m j", t=4, j=4),
+                    in_=raw[:].rearrange("p (j m t) -> p t m j", t=4, j=4))
+            else:
+                nc.scalar.copy(
+                    out=rounded[:].rearrange("p (t m j) -> p m j t", t=4, j=4),
+                    in_=raw[:].rearrange("p (j m t) -> p m j t", t=4, j=4))
             codes = held(name + "_codes", GROUP, U32, after)
             scales = held(name + "_scales", GROUP, U8)
             nc.vector.quantize_mx(out=codes[:].bitcast(FP8X4), scales=scales[:], in_=rounded[:])
@@ -230,7 +235,7 @@ def tile_list_haggling_features_kernel(
         weight_plane = reorder("weight_plane", weight_plane_raw, U8, H, 16)
         for b in range(2):
             keep_seller(b)
-        w3q[0, 0] = quantise_weight("w3_00", w3_raw[0, 0], "seller_tab")
+        w3q[0, 0] = quantise_weight("w3_00", w3_raw[0, 0], "seller_tab", True)
         house_w[0] = gather_halves("house_w0", house_tab[0], U16, house_list)
         w3q[1, 0] = quantise_weight("w3_10", w3_raw[1, 0], "house_tab0")
         house_w[1] = gather_halves("house_w1", house_tab[1], U16, house_list)

@@ -20,13 +20,10 @@ P = 128
 BANK = 512
 GROUP = 512
 HALF = S // 2
-QUARTER = S // 4
 UNIT = S // 8
 BANKS = 8
-ROUNDED_SLOTS = 3
-RESULT_SLOTS = 8
+RESULT_SLOTS = 12
 REPEATED_SLICE = (1, 3)
-SCALAR_GAIN_BANKS = 6
 
 
 def tile_list_haggling_features_kernel(
@@ -54,36 +51,36 @@ def tile_list_haggling_features_kernel(
         def next_bank():
             return psum.tile([P, BANK], F32, name=slot_name("bank", BANKS))
 
-        warm = held("warm", 8, F32)
-        nc.vector.memset(warm[:], 0.0)
-        nc.scalar.activation(warm[:, 1:2], warm[:, 0:1], ACT.Sigmoid)
-
         seller_rows = held("seller_rows", T // 4, I32)
         buyer_rows = held("buyer_rows", T // 4, I32)
         house_rows = held("house_rows", T3 // 4, I32)
         weight_plane_raw = held("weight_plane_raw", H // 4, I32)
         pair_planes = held("pair_planes", 2 * S // 4, I32)
-        house_planes = [held("house_planes%d" % a, S // 4, I32) for a in range(2)]
-        for tile in (seller_rows, buyer_rows, house_rows, pair_planes, weight_plane_raw, *house_planes):
+        last_plane = held("last_plane", S // 4, I32)
+        for tile in (buyer_rows, seller_rows, house_rows, weight_plane_raw, pair_planes, last_plane):
             nc.vector.memset(tile[:], 0)
 
-        def load_plane(scales, row0):
+        warm = held("warm", 8, F32)
+        nc.gpsimd.memset(warm[:], 0.0)
+        nc.scalar.activation(warm[:, 1:2], warm[:, 0:1], ACT.Sigmoid)
+
+        def load_plane(tile, scales, row0, quads):
             rows = 4 * scales.shape[0]
-            for quad in range(4):
+            for quad in quads:
                 src = scales[:, 4 * quad:4 * quad + 4, :] if rows > 4 else scales[0, 4 * quad:4 * quad + 4, :]
                 first = 32 * quad + row0
-                nc.sync.dma_start(out=weight_plane_raw[first:first + rows, :], in_=src.bitcast(I32))
+                nc.sync.dma_start(out=tile[first:first + rows, :], in_=src.bitcast(I32))
 
         def load_rows(tile, rows, first):
             nc.sync.dma_start(out=tile[first:P:8, :], in_=rows.bitcast(I32))
 
-        def place_rows(plane, picked, first):
-            for i in range(4):
-                nc.sync.dma_start(out=plane[i:P:32, :], in_=picked[first + 8 * i:P:32, :].bitcast(I32))
+        def place_rows(plane, picked, first, rows):
+            for i in rows:
+                nc.sync.dma_start(out=plane[i:P:32, :], in_=picked.bitcast(I32)[first + 8 * i:P:32, :])
 
-        def load_weight(name, w, a, b, after=None):
-            raw = held(name, 4 * GROUP, F32, after)
-            rows = w[512 * a:512 * (a + 1), GROUP * b:GROUP * (b + 1)]
+        def load_weight(name, w, a, c0, cols=GROUP, after=None):
+            raw = held(name, 4 * cols, F32, after)
+            rows = w[512 * a:512 * (a + 1), c0:c0 + cols]
             nc.sync.dma_start(
                 out=raw[:].rearrange("p (j c) -> p j c", j=4), in_=rows.rearrange("(p j) c -> p j c", j=4))
             return raw
@@ -93,70 +90,58 @@ def tile_list_haggling_features_kernel(
             nc.sync.dma_start(out=table[:], in_=words.bitcast(I32))
             return table
 
+        def load_w4(b):
+            raw = held("w4_raw%d" % b, 2 * GROUP, I32)
+            words = w4_words[:, :, GROUP * b:GROUP * (b + 1), :]
+            nc.sync.dma_start(
+                out=raw[:].rearrange("p (a c) -> p a c", a=2), in_=words.rearrange("a p c i -> p a (c i)").bitcast(I32))
+            return raw
+
         seller_list = keep.tile([P, S // 16], U16, name="seller_list")
         buyer_list = keep.tile([P, S // 16], U16, name="buyer_list")
         house_list = keep.tile([P, S // 16], U16, name="house_list")
         w1_raw = held("w1_raw", H // 2, I32)
-        w4_raw = held("w4_raw", 2 * N, I32)
         gains = held("gains", 8, F32)
-        w2_raw, w3_raw, house_tab = {}, {}, {}
-
-        nc.sync.dma_start(seller_list[:], offs2)
-        nc.sync.dma_start(buyer_list[:], offs)
-        nc.sync.dma_start(out=w1_raw[:], in_=w1_words[0].bitcast(I32))
-        load_rows(seller_rows, tab2_scales[0], 0)
-        load_rows(buyer_rows, tab_scales[0], 0)
-        w2_raw[0] = load_weight("w2_raw0", w2, 0, 0)
-        nc.sync.dma_start(house_list[:], offs3)
-        load_rows(house_rows, tab3_scales[0], 0)
-        load_rows(house_rows, tab3_scales[1], 4)
-        w2_raw[1] = load_weight("w2_raw1", w2, 0, 1)
-        load_plane(w1_scales, 0)
-        w3_raw[0, 0] = load_weight("w3_raw00", w3, 0, 0)
-        load_plane(w4_scales, 4)
-        seller_tab = load_words("seller_tab", tab2_words[0].rearrange("p t i -> p (t i)"))
+        w2_raw, w3_raw, w4_raw, house_tab = {}, {}, {}, {}
 
         def gather_into(dst, window, dtype, entries):
             nc.vector.tensor_copy(dst, window[:].bitcast(dtype).indirect(entries))
 
-        def gather_halves(name, window, dtype, lst):
-            halves = []
-            for half in range(2):
-                picked = held("%s%d" % (name, half), HALF, dtype)
-                gather_into(picked[:], window, dtype, lst[:, HALF * half // 16:HALF * (half + 1) // 16])
-                halves.append(picked)
-            return halves
+        def gather_half(name, window, dtype, lst, half, after=None):
+            picked = held("%s%d" % (name, half), HALF, dtype, after)
+            gather_into(picked[:], window, dtype, lst[:, HALF * half // 16:HALF * (half + 1) // 16])
+            return picked
 
-        def quantise_weight(name, raw, after=None, on_gpsimd=False):
-            rounded = in_turn("rounded", 4 * GROUP, BF16, ROUNDED_SLOTS)
-            if on_gpsimd:
-                nc.gpsimd.tensor_copy(
-                    out=rounded[:].rearrange("p (t m j) -> p t m j", t=4, j=4),
-                    in_=raw[:].rearrange("p (j m t) -> p t m j", t=4, j=4))
-            else:
+        def round_weight(slot, *pieces):
+            rounded = held("rounded", 4 * GROUP, BF16, "slot%d" % slot)
+            span = P // len(pieces)
+            for e, raw in enumerate(pieces):
                 nc.scalar.copy(
-                    out=rounded[:].rearrange("p (t m j) -> p m j t", t=4, j=4),
+                    out=rounded[:].rearrange("p (t m j) -> p m j t", t=4, j=4)[:, span * e:span * (e + 1), :, :],
                     in_=raw[:].rearrange("p (j m t) -> p m j t", t=4, j=4))
+            return rounded
+
+        def quantise(name, rounded, after=None):
             codes = held(name + "_codes", GROUP, U32, after)
             scales = held(name + "_scales", GROUP, U8)
             nc.vector.quantize_mx(out=codes[:].bitcast(FP8X4), scales=scales[:], in_=rounded[:])
             return codes, scales
 
-        def reorder(name, raw, dtype, cols, run):
-            ordered = held(name, cols, dtype)
+        def reorder(name, raw, dtype, cols, run, after=None):
+            ordered = held(name, cols, dtype, after)
             nc.vector.tensor_copy(
                 out=ordered[:].rearrange("p (b t c i) -> p b c t i", t=4, c=P // run, i=run),
                 in_=raw[:].bitcast(dtype).rearrange("p (b c i t) -> p b c t i", t=4, c=P // run, i=run))
             return ordered
 
-        w2q, w3q, house_w, gate, kept = {}, {}, {}, {}, {}
+        w2q, w3q, w4_codes, seller_w, buyer_w, house_w, gate, kept, hq = {}, {}, {}, {}, {}, {}, {}, {}, {}
 
         def seller_pass(dst, b, t, j0, n, start, stop):
             codes, scales = w2q[b]
             half, c0 = divmod(j0, HALF)
             nc.tensor.matmul_mx(
                 out=dst, lhsT=codes[:, P * t:P * (t + 1)].bitcast(FP8X4), lhsT_scale=scales[:, P * t:P * (t + 1)],
-                rhs=seller_w[half][:, c0:c0 + n].bitcast(FP8X4), rhs_scale=seller_plane[:, j0:j0 + n],
+                rhs=seller_w[half][:, c0:c0 + n].bitcast(FP8X4), rhs_scale=seller_plane[4:P, j0:j0 + n],
                 start=start, stop=stop)
 
         def buyer_pass(dst, b, t, j0, n, start, stop):
@@ -167,170 +152,189 @@ def tile_list_haggling_features_kernel(
                 rhs=buyer_w[half][:, c0:c0 + n].bitcast(FP8X4), rhs_scale=buyer_plane[:, j0:j0 + n],
                 start=start, stop=stop)
 
-        def keep_seller(b):
-            kept[b] = held("kept%d" % b, 4 * HALF, F32)
+        def keep_seller(b, after=None):
+            kept[b] = held("kept%d" % b, 4 * HALF, F32, after)
             for t in range(4):
                 if (b, t) != REPEATED_SLICE:
                     bank = next_bank()
-                    seller_pass(bank[:], b, t, 0, HALF, True, True)
+                    seller_pass(bank[:], b, t, HALF, HALF, True, True)
                     nc.scalar.copy(out=kept[b][:, HALF * t:HALF * (t + 1)], in_=bank[:])
 
-        def gate_first_half(b, after):
-            logits = held("logits%d" % b, 4 * HALF, F32)
-            gate[b, 0] = held("gate%d0" % b, 4 * HALF, F32, after)
-            for t in range(4):
-                row = logits[:, HALF * t:HALF * (t + 1)]
-                bank = next_bank()
-                if (b, t) != REPEATED_SLICE:
-                    buyer_pass(bank[:], b, t, 0, HALF, True, True)
-                    nc.vector.tensor_tensor(row, bank[:], kept[b][:, HALF * t:HALF * (t + 1)], ALU.add)
-                else:
-                    buyer_pass(bank[:], b, t, 0, HALF, True, False)
-                    seller_pass(bank[:], b, t, 0, HALF, False, True)
-                    nc.scalar.copy(out=row, in_=bank[:])
-            nc.scalar.activation(
-                gate[b, 0][:].rearrange("p (c i t) -> p c t i", i=4, t=4),
-                logits[:].rearrange("p (t c i) -> p c t i", i=4, t=4), ACT.Sigmoid)
-
-        def gate_second_half(b):
-            gate[b, 1] = held("gate%d1" % b, 4 * HALF, F32, "logits%d" % b)
+        def gate_first_half(b):
+            gate[b, 0] = held("gate%d0" % b, 4 * HALF, F32)
             for u in range(4):
                 bank = next_bank()
                 for t in range(4):
-                    dst = bank[:, UNIT * t:UNIT * (t + 1)]
-                    seller_pass(dst, b, t, HALF + UNIT * u, UNIT, True, False)
-                    buyer_pass(dst, b, t, HALF + UNIT * u, UNIT, False, True)
+                    seller_pass(bank[:, UNIT * t:UNIT * (t + 1)], b, t, UNIT * u, UNIT, t == 0, False)
+                for t in range(4):
+                    buyer_pass(bank[:, UNIT * t:UNIT * (t + 1)], b, t, UNIT * u, UNIT, False, t == 3)
                 nc.scalar.activation(
-                    gate[b, 1][:, BANK * u:BANK * (u + 1)].rearrange("p (j t) -> p j t", t=4),
+                    gate[b, 0][:, BANK * u:BANK * (u + 1)].rearrange("p (j t) -> p j t", t=4),
                     bank[:].rearrange("p (t j) -> p j t", t=4), ACT.Sigmoid)
 
-        w1_codes = reorder("w1_codes", w1_raw, U16, H, 8)
-        pair_picked = held("pair_picked", 2 * S, U8)
-        gather_into(pair_picked[:, 0:S], seller_rows, U8, seller_list[:])
-        gather_into(pair_picked[:, S:2 * S], buyer_rows, U8, buyer_list[:])
-        w2q[0] = quantise_weight("w2_0", w2_raw[0])
-        house_picked = held("house_picked", S, U8)
-        gather_into(house_picked[:], house_rows, U8, house_list[:])
-        place_rows(pair_planes, pair_picked, 0)
+        def kept_logits(logits, b):
+            for t in range(4):
+                if (b, t) != REPEATED_SLICE:
+                    bank = next_bank()
+                    buyer_pass(bank[:], b, t, HALF, HALF, True, True)
+                    nc.vector.tensor_tensor(
+                        logits[:, HALF * t:HALF * (t + 1)], bank[:], kept[b][:, HALF * t:HALF * (t + 1)], ALU.add)
 
-        buyer_tab = load_words("buyer_tab", tab_words[0].rearrange("p t i -> p (t i)"))
-        w3_raw[1, 0] = load_weight("w3_raw10", w3, 1, 0)
-        for a in range(2):
-            place_rows(house_planes[a], house_picked, 4 * a)
-            house_tab[a] = load_words("house_tab%d" % a, tab3_words[a])
-        for a in range(2):
-            w3_raw[a, 1] = load_weight("w3_raw%d1" % a, w3, a, 1, "w2_raw%d" % a)
-        nc.sync.dma_start(
-            out=w4_raw[:].rearrange("p (a c) -> p a c", a=2),
-            in_=w4_words.rearrange("a p c i -> p a (c i)").bitcast(I32))
-        nc.sync.dma_start(
-            out=gains[:].rearrange("p (b t) -> p b t", t=4),
-            in_=gain.rearrange("(b p t) -> p b t", b=2, t=4))
-        seller_plane = pair_planes[:].bitcast(U8)[:, 0:S]
-        buyer_plane = pair_planes[:].bitcast(U8)[:, S:2 * S]
+        def repeated_logits(logits):
+            b, t = REPEATED_SLICE
+            bank = next_bank()
+            buyer_pass(bank[:], b, t, HALF, HALF, True, False)
+            seller_pass(bank[:], b, t, HALF, HALF, False, True)
+            nc.scalar.copy(out=logits[:, HALF * t:HALF * (t + 1)], in_=bank[:])
 
-        seller_w = gather_halves("seller_w", seller_tab, U32, seller_list)
-        w2q[1] = quantise_weight("w2_1", w2_raw[1], "house_rows")
-        buyer_w = gather_halves("buyer_w", buyer_tab, U32, buyer_list)
-        weight_plane = reorder("weight_plane", weight_plane_raw, U8, H, 16)
-        for b in range(2):
-            keep_seller(b)
-        w3q[0, 0] = quantise_weight("w3_00", w3_raw[0, 0], "seller_tab", True)
-        house_w[0] = gather_halves("house_w0", house_tab[0], U16, house_list)
-        w3q[1, 0] = quantise_weight("w3_10", w3_raw[1, 0], "house_tab0")
-        house_w[1] = gather_halves("house_w1", house_tab[1], U16, house_list)
-        for a in range(2):
-            w3q[a, 1] = quantise_weight("w3_%d1" % a, w3_raw[a, 1])
-        gate_first_half(0, "w3_raw10")
-        gate_first_half(1, "w2_raw1")
-        gate_second_half(0)
+        def gate_second_half(b, logits, after):
+            gate[b, 1] = held("gate%d1" % b, 4 * HALF, F32, after)
+            nc.scalar.activation(
+                gate[b, 1][:].rearrange("p (c i t) -> p c t i", i=4, t=4),
+                logits.rearrange("p (t c i) -> p c t i", i=4, t=4), ACT.Sigmoid)
 
-        h_codes = {(b, q): held("h_codes%d%d" % (b, q), QUARTER, U32) for b in range(2) for q in range(4)}
-        h_scales = {(b, q): held("h_scales%d%d" % (b, q), QUARTER, U8) for b in range(2) for q in range(4)}
+        h_rounded = {}
 
-        def gated_house(b, q):
-            half, first_unit = q // 2, 2 * (q % 2)
-            banks = []
-            for u in (first_unit, first_unit + 1):
-                j0 = HALF * half + UNIT * u
-                bank = next_bank()
-                banks.append(bank)
-                for a in range(2):
-                    codes, scales = w3q[a, b]
-                    for t in range(4):
-                        nc.tensor.matmul_mx(
-                            out=bank[:, UNIT * t:UNIT * (t + 1)],
-                            lhsT=codes[:, P * t:P * (t + 1)].bitcast(FP8X4), lhsT_scale=scales[:, P * t:P * (t + 1)],
-                            rhs=house_w[a][half][:, UNIT * u:UNIT * (u + 1)].bitcast(FP4X4),
-                            rhs_scale=house_planes[a][:].bitcast(U8)[:, j0:j0 + UNIT],
-                            start=(a == 0 and t == 0), stop=(a == 1 and t == 3))
-            h = held("h%d%d" % (b, q), 2 * BANK, BF16)
-            for e, bank in enumerate(banks):
-                u = first_unit + e
-                nc.vector.tensor_tensor(
-                    h[:, BANK * e:BANK * (e + 1)].rearrange("p (j t) -> p j t", t=4),
-                    bank[:].rearrange("p (t j) -> p j t", t=4),
-                    gate[b, half][:, BANK * u:BANK * (u + 1)].rearrange("p (j t) -> p j t", t=4), ALU.mult)
-            return h
+        def gated_unit(b, half, u):
+            if u == 0:
+                h_rounded[b, half] = held("h%d%d" % (b, half), 4 * HALF, BF16)
+            j0 = HALF * half + UNIT * u
+            bank = next_bank()
+            for a in range(2):
+                codes, scales = w3q[a, b]
+                for t in range(4):
+                    nc.tensor.matmul_mx(
+                        out=bank[:, UNIT * t:UNIT * (t + 1)],
+                        lhsT=codes[:, P * t:P * (t + 1)].bitcast(FP8X4), lhsT_scale=scales[:, P * t:P * (t + 1)],
+                        rhs=house_w[a, half][:, UNIT * u:UNIT * (u + 1)].bitcast(FP4X4),
+                        rhs_scale=house_plane[a][:, j0:j0 + UNIT],
+                        start=(a == 0 and t == 0), stop=(a == 1 and t == 3))
+            nc.vector.tensor_tensor(
+                h_rounded[b, half][:, BANK * u:BANK * (u + 1)].rearrange("p (j t) -> p j t", t=4),
+                bank[:].rearrange("p (t j) -> p j t", t=4),
+                gate[b, half][:, BANK * u:BANK * (u + 1)].rearrange("p (j t) -> p j t", t=4), ALU.mult)
 
-        def gated_pair(steps):
-            pieces = [gated_house(b, q) for b, q in steps]
-            for step, h in zip(steps, pieces):
-                nc.vector.quantize_mx(out=h_codes[step][:].bitcast(FP8X4), scales=h_scales[step][:], in_=h[:])
-
-        def mix_pass(dst, a, b, t, q, start, stop):
-            m0 = GROUP * b + P * t
-            nc.tensor.matmul_mx(
-                out=dst, lhsT=w4_codes[:, N * a + m0:N * a + m0 + P].bitcast(FP8X4),
-                lhsT_scale=weight_plane[4 + 4 * a:P, m0:m0 + P],
-                rhs=h_codes[a, q][:].bitcast(FP8X4), rhs_scale=h_scales[a, q][:],
-                start=start, stop=stop)
+        def quantise_h(b, half):
+            hq[b, half] = quantise("h%d%d" % (b, half), h_rounded[b, half])
 
         out_rows = out.rearrange("(b p t) j -> b p t j", b=2, t=4)
 
-        def output_quarter(q):
-            n = QUARTER
-            j0 = n * q
-            for b in range(2):
-                for t0 in (0, 2):
-                    bank = next_bank()
-                    res = in_turn("res", BANK, F32, RESULT_SLOTS)
-                    repeated = [e for e in range(2) if j0 >= HALF or (b, t0 + e) == REPEATED_SLICE]
-                    for e in repeated:
-                        seller_pass(bank[:, n * e:n * (e + 1)], b, t0 + e, j0, n, e == repeated[0], False)
-                    for a in range(2):
-                        for e in range(2):
-                            opens = not repeated and (a, e) == (0, 0)
-                            mix_pass(bank[:, n * e:n * (e + 1)], a, b, t0 + e, q, opens, (a, e) == (1, 1))
-                    if not repeated:
-                        nc.vector.tensor_tensor(
-                            res[:].rearrange("p (e j) -> p e j", e=2), bank[:].rearrange("p (e j) -> p e j", e=2),
-                            kept[b][:].rearrange("p (t j) -> p t j", j=HALF)[:, t0:t0 + 2, j0:j0 + n], ALU.add)
-                        nc.scalar.activation(res[:], res[:], ACT.Tanh)
-                    elif repeated == [1]:
-                        c0 = HALF * t0 + j0
-                        nc.vector.tensor_tensor(res[:, 0:n], bank[:, 0:n], kept[b][:, c0:c0 + n], ALU.add)
-                        nc.scalar.activation(res[:, n:2 * n], bank[:, n:2 * n], ACT.Tanh)
-                        nc.scalar.activation(res[:, 0:n], res[:, 0:n], ACT.Tanh)
-                    else:
-                        nc.scalar.activation(res[:], bank[:], ACT.Tanh)
-                    for e in range(2):
-                        part = res[:, n * e:n * (e + 1)]
-                        col = gains[:, 4 * b + t0 + e:4 * b + t0 + e + 1]
-                        if 4 * q + 2 * b + t0 // 2 < SCALAR_GAIN_BANKS:
-                            nc.scalar.activation(part, part, ACT.Copy, scale=col)
-                        else:
-                            nc.vector.tensor_scalar(part, part, col, None, ALU.mult)
-                    nc.sync.dma_start(
-                        out=out_rows[b, :, t0:t0 + 2, j0:j0 + n], in_=res[:].rearrange("p (e j) -> p e j", e=2))
+        def output_tile(b, t, half, gain_engine):
+            j0 = HALF * half
+            bank = next_bank()
+            res = in_turn("res", BANK, F32, RESULT_SLOTS)
+            repeated = half == 0 or (b, t) == REPEATED_SLICE
+            if repeated:
+                seller_pass(bank[:], b, t, j0, HALF, True, False)
+            for a in range(2):
+                m0 = GROUP * a + P * t
+                codes, scales = hq[a, half]
+                nc.tensor.matmul_mx(
+                    out=bank[:], lhsT=w4_codes[b][:, m0:m0 + P].bitcast(FP8X4),
+                    lhsT_scale=weight_plane[4 + 4 * a:P, GROUP * b + P * t:GROUP * b + P * (t + 1)],
+                    rhs=codes[:].bitcast(FP8X4), rhs_scale=scales[:],
+                    start=(a == 0 and not repeated), stop=(a == 1))
+            if repeated:
+                nc.scalar.activation(res[:], bank[:], ACT.Tanh)
+            else:
+                nc.vector.tensor_tensor(res[:], bank[:], kept[b][:, HALF * t:HALF * (t + 1)], ALU.add)
+                nc.scalar.activation(res[:], res[:], ACT.Tanh)
+            col = gains[:, 4 * b + t:4 * b + t + 1]
+            if gain_engine is nc.scalar:
+                nc.scalar.activation(res[:], res[:], ACT.Copy, scale=col)
+            else:
+                gain_engine.tensor_scalar(res[:], res[:], col, 0.0, ALU.mult, ALU.add)
+            nc.sync.dma_start(out=out_rows[b, :, t, j0:j0 + HALF], in_=res[:])
 
-        gated_pair([(0, 0), (0, 1)])
-        w4_codes = reorder("w4_codes", w4_raw, I32, 2 * N, 4)
-        gated_pair([(1, 0), (1, 1)])
-        gate_second_half(1)
-        output_quarter(0)
-        gated_pair([(0, 2), (1, 2)])
-        output_quarter(1)
-        gated_pair([(0, 3), (1, 3)])
-        output_quarter(2)
-        output_quarter(3)
+        nc.sync.dma_start(buyer_list[:], offs)
+        w2_first = load_weight("w2_first", w2, 0, 0, GROUP // 2)
+        load_rows(buyer_rows, tab_scales[0], 0)
+        nc.sync.dma_start(seller_list[:], offs2)
+        w2_second = load_weight("w2_second", w2, 0, GROUP // 2, GROUP // 2)
+        load_plane(seller_rows, tab2_scales, 4, range(4))
+        w2_raw[1] = load_weight("w2_raw1", w2, 0, GROUP)
+        nc.sync.dma_start(house_list[:], offs3)
+        load_rows(house_rows, tab3_scales[0], 0)
+        load_rows(house_rows, tab3_scales[1], 4)
+        w3_raw[0, 0] = load_weight("w3_raw00", w3, 0, 0)
+        load_plane(weight_plane_raw, w1_scales, 0, (0, 1))
+        seller_tab = load_words("seller_tab", tab2_words[0].rearrange("p t i -> p (t i)"))
+        load_plane(weight_plane_raw, w1_scales, 0, (2, 3))
+        nc.sync.dma_start(out=w1_raw[:], in_=w1_words[0].bitcast(I32))
+        load_plane(weight_plane_raw, w4_scales, 4, (0, 1))
+        buyer_tab = load_words("buyer_tab", tab_words[0].rearrange("p t i -> p (t i)"))
+
+        picked = held("picked", 2 * S, U8)
+        gather_into(picked[:, 0:S], buyer_rows, U8, buyer_list[:])
+        seller_plane = held("seller_plane", S, U8)
+        gather_into(seller_plane[:], seller_rows, U8, seller_list[:])
+        w2q[0] = quantise("w2_0", round_weight(0, w2_first, w2_second), "seller_rows")
+        gather_into(picked[:, S:2 * S], house_rows, U8, house_list[:])
+        load_plane(weight_plane_raw, w4_scales, 4, (2, 3))
+        place_rows(pair_planes, picked[:], 0, range(4))
+        house_tab[0] = load_words("house_tab0", tab3_words[0])
+        place_rows(last_plane, picked[:, S:2 * S], 4, range(4))
+        house_tab[1] = load_words("house_tab1", tab3_words[1])
+        w3_raw[1, 0] = load_weight("w3_raw10", w3, 1, 0)
+        w3_raw[0, 1] = load_weight("w3_raw01", w3, 0, GROUP, after="w2_raw1")
+        nc.sync.dma_start(
+            out=gains[:].rearrange("p (b t) -> p b t", t=4),
+            in_=gain.rearrange("(b p t) -> p b t", b=2, t=4))
+        w3_last = [
+            load_weight("w3_last%d" % e, w3, 1, GROUP + GROUP // 2 * e, GROUP // 2, after)
+            for e, after in enumerate(("w2_first", "w2_second"))]
+        for b in range(2):
+            w4_raw[b] = load_w4(b)
+        buyer_plane = pair_planes[:].bitcast(U8)[:, 0:S]
+        house_plane = [pair_planes[:].bitcast(U8)[:, S:2 * S], last_plane[:].bitcast(U8)]
+
+        w2q[1] = quantise("w2_1", round_weight(1, w2_raw[1]), "house_rows")
+        rounded00 = round_weight(2, w3_raw[0, 0])
+        for half in (1, 0):
+            seller_w[half] = gather_half("seller_w", seller_tab, U32, seller_list, half)
+        w1_codes = reorder("w1_codes", w1_raw, U16, H, 8)
+        weight_plane = reorder("weight_plane", weight_plane_raw, U8, H, 16)
+        buyer_w[0] = gather_half("buyer_w", buyer_tab, U32, buyer_list, 0, "weight_plane_raw")
+        buyer_w[1] = gather_half("buyer_w", buyer_tab, U32, buyer_list, 1)
+        w3q[0, 0] = quantise("w3_00", rounded00, "buyer_tab")
+        keep_seller(0, "w3_raw00")
+        gate_first_half(0)
+        keep_seller(1)
+        gate_first_half(1)
+        for a in range(2):
+            for half in range(2):
+                house_w[a, half] = gather_half("house_w%d" % a, house_tab[a], U16, house_list, half)
+        rounded10 = round_weight(0, w3_raw[1, 0])
+        logits0 = held("logits0", 4 * HALF, F32, "house_tab1")[:]
+        kept_logits(logits0, 0)
+        w3q[1, 0] = quantise("w3_10", rounded10)
+        logits1 = held("logits1", 4 * HALF, F32, "slot0")[:]
+        kept_logits(logits1, 1)
+        repeated_logits(logits1)
+        for u in range(4):
+            gated_unit(0, 0, u)
+        w3q[0, 1] = quantise("w3_01", round_weight(1, w3_raw[0, 1]))
+        quantise_h(0, 0)
+        w3q[1, 1] = quantise("w3_11", round_weight(2, *w3_last))
+        w4_codes[0] = reorder("w4_codes0", w4_raw[0], I32, 2 * GROUP, 4, "slot2")
+        gate_second_half(0, logits0, "w2_second")
+        gate_second_half(1, logits1, "house_tab1")
+        for u in range(4):
+            gated_unit(1, 0, u)
+        for u in range(4):
+            gated_unit(0, 1, u)
+            if u == 0:
+                quantise_h(1, 0)
+        for t in range(4):
+            output_tile(0, t, 0, nc.scalar)
+        w4_codes[1] = reorder("w4_codes1", w4_raw[1], I32, 2 * GROUP, 4, "h10")
+        quantise_h(0, 1)
+        for u in range(4):
+            gated_unit(1, 1, u)
+        output_tile(1, 0, 0, nc.gpsimd)
+        quantise_h(1, 1)
+        for t in range(1, 4):
+            output_tile(1, t, 0, nc.gpsimd)
+        for b in range(2):
+            for t in range(4):
+                output_tile(b, t, 1, nc.gpsimd if 4 * b + t < 4 else nc.vector)

@@ -23,6 +23,7 @@ HALF = S // 2
 UNIT = S // 8
 BANKS = 8
 RESULT_SLOTS = 12
+LAST_VECTOR_SHARE = 0
 REPEATED_SLICE = (1, 3)
 
 
@@ -54,29 +55,34 @@ def tile_list_haggling_features_kernel(
         seller_rows = held("seller_rows", T // 4, I32)
         buyer_rows = held("buyer_rows", T // 4, I32)
         house_rows = held("house_rows", T3 // 4, I32)
-        weight_plane_raw = held("weight_plane_raw", H // 4, I32)
+        w1_rows = held("w1_rows", H // 4, I32)
+        w4_rows = held("w4_rows", N // 4, I32)
         pair_planes = held("pair_planes", 2 * S // 4, I32)
-        last_plane = held("last_plane", S // 4, I32)
-        for tile in (buyer_rows, seller_rows, house_rows, weight_plane_raw, pair_planes, last_plane):
+        house_planes = [held("house_plane%d" % a, S // 4, I32) for a in range(2)]
+        for tile in (seller_rows, buyer_rows, house_rows, w1_rows, pair_planes, *house_planes, w4_rows):
             nc.vector.memset(tile[:], 0)
 
         warm = held("warm", 8, F32)
-        nc.gpsimd.memset(warm[:], 0.0)
+        nc.vector.memset(warm[:], 0.0)
         nc.scalar.activation(warm[:, 1:2], warm[:, 0:1], ACT.Sigmoid)
 
-        def load_plane(tile, scales, row0, quads):
-            rows = 4 * scales.shape[0]
-            for quad in quads:
-                src = scales[:, 4 * quad:4 * quad + 4, :] if rows > 4 else scales[0, 4 * quad:4 * quad + 4, :]
-                first = 32 * quad + row0
-                nc.sync.dma_start(out=tile[first:first + rows, :], in_=src.bitcast(I32))
+        def load_w1_plane(tile):
+            for i in range(4):
+                nc.sync.dma_start(out=tile[i:P:32, :], in_=w1_scales[0, i:16:4, :].bitcast(I32))
 
-        def load_rows(tile, rows, first):
-            nc.sync.dma_start(out=tile[first:P:8, :], in_=rows.bitcast(I32))
+        def load_w4_planes(tile):
+            for quad in (0, 2, 1, 3):
+                src = w4_scales[:, 4 * quad:4 * quad + 4, :]
+                nc.sync.dma_start(out=tile[32 * quad:32 * quad + 8, :], in_=src.bitcast(I32))
 
-        def place_rows(plane, picked, first, rows):
+        def load_rows(tile, scales):
+            rows = scales.rearrange("a s t -> (a s) t")
+            nc.sync.dma_start(out=tile[0:P:P // rows.shape[0], :], in_=rows.bitcast(I32))
+
+        def place_rows(plane, picked, first, step, rows):
             for i in rows:
-                nc.sync.dma_start(out=plane[i:P:32, :], in_=picked.bitcast(I32)[first + 8 * i:P:32, :])
+                src = picked[:].bitcast(I32)[first + step * i:first + 16 * step:4 * step, :]
+                nc.sync.dma_start(out=plane[i:P:32, :], in_=src)
 
         def load_weight(name, w, a, c0, cols=GROUP, after=None):
             raw = held(name, 4 * cols, F32, after)
@@ -112,13 +118,14 @@ def tile_list_haggling_features_kernel(
             gather_into(picked[:], window, dtype, lst[:, HALF * half // 16:HALF * (half + 1) // 16])
             return picked
 
-        def round_weight(slot, *pieces):
+        def round_weight(slot, raw, b=0, vector_share=0):
             rounded = held("rounded", 4 * GROUP, BF16, "slot%d" % slot)
-            span = P // len(pieces)
-            for e, raw in enumerate(pieces):
-                nc.scalar.copy(
-                    out=rounded[:].rearrange("p (t m j) -> p m j t", t=4, j=4)[:, span * e:span * (e + 1), :, :],
-                    in_=raw[:].rearrange("p (j m t) -> p m j t", t=4, j=4))
+            dst = rounded[:].rearrange("p (t m j) -> p m j t", t=4, j=4)
+            src = raw[:].rearrange("p (j m t) -> p m j t", t=4, j=4)[:, P * b:P * (b + 1), :, :]
+            split = P - vector_share
+            nc.scalar.copy(out=dst[:, 0:split, :, :], in_=src[:, 0:split, :, :])
+            if vector_share:
+                nc.vector.tensor_copy(out=dst[:, split:P, :, :], in_=src[:, split:P, :, :])
             return rounded
 
         def quantise(name, rounded, after=None):
@@ -141,14 +148,14 @@ def tile_list_haggling_features_kernel(
             half, c0 = divmod(j0, HALF)
             nc.tensor.matmul_mx(
                 out=dst, lhsT=codes[:, P * t:P * (t + 1)].bitcast(FP8X4), lhsT_scale=scales[:, P * t:P * (t + 1)],
-                rhs=seller_w[half][:, c0:c0 + n].bitcast(FP8X4), rhs_scale=seller_plane[4:P, j0:j0 + n],
+                rhs=seller_w[half][:, c0:c0 + n].bitcast(FP8X4), rhs_scale=seller_plane[:, j0:j0 + n],
                 start=start, stop=stop)
 
         def buyer_pass(dst, b, t, j0, n, start, stop):
             half, c0 = divmod(j0, HALF)
             m0 = GROUP * b + P * t
             nc.tensor.matmul_mx(
-                out=dst, lhsT=w1_codes[:, m0:m0 + P].bitcast(FP4X4), lhsT_scale=weight_plane[:, m0:m0 + P],
+                out=dst, lhsT=w1_codes[:, m0:m0 + P].bitcast(FP4X4), lhsT_scale=w1_plane[:, m0:m0 + P],
                 rhs=buyer_w[half][:, c0:c0 + n].bitcast(FP8X4), rhs_scale=buyer_plane[:, j0:j0 + n],
                 start=start, stop=stop)
 
@@ -160,8 +167,8 @@ def tile_list_haggling_features_kernel(
                     seller_pass(bank[:], b, t, HALF, HALF, True, True)
                     nc.scalar.copy(out=kept[b][:, HALF * t:HALF * (t + 1)], in_=bank[:])
 
-        def gate_first_half(b):
-            gate[b, 0] = held("gate%d0" % b, 4 * HALF, F32)
+        def gate_first_half(b, after=None):
+            gate[b, 0] = held("gate%d0" % b, 4 * HALF, F32, after)
             for u in range(4):
                 bank = next_bank()
                 for t in range(4):
@@ -195,9 +202,9 @@ def tile_list_haggling_features_kernel(
 
         h_rounded = {}
 
-        def gated_unit(b, half, u):
+        def gated_unit(b, half, u, after=None):
             if u == 0:
-                h_rounded[b, half] = held("h%d%d" % (b, half), 4 * HALF, BF16)
+                h_rounded[b, half] = held("h%d%d" % (b, half), 4 * HALF, BF16, after)
             j0 = HALF * half + UNIT * u
             bank = next_bank()
             for a in range(2):
@@ -231,7 +238,7 @@ def tile_list_haggling_features_kernel(
                 codes, scales = hq[a, half]
                 nc.tensor.matmul_mx(
                     out=bank[:], lhsT=w4_codes[b][:, m0:m0 + P].bitcast(FP8X4),
-                    lhsT_scale=weight_plane[4 + 4 * a:P, GROUP * b + P * t:GROUP * b + P * (t + 1)],
+                    lhsT_scale=w4_plane[4 * a:P, GROUP * b + P * t:GROUP * b + P * (t + 1)],
                     rhs=codes[:].bitcast(FP8X4), rhs_scale=scales[:],
                     start=(a == 0 and not repeated), stop=(a == 1))
             if repeated:
@@ -246,95 +253,102 @@ def tile_list_haggling_features_kernel(
                 gain_engine.tensor_scalar(res[:], res[:], col, 0.0, ALU.mult, ALU.add)
             nc.sync.dma_start(out=out_rows[b, :, t, j0:j0 + HALF], in_=res[:])
 
-        nc.sync.dma_start(buyer_list[:], offs)
-        w2_first = load_weight("w2_first", w2, 0, 0, GROUP // 2)
-        load_rows(buyer_rows, tab_scales[0], 0)
         nc.sync.dma_start(seller_list[:], offs2)
-        w2_second = load_weight("w2_second", w2, 0, GROUP // 2, GROUP // 2)
-        load_plane(seller_rows, tab2_scales, 4, range(4))
-        w2_raw[1] = load_weight("w2_raw1", w2, 0, GROUP)
-        nc.sync.dma_start(house_list[:], offs3)
-        load_rows(house_rows, tab3_scales[0], 0)
-        load_rows(house_rows, tab3_scales[1], 4)
-        w3_raw[0, 0] = load_weight("w3_raw00", w3, 0, 0)
-        load_plane(weight_plane_raw, w1_scales, 0, (0, 1))
-        seller_tab = load_words("seller_tab", tab2_words[0].rearrange("p t i -> p (t i)"))
-        load_plane(weight_plane_raw, w1_scales, 0, (2, 3))
         nc.sync.dma_start(out=w1_raw[:], in_=w1_words[0].bitcast(I32))
-        load_plane(weight_plane_raw, w4_scales, 4, (0, 1))
-        buyer_tab = load_words("buyer_tab", tab_words[0].rearrange("p t i -> p (t i)"))
+        load_rows(seller_rows, tab2_scales)
+        nc.sync.dma_start(buyer_list[:], offs)
+        load_rows(buyer_rows, tab_scales)
+        w2_raw[0] = load_weight("w2_raw0", w2, 0, 0)
+        nc.sync.dma_start(house_list[:], offs3)
+        load_rows(house_rows, tab3_scales)
+        w2_raw[1] = load_weight("w2_raw1", w2, 0, GROUP)
+        load_w1_plane(w1_rows)
+        seller_tab = load_words("seller_tab", tab2_words[0].rearrange("p t i -> p (t i)"))
 
-        picked = held("picked", 2 * S, U8)
-        gather_into(picked[:, 0:S], buyer_rows, U8, buyer_list[:])
-        seller_plane = held("seller_plane", S, U8)
-        gather_into(seller_plane[:], seller_rows, U8, seller_list[:])
-        w2q[0] = quantise("w2_0", round_weight(0, w2_first, w2_second), "seller_rows")
-        gather_into(picked[:, S:2 * S], house_rows, U8, house_list[:])
-        load_plane(weight_plane_raw, w4_scales, 4, (2, 3))
-        place_rows(pair_planes, picked[:], 0, range(4))
+        pair_picked = held("pair_picked", 2 * S, U8)
+        gather_into(pair_picked[:, 0:S], seller_rows, U8, seller_list[:])
+        gather_into(pair_picked[:, S:2 * S], buyer_rows, U8, buyer_list[:])
+        house_picked = held("house_picked", S, U8)
+        gather_into(house_picked[:], house_rows, U8, house_list[:])
+        place_rows(pair_planes, pair_picked, 0, 8, range(4))
+        buyer_tab = load_words("buyer_tab", tab_words[0].rearrange("p t i -> p (t i)"))
+        w3_raw[0, 0] = load_weight("w3_raw00", w3, 0, 0)
+        place_rows(house_planes[0], house_picked, 0, 4, range(4))
         house_tab[0] = load_words("house_tab0", tab3_words[0])
-        place_rows(last_plane, picked[:, S:2 * S], 4, range(4))
-        house_tab[1] = load_words("house_tab1", tab3_words[1])
         w3_raw[1, 0] = load_weight("w3_raw10", w3, 1, 0)
-        w3_raw[0, 1] = load_weight("w3_raw01", w3, 0, GROUP, after="w2_raw1")
+        place_rows(house_planes[1], house_picked, 64, 4, range(4))
+        house_tab[1] = load_words("house_tab1", tab3_words[1])
+        w3_raw[0, 1] = load_weight("w3_raw01", w3, 0, GROUP)
+        w3_raw[1, 1] = load_weight("w3_raw11", w3, 1, GROUP)
+        load_w4_planes(w4_rows)
+        w4_raw[0] = load_w4(0)
         nc.sync.dma_start(
             out=gains[:].rearrange("p (b t) -> p b t", t=4),
             in_=gain.rearrange("(b p t) -> p b t", b=2, t=4))
-        w3_last = [
-            load_weight("w3_last%d" % e, w3, 1, GROUP + GROUP // 2 * e, GROUP // 2, after)
-            for e, after in enumerate(("w2_first", "w2_second"))]
-        for b in range(2):
-            w4_raw[b] = load_w4(b)
-        buyer_plane = pair_planes[:].bitcast(U8)[:, 0:S]
-        house_plane = [pair_planes[:].bitcast(U8)[:, S:2 * S], last_plane[:].bitcast(U8)]
+        w4_raw[1] = load_w4(1)
+        seller_plane = pair_planes[:].bitcast(U8)[:, 0:S]
+        buyer_plane = pair_planes[:].bitcast(U8)[:, S:2 * S]
+        house_plane = [plane[:].bitcast(U8) for plane in house_planes]
 
-        w2q[1] = quantise("w2_1", round_weight(1, w2_raw[1]), "house_rows")
-        rounded00 = round_weight(2, w3_raw[0, 0])
+        w2q[0] = quantise("w2_0", round_weight(0, w2_raw[0]), "buyer_rows")
+        rounded21 = round_weight(1, w2_raw[1])
         for half in (1, 0):
             seller_w[half] = gather_half("seller_w", seller_tab, U32, seller_list, half)
+        w2q[1] = quantise("w2_1", rounded21, "seller_tab")
+        w1_plane = reorder("w1_plane", w1_rows, U8, H, 16, "house_rows")
         w1_codes = reorder("w1_codes", w1_raw, U16, H, 8)
-        weight_plane = reorder("weight_plane", weight_plane_raw, U8, H, 16)
-        buyer_w[0] = gather_half("buyer_w", buyer_tab, U32, buyer_list, 0, "weight_plane_raw")
-        buyer_w[1] = gather_half("buyer_w", buyer_tab, U32, buyer_list, 1)
-        w3q[0, 0] = quantise("w3_00", rounded00, "buyer_tab")
-        keep_seller(0, "w3_raw00")
-        gate_first_half(0)
-        keep_seller(1)
-        gate_first_half(1)
-        for a in range(2):
-            for half in range(2):
-                house_w[a, half] = gather_half("house_w%d" % a, house_tab[a], U16, house_list, half)
-        rounded10 = round_weight(0, w3_raw[1, 0])
-        logits0 = held("logits0", 4 * HALF, F32, "house_tab1")[:]
+        for half in (1, 0):
+            buyer_w[half] = gather_half("buyer_w", buyer_tab, U32, buyer_list, half)
+        for b in range(2):
+            keep_seller(b)
+        logits0 = held("logits0", 4 * HALF, F32, "buyer_tab")[:]
         kept_logits(logits0, 0)
-        w3q[1, 0] = quantise("w3_10", rounded10)
-        logits1 = held("logits1", 4 * HALF, F32, "slot0")[:]
+        rounded00 = round_weight(2, w3_raw[0, 0])
+        gate_first_half(0, "w3_raw00")
+        for half in range(2):
+            house_w[0, half] = gather_half("house_w0", house_tab[0], U16, house_list, half)
+        w3q[0, 0] = quantise("w3_00", rounded00, "house_tab0")
+        logits1 = held("logits1", 4 * HALF, F32, "slot2")[:]
         kept_logits(logits1, 1)
-        repeated_logits(logits1)
+        rounded10 = round_weight(0, w3_raw[1, 0])
+        gate_first_half(1, "w3_raw10")
+        house_w[1, 0] = gather_half("house_w1", house_tab[1], U16, house_list, 0)
+        w3q[1, 0] = quantise("w3_10", rounded10)
+        house_w[1, 1] = gather_half("house_w1", house_tab[1], U16, house_list, 1)
         for u in range(4):
             gated_unit(0, 0, u)
+        repeated_logits(logits1)
         w3q[0, 1] = quantise("w3_01", round_weight(1, w3_raw[0, 1]))
         quantise_h(0, 0)
-        w3q[1, 1] = quantise("w3_11", round_weight(2, *w3_last))
-        w4_codes[0] = reorder("w4_codes0", w4_raw[0], I32, 2 * GROUP, 4, "slot2")
-        gate_second_half(0, logits0, "w2_second")
-        gate_second_half(1, logits1, "house_tab1")
+        w3q[1, 1] = quantise("w3_11", round_weight(0, w3_raw[1, 1], 0, LAST_VECTOR_SHARE))
+        w4_codes[0] = reorder("w4_codes0", w4_raw[0], I32, 2 * GROUP, 4, "slot0")
+        w4_plane = reorder("w4_plane", w4_rows, U8, N, 16)
+        gate_second_half(0, logits0, "w3_raw11")
+        gate_second_half(1, logits1, "buyer_tab")
         for u in range(4):
-            gated_unit(1, 0, u)
+            gated_unit(1, 0, u, "w4_raw0")
         for u in range(4):
             gated_unit(0, 1, u)
             if u == 0:
                 quantise_h(1, 0)
-        for t in range(4):
-            output_tile(0, t, 0, nc.scalar)
-        w4_codes[1] = reorder("w4_codes1", w4_raw[1], I32, 2 * GROUP, 4, "h10")
+        output_tile(0, 0, 0, nc.scalar)
+        output_tile(0, 1, 0, nc.scalar)
+        output_tile(0, 2, 0, nc.scalar)
+        output_tile(0, 3, 0, nc.scalar)
+        w4_codes[1] = reorder("w4_codes1", w4_raw[1], I32, 2 * GROUP, 4, "w4_raw0")
         quantise_h(0, 1)
         for u in range(4):
             gated_unit(1, 1, u)
         output_tile(1, 0, 0, nc.gpsimd)
         quantise_h(1, 1)
-        for t in range(1, 4):
-            output_tile(1, t, 0, nc.gpsimd)
-        for b in range(2):
-            for t in range(4):
-                output_tile(b, t, 1, nc.gpsimd if 4 * b + t < 4 else nc.vector)
+        output_tile(1, 1, 0, nc.gpsimd)
+        output_tile(1, 2, 0, nc.gpsimd)
+        output_tile(0, 0, 1, nc.gpsimd)
+        output_tile(0, 1, 1, nc.gpsimd)
+        output_tile(0, 2, 1, nc.gpsimd)
+        output_tile(0, 3, 1, nc.gpsimd)
+        output_tile(1, 0, 1, nc.gpsimd)
+        output_tile(1, 1, 1, nc.vector)
+        output_tile(1, 2, 1, nc.vector)
+        output_tile(1, 3, 0, nc.vector)
+        output_tile(1, 3, 1, nc.vector)

@@ -23,7 +23,6 @@ HALF = S // 2
 UNIT = S // 8
 BANKS = 8
 RESULT_SLOTS = 12
-LAST_VECTOR_SHARE = 0
 REPEATED_SLICE = (1, 3)
 
 
@@ -118,14 +117,20 @@ def tile_list_haggling_features_kernel(
             gather_into(picked[:], window, dtype, lst[:, HALF * half // 16:HALF * (half + 1) // 16])
             return picked
 
-        def round_weight(slot, raw, b=0, vector_share=0):
+        def round_weight(slot, *pieces):
             rounded = held("rounded", 4 * GROUP, BF16, "slot%d" % slot)
-            dst = rounded[:].rearrange("p (t m j) -> p m j t", t=4, j=4)
-            src = raw[:].rearrange("p (j m t) -> p m j t", t=4, j=4)[:, P * b:P * (b + 1), :, :]
-            split = P - vector_share
-            nc.scalar.copy(out=dst[:, 0:split, :, :], in_=src[:, 0:split, :, :])
-            if vector_share:
-                nc.vector.tensor_copy(out=dst[:, split:P, :, :], in_=src[:, split:P, :, :])
+            span = P // len(pieces)
+            for e, raw in enumerate(pieces):
+                nc.scalar.copy(
+                    out=rounded[:].rearrange("p (t m j) -> p m j t", t=4, j=4)[:, span * e:span * (e + 1), :, :],
+                    in_=raw[:].rearrange("p (j m t) -> p m j t", t=4, j=4))
+            return rounded
+
+        def round_on_gpsimd(slot, raw):
+            rounded = held("rounded", 4 * GROUP, BF16, "slot%d" % slot)
+            nc.gpsimd.tensor_copy(
+                out=rounded[:].rearrange("p (t m j) -> p t m j", t=4, j=4),
+                in_=raw[:].rearrange("p (j m t) -> p t m j", t=4, j=4))
             return rounded
 
         def quantise(name, rounded, after=None):
@@ -139,6 +144,13 @@ def tile_list_haggling_features_kernel(
             nc.vector.tensor_copy(
                 out=ordered[:].rearrange("p (b t c i) -> p b c t i", t=4, c=P // run, i=run),
                 in_=raw[:].bitcast(dtype).rearrange("p (b c i t) -> p b c t i", t=4, c=P // run, i=run))
+            return ordered
+
+        def reorder_on_gpsimd(name, raw, dtype, cols, after=None):
+            ordered = held(name, cols, dtype, after)
+            nc.gpsimd.tensor_copy(
+                out=ordered[:].rearrange("p (b t m) -> p b t m", t=4, m=P),
+                in_=raw[:].bitcast(dtype).rearrange("p (b m t) -> p b t m", t=4, m=P))
             return ordered
 
         w2q, w3q, w4_codes, seller_w, buyer_w, house_w, gate, kept, hq = {}, {}, {}, {}, {}, {}, {}, {}, {}
@@ -221,8 +233,8 @@ def tile_list_haggling_features_kernel(
                 bank[:].rearrange("p (t j) -> p j t", t=4),
                 gate[b, half][:, BANK * u:BANK * (u + 1)].rearrange("p (j t) -> p j t", t=4), ALU.mult)
 
-        def quantise_h(b, half):
-            hq[b, half] = quantise("h%d%d" % (b, half), h_rounded[b, half])
+        def quantise_h(b, half, after=None):
+            hq[b, half] = quantise("h%d%d" % (b, half), h_rounded[b, half], after)
 
         out_rows = out.rearrange("(b p t) j -> b p t j", b=2, t=4)
 
@@ -279,7 +291,7 @@ def tile_list_haggling_features_kernel(
         place_rows(house_planes[1], house_picked, 64, 4, range(4))
         house_tab[1] = load_words("house_tab1", tab3_words[1])
         w3_raw[0, 1] = load_weight("w3_raw01", w3, 0, GROUP)
-        w3_raw[1, 1] = load_weight("w3_raw11", w3, 1, GROUP)
+        w3_last = [load_weight("w3_last%d" % e, w3, 1, GROUP + GROUP // 2 * e, GROUP // 2) for e in range(2)]
         load_w4_planes(w4_rows)
         w4_raw[0] = load_w4(0)
         nc.sync.dma_start(
@@ -303,13 +315,14 @@ def tile_list_haggling_features_kernel(
             keep_seller(b)
         logits0 = held("logits0", 4 * HALF, F32, "buyer_tab")[:]
         kept_logits(logits0, 0)
-        rounded00 = round_weight(2, w3_raw[0, 0])
-        gate_first_half(0, "w3_raw00")
+        logits1 = held("logits1", 4 * HALF, F32)[:]
+        kept_logits(logits1, 1)
+        repeated_logits(logits1)
+        rounded00 = round_on_gpsimd(2, w3_raw[0, 0])
+        gate_first_half(0)
         for half in range(2):
             house_w[0, half] = gather_half("house_w0", house_tab[0], U16, house_list, half)
         w3q[0, 0] = quantise("w3_00", rounded00, "house_tab0")
-        logits1 = held("logits1", 4 * HALF, F32, "slot2")[:]
-        kept_logits(logits1, 1)
         rounded10 = round_weight(0, w3_raw[1, 0])
         gate_first_half(1, "w3_raw10")
         house_w[1, 0] = gather_half("house_w1", house_tab[1], U16, house_list, 0)
@@ -317,16 +330,15 @@ def tile_list_haggling_features_kernel(
         house_w[1, 1] = gather_half("house_w1", house_tab[1], U16, house_list, 1)
         for u in range(4):
             gated_unit(0, 0, u)
-        repeated_logits(logits1)
         w3q[0, 1] = quantise("w3_01", round_weight(1, w3_raw[0, 1]))
-        quantise_h(0, 0)
-        w3q[1, 1] = quantise("w3_11", round_weight(0, w3_raw[1, 1], 0, LAST_VECTOR_SHARE))
-        w4_codes[0] = reorder("w4_codes0", w4_raw[0], I32, 2 * GROUP, 4, "slot0")
+        quantise_h(0, 0, "slot1")
+        w3q[1, 1] = quantise("w3_11", round_weight(0, *w3_last))
+        w4_codes[0] = reorder_on_gpsimd("w4_codes0", w4_raw[0], I32, 2 * GROUP, "slot0")
         w4_plane = reorder("w4_plane", w4_rows, U8, N, 16)
-        gate_second_half(0, logits0, "w3_raw11")
+        gate_second_half(0, logits0, "w3_last1")
         gate_second_half(1, logits1, "buyer_tab")
         for u in range(4):
-            gated_unit(1, 0, u, "w4_raw0")
+            gated_unit(1, 0, u)
         for u in range(4):
             gated_unit(0, 1, u)
             if u == 0:
@@ -335,11 +347,11 @@ def tile_list_haggling_features_kernel(
         output_tile(0, 1, 0, nc.scalar)
         output_tile(0, 2, 0, nc.scalar)
         output_tile(0, 3, 0, nc.scalar)
-        w4_codes[1] = reorder("w4_codes1", w4_raw[1], I32, 2 * GROUP, 4, "w4_raw0")
-        quantise_h(0, 1)
+        w4_codes[1] = reorder_on_gpsimd("w4_codes1", w4_raw[1], I32, 2 * GROUP, "h10")
         for u in range(4):
             gated_unit(1, 1, u)
-        output_tile(1, 0, 0, nc.gpsimd)
+        output_tile(1, 0, 0, nc.scalar)
+        quantise_h(0, 1, "buyer_tab")
         quantise_h(1, 1)
         output_tile(1, 1, 0, nc.gpsimd)
         output_tile(1, 2, 0, nc.gpsimd)
@@ -347,7 +359,7 @@ def tile_list_haggling_features_kernel(
         output_tile(0, 1, 1, nc.gpsimd)
         output_tile(0, 2, 1, nc.gpsimd)
         output_tile(0, 3, 1, nc.gpsimd)
-        output_tile(1, 0, 1, nc.gpsimd)
+        output_tile(1, 0, 1, nc.vector)
         output_tile(1, 1, 1, nc.vector)
         output_tile(1, 2, 1, nc.vector)
         output_tile(1, 3, 0, nc.vector)

@@ -139,19 +139,13 @@ def tile_list_haggling_features_kernel(
             nc.vector.quantize_mx(out=codes[:].bitcast(FP8X4), scales=scales[:], in_=rounded[:])
             return codes, scales
 
-        def reorder(name, raw, dtype, cols, run, after=None):
+        def reorder(name, raw, dtype, cols, run, after=None, engine=nc.vector):
             ordered = held(name, cols, dtype, after)
-            nc.vector.tensor_copy(
+            engine.tensor_copy(
                 out=ordered[:].rearrange("p (b t c i) -> p b c t i", t=4, c=P // run, i=run),
                 in_=raw[:].bitcast(dtype).rearrange("p (b c i t) -> p b c t i", t=4, c=P // run, i=run))
             return ordered
 
-        def reorder_on_gpsimd(name, raw, dtype, cols, after=None):
-            ordered = held(name, cols, dtype, after)
-            nc.gpsimd.tensor_copy(
-                out=ordered[:].rearrange("p (b t m) -> p b t m", t=4, m=P),
-                in_=raw[:].bitcast(dtype).rearrange("p (b m t) -> p b t m", t=4, m=P))
-            return ordered
 
         w2q, w3q, w4_codes, seller_w, buyer_w, house_w, gate, kept, hq = {}, {}, {}, {}, {}, {}, {}, {}, {}
 
@@ -333,7 +327,7 @@ def tile_list_haggling_features_kernel(
         w3q[0, 1] = quantise("w3_01", round_weight(1, w3_raw[0, 1]))
         quantise_h(0, 0, "slot1")
         w3q[1, 1] = quantise("w3_11", round_weight(0, *w3_last))
-        w4_codes[0] = reorder_on_gpsimd("w4_codes0", w4_raw[0], I32, 2 * GROUP, "slot0")
+        w4_codes[0] = reorder("w4_codes0", w4_raw[0], I32, 2 * GROUP, 4, "slot0", nc.gpsimd)
         w4_plane = reorder("w4_plane", w4_rows, U8, N, 16)
         gate_second_half(0, logits0, "w3_last1")
         gate_second_half(1, logits1, "buyer_tab")
@@ -347,7 +341,7 @@ def tile_list_haggling_features_kernel(
         output_tile(0, 1, 0, nc.scalar)
         output_tile(0, 2, 0, nc.scalar)
         output_tile(0, 3, 0, nc.scalar)
-        w4_codes[1] = reorder_on_gpsimd("w4_codes1", w4_raw[1], I32, 2 * GROUP, "h10")
+        w4_codes[1] = reorder("w4_codes1", w4_raw[1], I32, 2 * GROUP, 4, "h10", nc.gpsimd)
         for u in range(4):
             gated_unit(1, 1, u)
         output_tile(1, 0, 0, nc.scalar)

@@ -23,7 +23,7 @@ HALF = S // 2
 UNIT = S // 8
 BANKS = 8
 RESULT_SLOTS = 12
-REPEATED_SLICE = (1, 3)
+REPEATED_SLICE = (3, 1)
 
 
 def tile_list_haggling_features_kernel(
@@ -33,7 +33,6 @@ def tile_list_haggling_features_kernel(
     nc = tc.nc
     with ExitStack() as ctx:
         keep = ctx.enter_context(tc.tile_pool(name="keep", bufs=1))
-        ring = ctx.enter_context(tc.tile_pool(name="ring", bufs=1))
         psum = ctx.enter_context(tc.psum_pool(name="psum", bufs=1))
 
         def held(name, cols, dtype, after=None):
@@ -45,25 +44,28 @@ def tile_list_haggling_features_kernel(
             turns[name] = turns.get(name, -1) + 1
             return "%s%d" % (name, turns[name] % slots)
 
-        def in_turn(name, cols, dtype, slots):
-            return ring.tile([P, cols], dtype, name=slot_name(name, slots), align_bytes=64)
+        def next_bank(which=None):
+            name = slot_name("bank", BANKS) if which is None else "bank%d" % which
+            return psum.tile([P, BANK], F32, name=name)
 
-        def next_bank():
-            return psum.tile([P, BANK], F32, name=slot_name("bank", BANKS))
+        def zeroed(name, cols, engine):
+            tile = held(name, cols, I32)
+            engine.memset(tile[:], 0)
+            return tile
 
-        seller_rows = held("seller_rows", T // 4, I32)
-        buyer_rows = held("buyer_rows", T // 4, I32)
-        house_rows = held("house_rows", T3 // 4, I32)
-        w1_rows = held("w1_rows", H // 4, I32)
-        w4_rows = held("w4_rows", N // 4, I32)
-        pair_planes = held("pair_planes", 2 * S // 4, I32)
-        house_planes = [held("house_plane%d" % a, S // 4, I32) for a in range(2)]
-        for tile in (seller_rows, buyer_rows, house_rows, w1_rows, pair_planes, *house_planes, w4_rows):
-            nc.vector.memset(tile[:], 0)
+        def load_list(name, entries):
+            tile = keep.tile([P, S // 16], U16, name=name)
+            nc.sync.dma_start(tile[:], entries)
+            return tile
 
-        warm = held("warm", 8, F32)
-        nc.vector.memset(warm[:], 0.0)
-        nc.scalar.activation(warm[:, 1:2], warm[:, 0:1], ACT.Sigmoid)
+        def load_rows(tile, scales):
+            rows = scales.rearrange("a s t -> (a s) t")
+            nc.sync.dma_start(out=tile[0:P:P // rows.shape[0], :], in_=rows.bitcast(I32))
+
+        def place_rows(plane, picked, first, step):
+            for i in range(4):
+                src = picked[:].bitcast(I32)[first + step * i:first + 16 * step:4 * step, :]
+                nc.sync.dma_start(out=plane[i:P:32, :], in_=src)
 
         def load_w1_plane(tile):
             for i in range(4):
@@ -72,42 +74,26 @@ def tile_list_haggling_features_kernel(
         def load_w4_planes(tile):
             for quad in (0, 2, 1, 3):
                 src = w4_scales[:, 4 * quad:4 * quad + 4, :]
-                nc.sync.dma_start(out=tile[32 * quad:32 * quad + 8, :], in_=src.bitcast(I32))
-
-        def load_rows(tile, scales):
-            rows = scales.rearrange("a s t -> (a s) t")
-            nc.sync.dma_start(out=tile[0:P:P // rows.shape[0], :], in_=rows.bitcast(I32))
-
-        def place_rows(plane, picked, first, step, rows):
-            for i in rows:
-                src = picked[:].bitcast(I32)[first + step * i:first + 16 * step:4 * step, :]
-                nc.sync.dma_start(out=plane[i:P:32, :], in_=src)
+                nc.sync.dma_start(out=tile[32 * quad + 8:32 * quad + 16, :], in_=src.bitcast(I32))
 
         def load_weight(name, w, a, c0, cols=GROUP, after=None):
             raw = held(name, 4 * cols, F32, after)
             rows = w[512 * a:512 * (a + 1), c0:c0 + cols]
-            nc.sync.dma_start(
-                out=raw[:].rearrange("p (j c) -> p j c", j=4), in_=rows.rearrange("(p j) c -> p j c", j=4))
-            return raw
+            view = raw[:].rearrange("p (j c) -> p j c", j=4)
+            nc.sync.dma_start(out=view, in_=rows.rearrange("(p j) c -> p j c", j=4))
+            return view
 
         def load_words(name, words):
             table = held(name, T, I32)
             nc.sync.dma_start(out=table[:], in_=words.bitcast(I32))
             return table
 
-        def load_w4(b):
-            raw = held("w4_raw%d" % b, 2 * GROUP, I32)
+        def load_w4(b, after=None):
+            raw = held("w4_raw%d" % b, 2 * GROUP, I32, after)
             words = w4_words[:, :, GROUP * b:GROUP * (b + 1), :]
             nc.sync.dma_start(
                 out=raw[:].rearrange("p (a c) -> p a c", a=2), in_=words.rearrange("a p c i -> p a (c i)").bitcast(I32))
             return raw
-
-        seller_list = keep.tile([P, S // 16], U16, name="seller_list")
-        buyer_list = keep.tile([P, S // 16], U16, name="buyer_list")
-        house_list = keep.tile([P, S // 16], U16, name="house_list")
-        w1_raw = held("w1_raw", H // 2, I32)
-        gains = held("gains", 8, F32)
-        w2_raw, w3_raw, w4_raw, house_tab = {}, {}, {}, {}
 
         def gather_into(dst, window, dtype, entries):
             nc.vector.tensor_copy(dst, window[:].bitcast(dtype).indirect(entries))
@@ -117,40 +103,70 @@ def tile_list_haggling_features_kernel(
             gather_into(picked[:], window, dtype, lst[:, HALF * half // 16:HALF * (half + 1) // 16])
             return picked
 
-        def round_weight(slot, *pieces):
-            rounded = held("rounded", 4 * GROUP, BF16, "slot%d" % slot)
-            span = P // len(pieces)
-            for e, raw in enumerate(pieces):
-                nc.scalar.copy(
-                    out=rounded[:].rearrange("p (t m j) -> p m j t", t=4, j=4)[:, span * e:span * (e + 1), :, :],
-                    in_=raw[:].rearrange("p (j m t) -> p m j t", t=4, j=4))
+        def rounded_tile(name, after=None):
+            return held(name, 4 * GROUP, BF16, after)
+
+        def round_columns(rounded, raw, m0, engine):
+            count = raw.shape[2] // 4
+            dst = rounded[:].rearrange("p (t m j) -> p m j t", t=4, j=4)[:, m0:m0 + count, :, :]
+            src = raw.rearrange("p j (m t) -> p m j t", t=4)
+            if engine is nc.scalar:
+                nc.scalar.copy(out=dst, in_=src)
+            elif engine is nc.vector:
+                nc.vector.tensor_copy(out=dst, in_=src)
+            else:
+                nc.gpsimd.tensor_scalar(
+                    dst.rearrange("p m j t -> p m t j"), src.rearrange("p m j t -> p m t j"), 1.0, 0.0, ALU.mult, ALU.add)
+
+        def round_group(name, raw, engine, after=None):
+            rounded = rounded_tile(name, after)
+            round_columns(rounded, raw, 0, engine)
             return rounded
 
-        def round_on_gpsimd(slot, raw):
-            rounded = held("rounded", 4 * GROUP, BF16, "slot%d" % slot)
-            nc.gpsimd.tensor_copy(
-                out=rounded[:].rearrange("p (t m j) -> p t m j", t=4, j=4),
-                in_=raw[:].rearrange("p (j m t) -> p t m j", t=4, j=4))
-            return rounded
-
-        def quantise(name, rounded, after=None):
+        def quantise(name, rounded, after=None, scales=None):
             codes = held(name + "_codes", GROUP, U32, after)
-            scales = held(name + "_scales", GROUP, U8)
+            if scales is None:
+                scales = held(name + "_scales", GROUP, U8)
             nc.vector.quantize_mx(out=codes[:].bitcast(FP8X4), scales=scales[:], in_=rounded[:])
             return codes, scales
 
-        def reorder(name, raw, dtype, cols, run, after=None, engine=nc.vector):
+        def round_on_gpsimd(rounded, raw, m0=0):
+            for e in range(raw.shape[2] // P):
+                round_columns(rounded, raw[:, :, P * e:P * (e + 1)], m0 + 32 * e, nc.gpsimd)
+            return rounded
+
+        def reorder_halfwords(name, raw):
+            ordered = held(name, H, U16)
+            for b in range(2):
+                nc.gpsimd.tensor_copy(
+                    out=ordered[:].bitcast(U8).rearrange("p (b t c i e) -> p b c t i e", b=2, t=4, i=8, e=2)[:, b],
+                    in_=raw[:].bitcast(U8).rearrange("p (b c i t e) -> p b c t i e", b=2, t=4, i=8, e=2)[:, b])
+            return ordered
+
+        def reorder(name, raw, dtype, cols, run, engine, after=None):
             ordered = held(name, cols, dtype, after)
             engine.tensor_copy(
                 out=ordered[:].rearrange("p (b t c i) -> p b c t i", t=4, c=P // run, i=run),
                 in_=raw[:].bitcast(dtype).rearrange("p (b c i t) -> p b c t i", t=4, c=P // run, i=run))
             return ordered
 
+        def reorder_on_gpsimd(name, raw, dtype, cols, run, piece, after=None):
+            ordered = held(name, cols, dtype, after)
+            for b in range(cols // GROUP):
+                dst = ordered[:].rearrange("p (b t c i) -> p b c t i", t=4, c=P // run, i=run)[:, b]
+                src = raw[:].bitcast(dtype).rearrange("p (b c i t) -> p b c t i", t=4, c=P // run, i=run)[:, b]
+                step = piece // (4 * run)
+                for c0 in range(0, P // run, step):
+                    nc.gpsimd.tensor_copy(out=dst[:, c0:c0 + step], in_=src[:, c0:c0 + step])
+            return ordered
 
-        w2q, w3q, w4_codes, seller_w, buyer_w, house_w, gate, kept, hq = {}, {}, {}, {}, {}, {}, {}, {}, {}
+        w2q, w3q, seller_w, buyer_w, house_w, gate, kept, logits, hq, h_rounded = {}, {}, {}, {}, {}, {}, {}, {}, {}, {}
 
-        def seller_pass(dst, b, t, j0, n, start, stop):
-            codes, scales = w2q[b]
+        def columns(tile, t):
+            return tile[:, HALF * t:HALF * (t + 1)]
+
+        def seller_pass(dst, weight, t, j0, n, start, stop):
+            codes, scales = weight
             half, c0 = divmod(j0, HALF)
             nc.tensor.matmul_mx(
                 out=dst, lhsT=codes[:, P * t:P * (t + 1)].bitcast(FP8X4), lhsT_scale=scales[:, P * t:P * (t + 1)],
@@ -165,196 +181,240 @@ def tile_list_haggling_features_kernel(
                 rhs=buyer_w[half][:, c0:c0 + n].bitcast(FP8X4), rhs_scale=buyer_plane[:, j0:j0 + n],
                 start=start, stop=stop)
 
-        def keep_seller(b, after=None):
-            kept[b] = held("kept%d" % b, 4 * HALF, F32, after)
+        def keep_seller(half, after=None):
+            kept[half] = held("kept%d" % half, 4 * HALF, F32, after)
             for t in range(4):
-                if (b, t) != REPEATED_SLICE:
+                if (t, half) != REPEATED_SLICE:
                     bank = next_bank()
-                    seller_pass(bank[:], b, t, HALF, HALF, True, True)
-                    nc.scalar.copy(out=kept[b][:, HALF * t:HALF * (t + 1)], in_=bank[:])
+                    seller_pass(bank[:], w2q[0], t, HALF * half, HALF, True, True)
+                    nc.scalar.copy(out=columns(kept[half], t), in_=bank[:])
 
-        def gate_first_half(b, after=None):
-            gate[b, 0] = held("gate%d0" % b, 4 * HALF, F32, after)
+        def kept_logits(half, after=None):
+            logits[half] = held("logits%d" % half, 4 * HALF, F32, after)
+            for t in range(4):
+                bank = next_bank()
+                dst = columns(logits[half], t)
+                if (t, half) == REPEATED_SLICE:
+                    buyer_pass(bank[:], 0, t, HALF * half, HALF, True, False)
+                    seller_pass(bank[:], w2q[0], t, HALF * half, HALF, False, True)
+                    nc.scalar.copy(out=dst, in_=bank[:])
+                else:
+                    buyer_pass(bank[:], 0, t, HALF * half, HALF, True, True)
+                    nc.vector.tensor_tensor(dst, bank[:], columns(kept[half], t), ALU.add)
+
+        def gate_from_logits(half, after=None):
+            gate[0, half] = held("gate0%d" % half, 4 * HALF, F32, after)
+            nc.scalar.activation(
+                gate[0, half][:].rearrange("p (c i t) -> p c t i", i=4, t=4),
+                logits[half][:].rearrange("p (t c i) -> p c t i", i=4, t=4), ACT.Sigmoid)
+
+        def gate_from_banks(half, after=None):
+            gate[1, half] = held("gate1%d" % half, 4 * HALF, F32, after)
             for u in range(4):
                 bank = next_bank()
+                j0 = HALF * half + UNIT * u
                 for t in range(4):
-                    seller_pass(bank[:, UNIT * t:UNIT * (t + 1)], b, t, UNIT * u, UNIT, t == 0, False)
+                    seller_pass(bank[:, UNIT * t:UNIT * (t + 1)], w2q[1], t, j0, UNIT, t == 0, False)
                 for t in range(4):
-                    buyer_pass(bank[:, UNIT * t:UNIT * (t + 1)], b, t, UNIT * u, UNIT, False, t == 3)
+                    buyer_pass(bank[:, UNIT * t:UNIT * (t + 1)], 1, t, j0, UNIT, False, t == 3)
                 nc.scalar.activation(
-                    gate[b, 0][:, BANK * u:BANK * (u + 1)].rearrange("p (j t) -> p j t", t=4),
+                    gate[1, half][:, BANK * u:BANK * (u + 1)].rearrange("p (j t) -> p j t", t=4),
                     bank[:].rearrange("p (t j) -> p j t", t=4), ACT.Sigmoid)
 
-        def kept_logits(logits, b):
+        def restore_order(plain, ordered):
+            for m0 in (0, P // 2):
+                nc.gpsimd.tensor_copy(
+                    out=plain.rearrange("p (m t) -> p m t", t=4)[:, m0:m0 + P // 2],
+                    in_=ordered.rearrange("p (t m) -> p m t", t=4)[:, m0:m0 + P // 2])
+            return plain
+
+        house_banks = {}
+
+        def house_pass(b, half, u, a, which=None):
+            if a == 0:
+                house_banks[b, half, u] = next_bank(which)
+            bank = house_banks[b, half, u]
+            j0 = HALF * half + UNIT * u
+            codes, scales = w3q[a, b]
             for t in range(4):
-                if (b, t) != REPEATED_SLICE:
-                    bank = next_bank()
-                    buyer_pass(bank[:], b, t, HALF, HALF, True, True)
-                    nc.vector.tensor_tensor(
-                        logits[:, HALF * t:HALF * (t + 1)], bank[:], kept[b][:, HALF * t:HALF * (t + 1)], ALU.add)
-
-        def repeated_logits(logits):
-            b, t = REPEATED_SLICE
-            bank = next_bank()
-            buyer_pass(bank[:], b, t, HALF, HALF, True, False)
-            seller_pass(bank[:], b, t, HALF, HALF, False, True)
-            nc.scalar.copy(out=logits[:, HALF * t:HALF * (t + 1)], in_=bank[:])
-
-        def gate_second_half(b, logits, after):
-            gate[b, 1] = held("gate%d1" % b, 4 * HALF, F32, after)
-            nc.scalar.activation(
-                gate[b, 1][:].rearrange("p (c i t) -> p c t i", i=4, t=4),
-                logits.rearrange("p (t c i) -> p c t i", i=4, t=4), ACT.Sigmoid)
-
-        h_rounded = {}
+                nc.tensor.matmul_mx(
+                    out=bank[:, UNIT * t:UNIT * (t + 1)],
+                    lhsT=codes[:, P * t:P * (t + 1)].bitcast(FP8X4), lhsT_scale=scales[:, P * t:P * (t + 1)],
+                    rhs=house_w[a, half][:, UNIT * u:UNIT * (u + 1)].bitcast(FP4X4),
+                    rhs_scale=house_plane[a][:, j0:j0 + UNIT],
+                    start=(a == 0 and t == 0), stop=(a == 1 and t == 3))
 
         def gated_unit(b, half, u, after=None):
             if u == 0:
                 h_rounded[b, half] = held("h%d%d" % (b, half), 4 * HALF, BF16, after)
-            j0 = HALF * half + UNIT * u
-            bank = next_bank()
-            for a in range(2):
-                codes, scales = w3q[a, b]
-                for t in range(4):
-                    nc.tensor.matmul_mx(
-                        out=bank[:, UNIT * t:UNIT * (t + 1)],
-                        lhsT=codes[:, P * t:P * (t + 1)].bitcast(FP8X4), lhsT_scale=scales[:, P * t:P * (t + 1)],
-                        rhs=house_w[a, half][:, UNIT * u:UNIT * (u + 1)].bitcast(FP4X4),
-                        rhs_scale=house_plane[a][:, j0:j0 + UNIT],
-                        start=(a == 0 and t == 0), stop=(a == 1 and t == 3))
             nc.vector.tensor_tensor(
                 h_rounded[b, half][:, BANK * u:BANK * (u + 1)].rearrange("p (j t) -> p j t", t=4),
-                bank[:].rearrange("p (t j) -> p j t", t=4),
+                house_banks[b, half, u][:].rearrange("p (t j) -> p j t", t=4),
                 gate[b, half][:, BANK * u:BANK * (u + 1)].rearrange("p (j t) -> p j t", t=4), ALU.mult)
+
+        def gated_half(b, half, after=None):
+            for u in range(4):
+                house_pass(b, half, u, 0)
+                house_pass(b, half, u, 1)
+                gated_unit(b, half, u, after)
 
         def quantise_h(b, half, after=None):
             hq[b, half] = quantise("h%d%d" % (b, half), h_rounded[b, half], after)
 
-        out_rows = out.rearrange("(b p t) j -> b p t j", b=2, t=4)
+        out_rows = [out[0:GROUP, :].rearrange("(p t) j -> p t j", t=4), out[GROUP:N, :].rearrange("(t p) j -> p t j", t=4)]
+        w4_codes, w4_planes = {}, {}
 
-        def output_tile(b, t, half, gain_engine):
+        def output_tile(b, t, half, gain_engine, which):
             j0 = HALF * half
-            bank = next_bank()
-            res = in_turn("res", BANK, F32, RESULT_SLOTS)
-            repeated = half == 0 or (b, t) == REPEATED_SLICE
+            bank = next_bank(which)
+            res = held(slot_name("res", RESULT_SLOTS), BANK, F32)
+            repeated = b == 1 or (t, half) == REPEATED_SLICE
             if repeated:
-                seller_pass(bank[:], b, t, j0, HALF, True, False)
+                seller_pass(bank[:], w2_plain if b == 1 else w2q[0], t, j0, HALF, True, False)
             for a in range(2):
                 m0 = GROUP * a + P * t
                 codes, scales = hq[a, half]
                 nc.tensor.matmul_mx(
                     out=bank[:], lhsT=w4_codes[b][:, m0:m0 + P].bitcast(FP8X4),
-                    lhsT_scale=w4_plane[4 * a:P, GROUP * b + P * t:GROUP * b + P * (t + 1)],
+                    lhsT_scale=w4_planes[b][8 + 4 * a:P, P * t:P * (t + 1)],
                     rhs=codes[:].bitcast(FP8X4), rhs_scale=scales[:],
                     start=(a == 0 and not repeated), stop=(a == 1))
             if repeated:
                 nc.scalar.activation(res[:], bank[:], ACT.Tanh)
             else:
-                nc.vector.tensor_tensor(res[:], bank[:], kept[b][:, HALF * t:HALF * (t + 1)], ALU.add)
+                nc.vector.tensor_tensor(res[:], bank[:], columns(kept[half], t), ALU.add)
                 nc.scalar.activation(res[:], res[:], ACT.Tanh)
-            col = gains[:, 4 * b + t:4 * b + t + 1]
+            col = gains[b][:, t:t + 1]
             if gain_engine is nc.scalar:
                 nc.scalar.activation(res[:], res[:], ACT.Copy, scale=col)
             else:
                 gain_engine.tensor_scalar(res[:], res[:], col, 0.0, ALU.mult, ALU.add)
-            nc.sync.dma_start(out=out_rows[b, :, t, j0:j0 + HALF], in_=res[:])
+            nc.sync.dma_start(out=out_rows[b][:, t, j0:j0 + HALF], in_=res[:])
 
-        nc.sync.dma_start(seller_list[:], offs2)
+        seller_rows = zeroed("seller_rows", T // 4, nc.vector)
+        buyer_rows = zeroed("buyer_rows", T // 4, nc.vector)
+        house_rows = zeroed("house_rows", T3 // 4, nc.vector)
+        pair_planes = zeroed("pair_planes", 2 * S // 4, nc.vector)
+        w1_rows = zeroed("w1_rows", H // 4, nc.vector)
+        w4_rows = zeroed("w4_rows", N // 4, nc.vector)
+        w21_scales = zeroed("w21_scales", GROUP // 4, nc.vector)
+        seller_plane = pair_planes[:].bitcast(U8)[:, 0:S]
+        buyer_plane = pair_planes[:].bitcast(U8)[:, S:2 * S]
+
+        warm = held("warm", 8, F32)
+        nc.vector.memset(warm[:], 0.0)
+        nc.scalar.activation(warm[:, 1:2], warm[:, 0:1], ACT.Sigmoid)
+
+        seller_list = load_list("seller_list", offs2)
+        w1_raw = held("w1_raw", H // 2, I32)
         nc.sync.dma_start(out=w1_raw[:], in_=w1_words[0].bitcast(I32))
         load_rows(seller_rows, tab2_scales)
-        nc.sync.dma_start(buyer_list[:], offs)
+        buyer_list = load_list("buyer_list", offs)
         load_rows(buyer_rows, tab_scales)
-        w2_raw[0] = load_weight("w2_raw0", w2, 0, 0)
-        nc.sync.dma_start(house_list[:], offs3)
+        w1_codes = reorder_halfwords("w1_codes", w1_raw)
+        house_pair = held("house_planes", 2 * S // 4, I32, "w1_raw")
+        nc.gpsimd.memset(house_pair[:], 0)
+        house_planes = [house_pair[:, S // 4 * a:S // 4 * (a + 1)] for a in range(2)]
+        house_plane = [plane.bitcast(U8) for plane in house_planes]
+        w2_raw = load_weight("w2_raw", w2, 0, 0, H)
+        house_list = load_list("house_list", offs3)
         load_rows(house_rows, tab3_scales)
-        w2_raw[1] = load_weight("w2_raw1", w2, 0, GROUP)
         load_w1_plane(w1_rows)
         seller_tab = load_words("seller_tab", tab2_words[0].rearrange("p t i -> p (t i)"))
-
         pair_picked = held("pair_picked", 2 * S, U8)
         gather_into(pair_picked[:, 0:S], seller_rows, U8, seller_list[:])
         gather_into(pair_picked[:, S:2 * S], buyer_rows, U8, buyer_list[:])
         house_picked = held("house_picked", S, U8)
         gather_into(house_picked[:], house_rows, U8, house_list[:])
-        place_rows(pair_planes, pair_picked, 0, 8, range(4))
+        place_rows(pair_planes, pair_picked, 0, 8)
         buyer_tab = load_words("buyer_tab", tab_words[0].rearrange("p t i -> p (t i)"))
-        w3_raw[0, 0] = load_weight("w3_raw00", w3, 0, 0)
-        place_rows(house_planes[0], house_picked, 0, 4, range(4))
-        house_tab[0] = load_words("house_tab0", tab3_words[0])
-        w3_raw[1, 0] = load_weight("w3_raw10", w3, 1, 0)
-        place_rows(house_planes[1], house_picked, 64, 4, range(4))
-        house_tab[1] = load_words("house_tab1", tab3_words[1])
-        w3_raw[0, 1] = load_weight("w3_raw01", w3, 0, GROUP)
+        house_tab0 = load_words("house_tab0", tab3_words[0])
+        w3_raw00 = load_weight("w3_raw00", w3, 0, 0)
+        place_rows(house_planes[0], house_picked, 0, 4)
+        house_tab1 = load_words("house_tab1", tab3_words[1])
+        w3_raw10 = load_weight("w3_raw10", w3, 1, 0)
+        place_rows(house_planes[1], house_picked, 64, 4)
+        w3_raw01 = load_weight("w3_raw01", w3, 0, GROUP)
         w3_last = [load_weight("w3_last%d" % e, w3, 1, GROUP + GROUP // 2 * e, GROUP // 2) for e in range(2)]
+        w4_codes[1] = load_w4(1)
         load_w4_planes(w4_rows)
-        w4_raw[0] = load_w4(0)
-        nc.sync.dma_start(
-            out=gains[:].rearrange("p (b t) -> p b t", t=4),
-            in_=gain.rearrange("(b p t) -> p b t", b=2, t=4))
-        w4_raw[1] = load_w4(1)
-        seller_plane = pair_planes[:].bitcast(U8)[:, 0:S]
-        buyer_plane = pair_planes[:].bitcast(U8)[:, S:2 * S]
-        house_plane = [plane[:].bitcast(U8) for plane in house_planes]
+        gains = [held("gains%d" % b, 8, F32) for b in range(2)]
+        with nc.allow_non_contiguous_dma(reason="one gain a partition and slice"):
+            nc.sync.dma_start(out=gains[1][:, 0:4], in_=gain[GROUP:N].rearrange("(t p) -> p t", t=4))
+        w4_raw0 = load_w4(0)
+        nc.sync.dma_start(out=gains[0][:, 0:4], in_=gain[0:GROUP].rearrange("(p t) -> p t", t=4))
+        w4_planes[1] = w4_rows[:].bitcast(U8)[:, GROUP:N]
 
-        w2q[0] = quantise("w2_0", round_weight(0, w2_raw[0]), "buyer_rows")
-        rounded21 = round_weight(1, w2_raw[1])
-        for half in (1, 0):
-            seller_w[half] = gather_half("seller_w", seller_tab, U32, seller_list, half)
-        w2q[1] = quantise("w2_1", rounded21, "seller_tab")
-        w1_plane = reorder("w1_plane", w1_rows, U8, H, 16, "house_rows")
-        w1_codes = reorder("w1_codes", w1_raw, U16, H, 8)
-        for half in (1, 0):
-            buyer_w[half] = gather_half("buyer_w", buyer_tab, U32, buyer_list, half)
-        for b in range(2):
-            keep_seller(b)
-        logits0 = held("logits0", 4 * HALF, F32, "buyer_tab")[:]
-        kept_logits(logits0, 0)
-        logits1 = held("logits1", 4 * HALF, F32)[:]
-        kept_logits(logits1, 1)
-        repeated_logits(logits1)
-        rounded00 = round_on_gpsimd(2, w3_raw[0, 0])
-        gate_first_half(0)
+        first_banks, second_banks = (7, 0, 1, 2), (3, 4, 5, 6)
+
+        def round_shared(rounded, raw, gpsimd_cols, m0=0):
+            round_on_gpsimd(rounded, raw[:, :, 0:gpsimd_cols], m0)
+            round_columns(rounded, raw[:, :, gpsimd_cols:raw.shape[2]], m0 + gpsimd_cols // 4, nc.scalar)
+            return rounded
+
+        r20 = round_shared(rounded_tile("r20"), w2_raw[:, :, 0:GROUP], 256)
+        r21 = round_shared(rounded_tile("r21"), w2_raw[:, :, GROUP:H], 128)
+        w1_plane = reorder_on_gpsimd("w1_plane", w1_rows, U8, H, 16, 256)
+        w2q[0] = quantise("w2_0", r20, "house_rows")
         for half in range(2):
-            house_w[0, half] = gather_half("house_w0", house_tab[0], U16, house_list, half)
-        w3q[0, 0] = quantise("w3_00", rounded00, "house_tab0")
-        rounded10 = round_weight(0, w3_raw[1, 0])
-        gate_first_half(1, "w3_raw10")
-        house_w[1, 0] = gather_half("house_w1", house_tab[1], U16, house_list, 0)
-        w3q[1, 0] = quantise("w3_10", rounded10)
-        house_w[1, 1] = gather_half("house_w1", house_tab[1], U16, house_list, 1)
+            seller_w[half] = gather_half("seller_w", seller_tab, U32, seller_list, half)
+        w2q[1] = quantise("w2_1", r21, "seller_tab", w21_scales[:].bitcast(U8))
+        for half in range(2):
+            keep_seller(half)
+        w2_plain = (restore_order(held("w2_plain", GROUP, U32)[:], w2q[1][0][:]),
+                    restore_order(held("w2_plain_scales", GROUP, U8)[:], w2q[1][1]))
+        for half in range(2):
+            buyer_w[half] = gather_half("buyer_w", buyer_tab, U32, buyer_list, half)
+        kept_logits(0, "w2_raw")
+        kept_logits(1, "buyer_tab")
+        gate_from_logits(0)
+        for half in range(2):
+            house_w[0, half] = gather_half("house_w0", house_tab0, U16, house_list, half)
+        r00 = round_on_gpsimd(rounded_tile("r00", "r20"), w3_raw00)
+        gate_from_banks(0)
+        w3q[0, 0] = quantise("w3_00", r00, None)
+        for half in range(2):
+            house_w[1, half] = gather_half("house_w1", house_tab1, U16, house_list, half)
+        r10 = round_shared(rounded_tile("r10"), w3_raw10, 256)
+        gate_from_banks(1, "w3_raw10")
+        w3q[1, 0] = quantise("w3_10", r10)
         for u in range(4):
+            house_pass(0, 0, u, 0, first_banks[u])
+        r01 = round_shared(rounded_tile("r01", "r10"), w3_raw01, 384)
+        for u in range(4):
+            house_pass(0, 0, u, 1)
             gated_unit(0, 0, u)
-        w3q[0, 1] = quantise("w3_01", round_weight(1, w3_raw[0, 1]))
-        quantise_h(0, 0, "slot1")
-        w3q[1, 1] = quantise("w3_11", round_weight(0, *w3_last))
-        w4_codes[0] = reorder("w4_codes0", w4_raw[0], I32, 2 * GROUP, 4, "slot0", nc.gpsimd)
-        w4_plane = reorder("w4_plane", w4_rows, U8, N, 16)
-        gate_second_half(0, logits0, "w3_last1")
-        gate_second_half(1, logits1, "buyer_tab")
         for u in range(4):
+            house_pass(0, 1, u, 0, second_banks[u])
+            house_pass(0, 1, u, 1)
+        w3q[0, 1] = quantise("w3_01", r01)
+        r11 = rounded_tile("r11", "r21")
+        round_columns(r11, w3_last[0], 0, nc.scalar)
+        round_shared(r11, w3_last[1], 128, 64)
+        for u in range(4):
+            house_pass(1, 0, u, 0, first_banks[u])
+        w3q[1, 1] = quantise("w3_11", r11)
+        quantise_h(0, 0, "r21")
+        gate_from_logits(1, "w3_last1")
+        for u in range(4):
+            house_pass(1, 0, u, 1)
             gated_unit(1, 0, u)
+        quantise_h(1, 0)
+        w4_codes[0] = reorder_on_gpsimd("w4_codes0", w4_raw0, I32, 2 * GROUP, 4, 256, "h00")
+        w4_planes[0] = reorder_on_gpsimd("w4_plane0", w4_rows[:, 0:GROUP // 4], U8, GROUP, 16, 256, "h10")
         for u in range(4):
             gated_unit(0, 1, u)
-            if u == 0:
-                quantise_h(1, 0)
-        output_tile(0, 0, 0, nc.scalar)
-        output_tile(0, 1, 0, nc.scalar)
-        output_tile(0, 2, 0, nc.scalar)
-        output_tile(0, 3, 0, nc.scalar)
-        w4_codes[1] = reorder("w4_codes1", w4_raw[1], I32, 2 * GROUP, 4, "h10", nc.gpsimd)
+            output_tile(1, u, 0, nc.gpsimd, first_banks[u])
+        for u in range(4):
+            house_pass(1, 1, u, 0, second_banks[u])
+            house_pass(1, 1, u, 1)
+        quantise_h(0, 1)
         for u in range(4):
             gated_unit(1, 1, u)
-        output_tile(1, 0, 0, nc.scalar)
-        quantise_h(0, 1, "buyer_tab")
         quantise_h(1, 1)
-        output_tile(1, 1, 0, nc.gpsimd)
-        output_tile(1, 2, 0, nc.gpsimd)
-        output_tile(0, 0, 1, nc.gpsimd)
-        output_tile(0, 1, 1, nc.gpsimd)
-        output_tile(0, 2, 1, nc.gpsimd)
-        output_tile(0, 3, 1, nc.gpsimd)
-        output_tile(1, 0, 1, nc.vector)
-        output_tile(1, 1, 1, nc.vector)
-        output_tile(1, 2, 1, nc.vector)
-        output_tile(1, 3, 0, nc.vector)
-        output_tile(1, 3, 1, nc.vector)
+        for t in range(4):
+            output_tile(0, t, 0, nc.gpsimd, first_banks[t])
+        for t in range(4):
+            output_tile(1, t, 1, nc.gpsimd, second_banks[t])
+        for t in range(4):
+            output_tile(0, t, 1, nc.vector, first_banks[t])

@@ -20,6 +20,7 @@ P = 128
 BANK = 512
 GROUP = 512
 HALF = S // 2
+QUARTER = S // 4
 UNIT = S // 8
 BANKS = 8
 RESULT_SLOTS = 12
@@ -135,14 +136,6 @@ def tile_list_haggling_features_kernel(
                 round_columns(rounded, raw[:, :, P * e:P * (e + 1)], m0 + 32 * e, nc.gpsimd)
             return rounded
 
-        def reorder_halfwords(name, raw):
-            ordered = held(name, H, U16)
-            for b in range(2):
-                nc.gpsimd.tensor_copy(
-                    out=ordered[:].bitcast(U8).rearrange("p (b t c i e) -> p b c t i e", b=2, t=4, i=8, e=2)[:, b],
-                    in_=raw[:].bitcast(U8).rearrange("p (b c i t e) -> p b c t i e", b=2, t=4, i=8, e=2)[:, b])
-            return ordered
-
         def reorder(name, raw, dtype, cols, run, engine, after=None):
             ordered = held(name, cols, dtype, after)
             engine.tensor_copy(
@@ -205,27 +198,28 @@ def tile_list_haggling_features_kernel(
         def gate_from_logits(half, after=None):
             gate[0, half] = held("gate0%d" % half, 4 * HALF, F32, after)
             nc.scalar.activation(
-                gate[0, half][:].rearrange("p (c i t) -> p c t i", i=4, t=4),
-                logits[half][:].rearrange("p (t c i) -> p c t i", i=4, t=4), ACT.Sigmoid)
+                gate[0, half][:].rearrange("p (s j e) -> p s j e", s=2, e=2),
+                logits[half][:].rearrange("p (s e j) -> p s j e", s=2, e=2), ACT.Sigmoid)
 
         def gate_from_banks(half, after=None):
             gate[1, half] = held("gate1%d" % half, 4 * HALF, F32, after)
-            for u in range(4):
-                bank = next_bank()
-                j0 = HALF * half + UNIT * u
-                for t in range(4):
-                    seller_pass(bank[:, UNIT * t:UNIT * (t + 1)], w2q[1], t, j0, UNIT, t == 0, False)
-                for t in range(4):
-                    buyer_pass(bank[:, UNIT * t:UNIT * (t + 1)], 1, t, j0, UNIT, False, t == 3)
-                nc.scalar.activation(
-                    gate[1, half][:, BANK * u:BANK * (u + 1)].rearrange("p (j t) -> p j t", t=4),
-                    bank[:].rearrange("p (t j) -> p j t", t=4), ACT.Sigmoid)
+            for c0 in (0, QUARTER):
+                for s in range(2):
+                    bank = next_bank()
+                    j0 = HALF * half + c0
+                    for e in range(2):
+                        seller_pass(bank[:, QUARTER * e:QUARTER * (e + 1)], w2q[1], 2 * s + e, j0, QUARTER, e == 0, False)
+                    for e in range(2):
+                        buyer_pass(bank[:, QUARTER * e:QUARTER * (e + 1)], 1, 2 * s + e, j0, QUARTER, False, e == 1)
+                    nc.scalar.activation(
+                        gate[1, half][:].rearrange("p (s j e) -> p s j e", s=2, e=2)[:, s, c0:c0 + QUARTER, :],
+                        bank[:].rearrange("p (e j) -> p j e", e=2), ACT.Sigmoid)
 
-        def restore_order(plain, ordered):
-            for m0 in (0, P // 2):
-                nc.gpsimd.tensor_copy(
-                    out=plain.rearrange("p (m t) -> p m t", t=4)[:, m0:m0 + P // 2],
-                    in_=ordered.rearrange("p (t m) -> p m t", t=4)[:, m0:m0 + P // 2])
+        def restore_order(plain, ordered, engine, pieces):
+            for m0 in range(0, P, P // pieces):
+                engine.tensor_copy(
+                    out=plain.rearrange("p (m t) -> p m t", t=4)[:, m0:m0 + P // pieces],
+                    in_=ordered.rearrange("p (t m) -> p m t", t=4)[:, m0:m0 + P // pieces])
             return plain
 
         house_banks = {}
@@ -248,9 +242,9 @@ def tile_list_haggling_features_kernel(
             if u == 0:
                 h_rounded[b, half] = held("h%d%d" % (b, half), 4 * HALF, BF16, after)
             nc.vector.tensor_tensor(
-                h_rounded[b, half][:, BANK * u:BANK * (u + 1)].rearrange("p (j t) -> p j t", t=4),
-                house_banks[b, half, u][:].rearrange("p (t j) -> p j t", t=4),
-                gate[b, half][:, BANK * u:BANK * (u + 1)].rearrange("p (j t) -> p j t", t=4), ALU.mult)
+                h_rounded[b, half][:, BANK * u:BANK * (u + 1)].rearrange("p (j s e) -> p j s e", s=2, e=2),
+                house_banks[b, half, u][:].rearrange("p (s e j) -> p j s e", s=2, e=2),
+                gate[b, half][:].rearrange("p (s j e) -> p j s e", s=2, e=2)[:, UNIT * u:UNIT * (u + 1)], ALU.mult)
 
         def gated_half(b, half, after=None):
             for u in range(4):
@@ -311,9 +305,7 @@ def tile_list_haggling_features_kernel(
         load_rows(seller_rows, tab2_scales)
         buyer_list = load_list("buyer_list", offs)
         load_rows(buyer_rows, tab_scales)
-        w1_codes = reorder_halfwords("w1_codes", w1_raw)
-        house_pair = held("house_planes", 2 * S // 4, I32, "w1_raw")
-        nc.gpsimd.memset(house_pair[:], 0)
+        house_pair = zeroed("house_planes", 2 * S // 4, nc.vector)
         house_planes = [house_pair[:, S // 4 * a:S // 4 * (a + 1)] for a in range(2)]
         house_plane = [plane.bitcast(U8) for plane in house_planes]
         w2_raw = load_weight("w2_raw", w2, 0, 0, H)
@@ -324,6 +316,7 @@ def tile_list_haggling_features_kernel(
         pair_picked = held("pair_picked", 2 * S, U8)
         gather_into(pair_picked[:, 0:S], seller_rows, U8, seller_list[:])
         gather_into(pair_picked[:, S:2 * S], buyer_rows, U8, buyer_list[:])
+        w1_codes = reorder("w1_codes", w1_raw, U16, H, 8, nc.vector)
         house_picked = held("house_picked", S, U8)
         gather_into(house_picked[:], house_rows, U8, house_list[:])
         place_rows(pair_planes, pair_picked, 0, 8)
@@ -332,16 +325,16 @@ def tile_list_haggling_features_kernel(
         w3_raw00 = load_weight("w3_raw00", w3, 0, 0)
         place_rows(house_planes[0], house_picked, 0, 4)
         house_tab1 = load_words("house_tab1", tab3_words[1])
-        w3_raw10 = load_weight("w3_raw10", w3, 1, 0)
+        w3_raw10 = [load_weight("w3_raw10%d" % e, w3, 1, GROUP // 2 * e, GROUP // 2) for e in range(2)]
         place_rows(house_planes[1], house_picked, 64, 4)
         w3_raw01 = load_weight("w3_raw01", w3, 0, GROUP)
         w3_last = [load_weight("w3_last%d" % e, w3, 1, GROUP + GROUP // 2 * e, GROUP // 2) for e in range(2)]
+        w4_raw0 = load_w4(0)
         w4_codes[1] = load_w4(1)
         load_w4_planes(w4_rows)
         gains = [held("gains%d" % b, 8, F32) for b in range(2)]
         with nc.allow_non_contiguous_dma(reason="one gain a partition and slice"):
             nc.sync.dma_start(out=gains[1][:, 0:4], in_=gain[GROUP:N].rearrange("(t p) -> p t", t=4))
-        w4_raw0 = load_w4(0)
         nc.sync.dma_start(out=gains[0][:, 0:4], in_=gain[0:GROUP].rearrange("(p t) -> p t", t=4))
         w4_planes[1] = w4_rows[:].bitcast(U8)[:, GROUP:N]
 
@@ -354,33 +347,34 @@ def tile_list_haggling_features_kernel(
 
         r20 = round_shared(rounded_tile("r20"), w2_raw[:, :, 0:GROUP], 256)
         r21 = round_shared(rounded_tile("r21"), w2_raw[:, :, GROUP:H], 128)
-        w1_plane = reorder_on_gpsimd("w1_plane", w1_rows, U8, H, 16, 256)
         w2q[0] = quantise("w2_0", r20, "house_rows")
+        w2q[1] = quantise("w2_1", r21, None, w21_scales[:].bitcast(U8))
+        w1_plane = reorder_on_gpsimd("w1_plane", w1_rows, U8, H, 16, 512, "r21")
         for half in range(2):
             seller_w[half] = gather_half("seller_w", seller_tab, U32, seller_list, half)
-        w2q[1] = quantise("w2_1", r21, "seller_tab", w21_scales[:].bitcast(U8))
         for half in range(2):
             keep_seller(half)
-        w2_plain = (restore_order(held("w2_plain", GROUP, U32)[:], w2q[1][0][:]),
-                    restore_order(held("w2_plain_scales", GROUP, U8)[:], w2q[1][1]))
+        w2_plain = (restore_order(held("w2_plain", GROUP, U32, "w1_rows")[:], w2q[1][0][:], nc.gpsimd, 1),
+                    restore_order(held("w2_plain_scales", GROUP, U8)[:], w2q[1][1], nc.vector, 1))
         for half in range(2):
             buyer_w[half] = gather_half("buyer_w", buyer_tab, U32, buyer_list, half)
         kept_logits(0, "w2_raw")
-        kept_logits(1, "buyer_tab")
+        gate_from_banks(0, "seller_tab")
         gate_from_logits(0)
         for half in range(2):
             house_w[0, half] = gather_half("house_w0", house_tab0, U16, house_list, half)
+        kept_logits(1, "buyer_tab")
         r00 = round_on_gpsimd(rounded_tile("r00", "r20"), w3_raw00)
-        gate_from_banks(0)
         w3q[0, 0] = quantise("w3_00", r00, None)
         for half in range(2):
             house_w[1, half] = gather_half("house_w1", house_tab1, U16, house_list, half)
-        r10 = round_shared(rounded_tile("r10"), w3_raw10, 256)
-        gate_from_banks(1, "w3_raw10")
+        r10 = round_on_gpsimd(rounded_tile("r10", "r20"), w3_raw10[0])
+        round_columns(r10, w3_raw10[1], 64, nc.scalar)
+        gate_from_banks(1, "w3_raw101")
         w3q[1, 0] = quantise("w3_10", r10)
         for u in range(4):
             house_pass(0, 0, u, 0, first_banks[u])
-        r01 = round_shared(rounded_tile("r01", "r10"), w3_raw01, 384)
+        r01 = round_shared(rounded_tile("r01", "r20"), w3_raw01, 384)
         for u in range(4):
             house_pass(0, 0, u, 1)
             gated_unit(0, 0, u)
@@ -394,14 +388,14 @@ def tile_list_haggling_features_kernel(
         for u in range(4):
             house_pass(1, 0, u, 0, first_banks[u])
         w3q[1, 1] = quantise("w3_11", r11)
+        w4_codes[0] = reorder("w4_codes0", w4_raw0, I32, 2 * GROUP, 4, nc.vector)
         quantise_h(0, 0, "r21")
         gate_from_logits(1, "w3_last1")
         for u in range(4):
             house_pass(1, 0, u, 1)
             gated_unit(1, 0, u)
         quantise_h(1, 0)
-        w4_codes[0] = reorder_on_gpsimd("w4_codes0", w4_raw0, I32, 2 * GROUP, 4, 256, "h00")
-        w4_planes[0] = reorder_on_gpsimd("w4_plane0", w4_rows[:, 0:GROUP // 4], U8, GROUP, 16, 256, "h10")
+        w4_planes[0] = reorder("w4_plane0", w4_rows[:, 0:GROUP // 4], U8, GROUP, 16, nc.vector, "h10")
         for u in range(4):
             gated_unit(0, 1, u)
             output_tile(1, u, 0, nc.gpsimd, first_banks[u])

@@ -49,8 +49,8 @@ def tile_list_haggling_features_kernel(
             name = slot_name("bank", BANKS) if which is None else "bank%d" % which
             return psum.tile([P, BANK], F32, name=name)
 
-        def zeroed(name, cols, engine):
-            tile = held(name, cols, I32)
+        def zeroed(name, cols, engine, after=None):
+            tile = held(name, cols, I32, after)
             engine.memset(tile[:], 0)
             return tile
 
@@ -67,10 +67,6 @@ def tile_list_haggling_features_kernel(
             for i in range(4):
                 src = picked[:].bitcast(I32)[first + step * i:first + 16 * step:4 * step, :]
                 nc.sync.dma_start(out=plane[i:P:32, :], in_=src)
-
-        def load_w1_plane(tile):
-            for i in range(4):
-                nc.sync.dma_start(out=tile[i:P:32, :], in_=w1_scales[0, i:16:4, :].bitcast(I32))
 
         def load_w4_planes(tile):
             for quad in (0, 2, 1, 3):
@@ -208,9 +204,9 @@ def tile_list_haggling_features_kernel(
                     bank = next_bank()
                     j0 = HALF * half + c0
                     for e in range(2):
-                        seller_pass(bank[:, QUARTER * e:QUARTER * (e + 1)], w2q[1], 2 * s + e, j0, QUARTER, e == 0, False)
+                        buyer_pass(bank[:, QUARTER * e:QUARTER * (e + 1)], 1, 2 * s + e, j0, QUARTER, e == 0, False)
                     for e in range(2):
-                        buyer_pass(bank[:, QUARTER * e:QUARTER * (e + 1)], 1, 2 * s + e, j0, QUARTER, False, e == 1)
+                        seller_pass(bank[:, QUARTER * e:QUARTER * (e + 1)], w2q[1], 2 * s + e, j0, QUARTER, False, e == 1)
                     nc.scalar.activation(
                         gate[1, half][:].rearrange("p (s j e) -> p s j e", s=2, e=2)[:, s, c0:c0 + QUARTER, :],
                         bank[:].rearrange("p (e j) -> p j e", e=2), ACT.Sigmoid)
@@ -238,22 +234,39 @@ def tile_list_haggling_features_kernel(
                     rhs_scale=house_plane[a][:, j0:j0 + UNIT],
                     start=(a == 0 and t == 0), stop=(a == 1 and t == 3))
 
-        def gated_unit(b, half, u, after=None):
-            if u == 0:
-                h_rounded[b, half] = held("h%d%d" % (b, half), 4 * HALF, BF16, after)
+        def h_tile(b, half, units, after=None):
+            tile = held("h%d%d%d" % (b, half, units[0]), BANK * len(units), BF16, after)
+            h_tiles.setdefault((b, half), []).append((units, tile))
+            for i, u in enumerate(units):
+                h_rounded[b, half, u] = tile[:, BANK * i:BANK * (i + 1)]
+
+        h_tiles = {}
+
+        def gated_unit(b, half, u):
             nc.vector.tensor_tensor(
-                h_rounded[b, half][:, BANK * u:BANK * (u + 1)].rearrange("p (j s e) -> p j s e", s=2, e=2),
+                h_rounded[b, half, u].rearrange("p (j s e) -> p j s e", s=2, e=2),
                 house_banks[b, half, u][:].rearrange("p (s e j) -> p j s e", s=2, e=2),
                 gate[b, half][:].rearrange("p (s j e) -> p j s e", s=2, e=2)[:, UNIT * u:UNIT * (u + 1)], ALU.mult)
 
-        def gated_half(b, half, after=None):
-            for u in range(4):
-                house_pass(b, half, u, 0)
-                house_pass(b, half, u, 1)
-                gated_unit(b, half, u, after)
+        def gated_unit_off_vector(b, half, u, staged):
+            dst = h_rounded[b, half, u]
+            house = staged[:, BANK * u:BANK * (u + 1)]
+            nc.scalar.copy(
+                out=house.rearrange("p (j t) -> p j t", t=4), in_=house_banks[b, half, u][:].rearrange("p (t j) -> p j t", t=4))
+            for c0 in (0, UNIT // 2):
+                entries = slice(c0, c0 + UNIT // 2)
+                nc.gpsimd.tensor_tensor(
+                    dst.rearrange("p (j s e) -> p j s e", s=2, e=2)[:, entries],
+                    house.rearrange("p (j s e) -> p j s e", s=2, e=2)[:, entries],
+                    gate[b, half][:].rearrange("p (s j e) -> p j s e", s=2, e=2)[:, UNIT * u + c0:UNIT * u + c0 + UNIT // 2],
+                    ALU.mult)
 
         def quantise_h(b, half, after=None):
-            hq[b, half] = quantise("h%d%d" % (b, half), h_rounded[b, half], after)
+            codes, scales = held("h%d%d_codes" % (b, half), HALF, U32, after), held("h%d%d_scales" % (b, half), HALF, U8)
+            for units, tile in h_tiles[b, half]:
+                entries = slice(UNIT * units[0], UNIT * (units[-1] + 1))
+                nc.vector.quantize_mx(out=codes[:, entries].bitcast(FP8X4), scales=scales[:, entries], in_=tile[:])
+            hq[b, half] = codes, scales
 
         out_rows = [out[0:GROUP, :].rearrange("(p t) j -> p t j", t=4), out[GROUP:N, :].rearrange("(t p) j -> p t j", t=4)]
         w4_codes, w4_planes = {}, {}
@@ -287,17 +300,19 @@ def tile_list_haggling_features_kernel(
 
         seller_rows = zeroed("seller_rows", T // 4, nc.vector)
         buyer_rows = zeroed("buyer_rows", T // 4, nc.vector)
-        house_rows = zeroed("house_rows", T3 // 4, nc.vector)
-        pair_planes = zeroed("pair_planes", 2 * S // 4, nc.vector)
         w1_rows = zeroed("w1_rows", H // 4, nc.vector)
-        w4_rows = zeroed("w4_rows", N // 4, nc.vector)
-        w21_scales = zeroed("w21_scales", GROUP // 4, nc.vector)
-        seller_plane = pair_planes[:].bitcast(U8)[:, 0:S]
-        buyer_plane = pair_planes[:].bitcast(U8)[:, S:2 * S]
+        house_rows = zeroed("house_rows", T3 // 4, nc.vector)
 
         warm = held("warm", 8, F32)
         nc.vector.memset(warm[:], 0.0)
         nc.scalar.activation(warm[:, 1:2], warm[:, 0:1], ACT.Sigmoid)
+
+        pair_planes = zeroed("pair_planes", 2 * S // 4, nc.vector)
+        w1_planes = zeroed("w1_plane", H // 4, nc.vector)
+        w21_scales = zeroed("w21_scales", GROUP // 4, nc.vector)
+        seller_plane = pair_planes[:].bitcast(U8)[:, 0:S]
+        buyer_plane = pair_planes[:].bitcast(U8)[:, S:2 * S]
+        w1_plane = w1_planes[:].bitcast(U8)
 
         seller_list = load_list("seller_list", offs2)
         w1_raw = held("w1_raw", H // 2, I32)
@@ -305,27 +320,30 @@ def tile_list_haggling_features_kernel(
         load_rows(seller_rows, tab2_scales)
         buyer_list = load_list("buyer_list", offs)
         load_rows(buyer_rows, tab_scales)
-        house_pair = zeroed("house_planes", 2 * S // 4, nc.vector)
-        house_planes = [house_pair[:, S // 4 * a:S // 4 * (a + 1)] for a in range(2)]
-        house_plane = [plane.bitcast(U8) for plane in house_planes]
+        load_rows(w1_rows, w1_scales)
         w2_raw = load_weight("w2_raw", w2, 0, 0, H)
         house_list = load_list("house_list", offs3)
         load_rows(house_rows, tab3_scales)
-        load_w1_plane(w1_rows)
         seller_tab = load_words("seller_tab", tab2_words[0].rearrange("p t i -> p (t i)"))
+        w1_codes = reorder("w1_codes", w1_raw, U16, H, 8, nc.vector)
+        w1_ordered = reorder_on_gpsimd("w1_ordered", w1_rows, U8, H, 16, 512)
+        house_pair = zeroed("house_planes", 2 * S // 4, nc.gpsimd, "w1_rows")
+        w4_rows = zeroed("w4_rows", N // 4, nc.gpsimd, "w1_raw")
+        house_planes = [house_pair[:, S // 4 * a:S // 4 * (a + 1)] for a in range(2)]
+        house_plane = [plane.bitcast(U8) for plane in house_planes]
         pair_picked = held("pair_picked", 2 * S, U8)
         gather_into(pair_picked[:, 0:S], seller_rows, U8, seller_list[:])
         gather_into(pair_picked[:, S:2 * S], buyer_rows, U8, buyer_list[:])
-        w1_codes = reorder("w1_codes", w1_raw, U16, H, 8, nc.vector)
         house_picked = held("house_picked", S, U8)
         gather_into(house_picked[:], house_rows, U8, house_list[:])
         place_rows(pair_planes, pair_picked, 0, 8)
         buyer_tab = load_words("buyer_tab", tab_words[0].rearrange("p t i -> p (t i)"))
-        house_tab0 = load_words("house_tab0", tab3_words[0])
+        place_rows(w1_planes, w1_ordered, 0, 8)
         w3_raw00 = load_weight("w3_raw00", w3, 0, 0)
+        house_tab0 = load_words("house_tab0", tab3_words[0])
         place_rows(house_planes[0], house_picked, 0, 4)
+        w3_raw10 = load_weight("w3_raw10", w3, 1, 0)
         house_tab1 = load_words("house_tab1", tab3_words[1])
-        w3_raw10 = [load_weight("w3_raw10%d" % e, w3, 1, GROUP // 2 * e, GROUP // 2) for e in range(2)]
         place_rows(house_planes[1], house_picked, 64, 4)
         w3_raw01 = load_weight("w3_raw01", w3, 0, GROUP)
         w3_last = [load_weight("w3_last%d" % e, w3, 1, GROUP + GROUP // 2 * e, GROUP // 2) for e in range(2)]
@@ -349,66 +367,76 @@ def tile_list_haggling_features_kernel(
         r21 = round_shared(rounded_tile("r21"), w2_raw[:, :, GROUP:H], 128)
         w2q[0] = quantise("w2_0", r20, "house_rows")
         w2q[1] = quantise("w2_1", r21, None, w21_scales[:].bitcast(U8))
-        w1_plane = reorder_on_gpsimd("w1_plane", w1_rows, U8, H, 16, 512, "r21")
         for half in range(2):
             seller_w[half] = gather_half("seller_w", seller_tab, U32, seller_list, half)
         for half in range(2):
             keep_seller(half)
-        w2_plain = (restore_order(held("w2_plain", GROUP, U32, "w1_rows")[:], w2q[1][0][:], nc.gpsimd, 1),
-                    restore_order(held("w2_plain_scales", GROUP, U8)[:], w2q[1][1], nc.vector, 1))
+        w2_plain = (restore_order(held("w2_plain", GROUP, U32)[:], w2q[1][0][:], nc.gpsimd, 1),
+                    restore_order(held("w2_plain_scales", GROUP, U8)[:], w2q[1][1], nc.gpsimd, 1))
         for half in range(2):
             buyer_w[half] = gather_half("buyer_w", buyer_tab, U32, buyer_list, half)
         kept_logits(0, "w2_raw")
         gate_from_banks(0, "seller_tab")
-        gate_from_logits(0)
-        for half in range(2):
-            house_w[0, half] = gather_half("house_w0", house_tab0, U16, house_list, half)
-        kept_logits(1, "buyer_tab")
+        gate_from_logits(0, "buyer_tab")
         r00 = round_on_gpsimd(rounded_tile("r00", "r20"), w3_raw00)
+        house_w[0, 0] = gather_half("house_w0", house_tab0, U16, house_list, 0)
         w3q[0, 0] = quantise("w3_00", r00, None)
-        for half in range(2):
-            house_w[1, half] = gather_half("house_w1", house_tab1, U16, house_list, half)
-        r10 = round_on_gpsimd(rounded_tile("r10", "r20"), w3_raw10[0])
-        round_columns(r10, w3_raw10[1], 64, nc.scalar)
-        gate_from_banks(1, "w3_raw101")
+        kept_logits(1, "r20")
+        gate_from_banks(1, "w3_raw00")
+        house_w[0, 1] = gather_half("house_w0", house_tab0, U16, house_list, 1)
+        r10 = round_on_gpsimd(rounded_tile("r10"), w3_raw10)
+        house_w[1, 0] = gather_half("house_w1", house_tab1, U16, house_list, 0)
         w3q[1, 0] = quantise("w3_10", r10)
+        house_w[1, 1] = gather_half("house_w1", house_tab1, U16, house_list, 1, "r10")
         for u in range(4):
             house_pass(0, 0, u, 0, first_banks[u])
-        r01 = round_shared(rounded_tile("r01", "r20"), w3_raw01, 384)
-        for u in range(4):
-            house_pass(0, 0, u, 1)
-            gated_unit(0, 0, u)
         for u in range(4):
             house_pass(0, 1, u, 0, second_banks[u])
-            house_pass(0, 1, u, 1)
+        r01 = round_shared(rounded_tile("r01"), w3_raw01, 256)
+        for u in range(4):
+            house_pass(0, 0, u, 1)
+        h_tile(0, 0, (0, 1))
+        for u in range(2):
+            gated_unit(0, 0, u)
         w3q[0, 1] = quantise("w3_01", r01)
+        h_tile(0, 0, (2, 3), "r01")
+        for u in range(2, 4):
+            gated_unit(0, 0, u)
+        for u in range(4):
+            house_pass(0, 1, u, 1)
         r11 = rounded_tile("r11", "r21")
         round_columns(r11, w3_last[0], 0, nc.scalar)
-        round_shared(r11, w3_last[1], 128, 64)
+        round_columns(r11, w3_last[1], 64, nc.scalar)
         for u in range(4):
             house_pass(1, 0, u, 0, first_banks[u])
         w3q[1, 1] = quantise("w3_11", r11)
         w4_codes[0] = reorder("w4_codes0", w4_raw0, I32, 2 * GROUP, 4, nc.vector)
         quantise_h(0, 0, "r21")
         gate_from_logits(1, "w3_last1")
+        staged = held("staged", 4 * HALF, F32, "r20")
+        h_tile(0, 1, (0, 1, 2, 3))
+        for u in range(3):
+            gated_unit_off_vector(0, 1, u, staged)
+        h_tile(1, 0, (0, 1, 2, 3))
         for u in range(4):
             house_pass(1, 0, u, 1)
             gated_unit(1, 0, u)
         quantise_h(1, 0)
-        w4_planes[0] = reorder("w4_plane0", w4_rows[:, 0:GROUP // 4], U8, GROUP, 16, nc.vector, "h10")
-        for u in range(4):
+        for u in range(3, 4):
             gated_unit(0, 1, u)
-            output_tile(1, u, 0, nc.gpsimd, first_banks[u])
+        w4_planes[0] = reorder("w4_plane0", w4_rows[:, 0:GROUP // 4], U8, GROUP, 16, nc.vector, "h100")
         for u in range(4):
             house_pass(1, 1, u, 0, second_banks[u])
             house_pass(1, 1, u, 1)
-        quantise_h(0, 1)
+        h_tile(1, 1, (0, 1, 2, 3))
         for u in range(4):
             gated_unit(1, 1, u)
+            output_tile(1, u, 0, nc.scalar if u < 2 else nc.gpsimd, first_banks[u])
         quantise_h(1, 1)
+        quantise_h(0, 1)
         for t in range(4):
-            output_tile(0, t, 0, nc.gpsimd, first_banks[t])
+            output_tile(0, t, 0, nc.gpsimd if t < 2 else nc.vector, first_banks[t])
         for t in range(4):
-            output_tile(1, t, 1, nc.gpsimd, second_banks[t])
+            output_tile(1, t, 1, nc.vector, second_banks[t])
         for t in range(4):
             output_tile(0, t, 1, nc.vector, first_banks[t])

@@ -197,6 +197,12 @@ def tile_list_haggling_features_kernel(
                 gate[0, half][:].rearrange("p (s j e) -> p s j e", s=2, e=2),
                 logits[half][:].rearrange("p (s e j) -> p s j e", s=2, e=2), ACT.Sigmoid)
 
+        def gate_in_h_order(half, after=None):
+            gate[0, half] = held("gate0%d" % half, 4 * HALF, F32, after)
+            nc.scalar.activation(
+                gate[0, half][:].rearrange("p (c i t) -> p c t i", i=4, t=4),
+                logits[half][:].rearrange("p (t c i) -> p c t i", i=4, t=4), ACT.Sigmoid)
+
         def gate_from_banks(half, after=None):
             gate[1, half] = held("gate1%d" % half, 4 * HALF, F32, after)
             for c0 in (0, QUARTER):
@@ -243,23 +249,21 @@ def tile_list_haggling_features_kernel(
         h_tiles = {}
 
         def gated_unit(b, half, u):
+            layout = "p (j s e) -> p j s e" if (b, half) == (0, 1) else "p (s j e) -> p j s e"
             nc.vector.tensor_tensor(
                 h_rounded[b, half, u].rearrange("p (j s e) -> p j s e", s=2, e=2),
                 house_banks[b, half, u][:].rearrange("p (s e j) -> p j s e", s=2, e=2),
-                gate[b, half][:].rearrange("p (s j e) -> p j s e", s=2, e=2)[:, UNIT * u:UNIT * (u + 1)], ALU.mult)
+                gate[b, half][:].rearrange(layout, s=2, e=2)[:, UNIT * u:UNIT * (u + 1)], ALU.mult)
 
-        def gated_unit_off_vector(b, half, u, staged):
+        def gated_unit_off_vector(b, half, u, staged, piece):
             dst = h_rounded[b, half, u]
             house = staged[:, BANK * u:BANK * (u + 1)]
             nc.scalar.copy(
                 out=house.rearrange("p (j t) -> p j t", t=4), in_=house_banks[b, half, u][:].rearrange("p (t j) -> p j t", t=4))
-            for c0 in (0, UNIT // 2):
-                entries = slice(c0, c0 + UNIT // 2)
+            for c0 in range(0, BANK, piece):
                 nc.gpsimd.tensor_tensor(
-                    dst.rearrange("p (j s e) -> p j s e", s=2, e=2)[:, entries],
-                    house.rearrange("p (j s e) -> p j s e", s=2, e=2)[:, entries],
-                    gate[b, half][:].rearrange("p (s j e) -> p j s e", s=2, e=2)[:, UNIT * u + c0:UNIT * u + c0 + UNIT // 2],
-                    ALU.mult)
+                    dst[:, c0:c0 + piece], house[:, c0:c0 + piece],
+                    gate[b, half][:, BANK * u + c0:BANK * u + c0 + piece], ALU.mult)
 
         def quantise_h(b, half, after=None):
             codes, scales = held("h%d%d_codes" % (b, half), HALF, U32, after), held("h%d%d_scales" % (b, half), HALF, U8)
@@ -412,11 +416,11 @@ def tile_list_haggling_features_kernel(
         w3q[1, 1] = quantise("w3_11", r11)
         w4_codes[0] = reorder("w4_codes0", w4_raw0, I32, 2 * GROUP, 4, nc.vector)
         quantise_h(0, 0, "r21")
-        gate_from_logits(1, "w3_last1")
+        gate_in_h_order(1, "w3_last1")
         staged = held("staged", 4 * HALF, F32, "r20")
         h_tile(0, 1, (0, 1, 2, 3))
         for u in range(3):
-            gated_unit_off_vector(0, 1, u, staged)
+            gated_unit_off_vector(0, 1, u, staged, 256)
         h_tile(1, 0, (0, 1, 2, 3))
         for u in range(4):
             house_pass(1, 0, u, 1)
@@ -435,8 +439,8 @@ def tile_list_haggling_features_kernel(
         quantise_h(1, 1)
         quantise_h(0, 1)
         for t in range(4):
-            output_tile(0, t, 0, nc.gpsimd if t < 2 else nc.vector, first_banks[t])
+            output_tile(0, t, 0, nc.gpsimd, first_banks[t])
         for t in range(4):
-            output_tile(1, t, 1, nc.vector, second_banks[t])
+            output_tile(0, t, 1, nc.vector, second_banks[t])
         for t in range(4):
-            output_tile(0, t, 1, nc.vector, first_banks[t])
+            output_tile(1, t, 1, nc.vector, first_banks[t])

@@ -325,9 +325,10 @@ def tile_list_haggling_features_kernel(
         buyer_list = load_list("buyer_list", offs)
         load_rows(buyer_rows, tab_scales)
         load_rows(w1_rows, w1_scales)
-        w2_raw = load_weight("w2_raw", w2, 0, 0, H)
+        w2_raw = [load_weight("w2_raw0", w2, 0, 0)]
         house_list = load_list("house_list", offs3)
         load_rows(house_rows, tab3_scales)
+        w2_raw.append(load_weight("w2_raw1", w2, 0, GROUP))
         seller_tab = load_words("seller_tab", tab2_words[0].rearrange("p t i -> p (t i)"))
         w1_codes = reorder("w1_codes", w1_raw, U16, H, 8, nc.vector)
         w1_ordered = reorder_on_gpsimd("w1_ordered", w1_rows, U8, H, 16, 512)
@@ -367,8 +368,8 @@ def tile_list_haggling_features_kernel(
             round_columns(rounded, raw[:, :, gpsimd_cols:raw.shape[2]], m0 + gpsimd_cols // 4, nc.scalar)
             return rounded
 
-        r20 = round_shared(rounded_tile("r20"), w2_raw[:, :, 0:GROUP], 256)
-        r21 = round_shared(rounded_tile("r21"), w2_raw[:, :, GROUP:H], 128)
+        r20 = round_group("r20", w2_raw[0], nc.scalar)
+        r21 = round_shared(rounded_tile("r21"), w2_raw[1], 128)
         w2q[0] = quantise("w2_0", r20, "house_rows")
         w2q[1] = quantise("w2_1", r21, None, w21_scales[:].bitcast(U8))
         for half in range(2):
@@ -379,9 +380,9 @@ def tile_list_haggling_features_kernel(
                     restore_order(held("w2_plain_scales", GROUP, U8)[:], w2q[1][1], nc.gpsimd, 1))
         for half in range(2):
             buyer_w[half] = gather_half("buyer_w", buyer_tab, U32, buyer_list, half)
-        kept_logits(0, "w2_raw")
+        kept_logits(0, "w2_raw0")
         gate_from_banks(0, "seller_tab")
-        gate_from_logits(0, "buyer_tab")
+        gate_from_logits(0, "w2_raw1")
         r00 = round_on_gpsimd(rounded_tile("r00", "r20"), w3_raw00)
         house_w[0, 0] = gather_half("house_w0", house_tab0, U16, house_list, 0)
         w3q[0, 0] = quantise("w3_00", r00, None)
@@ -403,7 +404,7 @@ def tile_list_haggling_features_kernel(
         for u in range(2):
             gated_unit(0, 0, u)
         w3q[0, 1] = quantise("w3_01", r01)
-        h_tile(0, 0, (2, 3), "r01")
+        h_tile(0, 0, (2, 3), "w3_raw01")
         for u in range(2, 4):
             gated_unit(0, 0, u)
         for u in range(4):

@@ -24,7 +24,7 @@ QUARTER = S // 4
 UNIT = S // 8
 BANKS = 8
 RESULT_SLOTS = 12
-REPEATED_SLICE = (3, 1)
+KEPT_ENTRIES = {(2, 1): 256, (3, 1): 0}
 
 
 def tile_list_haggling_features_kernel(
@@ -173,23 +173,25 @@ def tile_list_haggling_features_kernel(
         def keep_seller(half, after=None):
             kept[half] = held("kept%d" % half, 4 * HALF, F32, after)
             for t in range(4):
-                if (t, half) != REPEATED_SLICE:
+                n = KEPT_ENTRIES.get((t, half), HALF)
+                if n:
                     bank = next_bank()
-                    seller_pass(bank[:], w2q[0], t, HALF * half, HALF, True, True)
-                    nc.scalar.copy(out=columns(kept[half], t), in_=bank[:])
+                    seller_pass(bank[:, 0:n], w2q[0], t, HALF * half, n, True, True)
+                    nc.scalar.copy(out=columns(kept[half], t)[:, 0:n], in_=bank[:, 0:n])
 
         def kept_logits(half, after=None):
             logits[half] = held("logits%d" % half, 4 * HALF, F32, after)
             for t in range(4):
                 bank = next_bank()
                 dst = columns(logits[half], t)
-                if (t, half) == REPEATED_SLICE:
-                    buyer_pass(bank[:], 0, t, HALF * half, HALF, True, False)
-                    seller_pass(bank[:], w2q[0], t, HALF * half, HALF, False, True)
-                    nc.scalar.copy(out=dst, in_=bank[:])
-                else:
-                    buyer_pass(bank[:], 0, t, HALF * half, HALF, True, True)
-                    nc.vector.tensor_tensor(dst, bank[:], columns(kept[half], t), ALU.add)
+                n = KEPT_ENTRIES.get((t, half), HALF)
+                buyer_pass(bank[:], 0, t, HALF * half, HALF, True, n == HALF)
+                if n < HALF:
+                    seller_pass(bank[:, n:HALF], w2q[0], t, HALF * half + n, HALF - n, False, True)
+                if n:
+                    nc.vector.tensor_tensor(dst[:, 0:n], bank[:, 0:n], columns(kept[half], t)[:, 0:n], ALU.add)
+                if n < HALF:
+                    nc.scalar.copy(out=dst[:, n:HALF], in_=bank[:, n:HALF])
 
         def gate_from_logits(half, after=None):
             gate[0, half] = held("gate0%d" % half, 4 * HALF, F32, after)
@@ -197,11 +199,15 @@ def tile_list_haggling_features_kernel(
                 gate[0, half][:].rearrange("p (s j e) -> p s j e", s=2, e=2),
                 logits[half][:].rearrange("p (s e j) -> p s j e", s=2, e=2), ACT.Sigmoid)
 
-        def gate_in_h_order(half, after=None):
-            gate[0, half] = held("gate0%d" % half, 4 * HALF, F32, after)
+        def gate_in_h_order(tile, first_unit):
+            for u in range(2):
+                plain_gate[first_unit + u] = tile[:, BANK * u:BANK * (u + 1)]
+            c0 = first_unit * UNIT // 4
             nc.scalar.activation(
-                gate[0, half][:].rearrange("p (c i t) -> p c t i", i=4, t=4),
-                logits[half][:].rearrange("p (t c i) -> p c t i", i=4, t=4), ACT.Sigmoid)
+                tile.rearrange("p (c i t) -> p c t i", i=4, t=4),
+                logits[1][:].rearrange("p (t c i) -> p c t i", i=4, t=4)[:, c0:c0 + UNIT // 2], ACT.Sigmoid)
+
+        plain_gate = {}
 
         def gate_from_banks(half, after=None):
             gate[1, half] = held("gate1%d" % half, 4 * HALF, F32, after)
@@ -249,21 +255,24 @@ def tile_list_haggling_features_kernel(
         h_tiles = {}
 
         def gated_unit(b, half, u):
-            layout = "p (j s e) -> p j s e" if (b, half) == (0, 1) else "p (s j e) -> p j s e"
+            if (b, half) == (0, 1):
+                factor = plain_gate[u].rearrange("p (j s e) -> p j s e", s=2, e=2)
+            else:
+                factor = gate[b, half][:].rearrange("p (s j e) -> p j s e", s=2, e=2)[:, UNIT * u:UNIT * (u + 1)]
             nc.vector.tensor_tensor(
                 h_rounded[b, half, u].rearrange("p (j s e) -> p j s e", s=2, e=2),
-                house_banks[b, half, u][:].rearrange("p (s e j) -> p j s e", s=2, e=2),
-                gate[b, half][:].rearrange(layout, s=2, e=2)[:, UNIT * u:UNIT * (u + 1)], ALU.mult)
+                house_banks[b, half, u][:].rearrange("p (s e j) -> p j s e", s=2, e=2), factor, ALU.mult)
 
-        def gated_unit_off_vector(b, half, u, staged, piece):
-            dst = h_rounded[b, half, u]
-            house = staged[:, BANK * u:BANK * (u + 1)]
+        def stage_unit(u, staged):
             nc.scalar.copy(
-                out=house.rearrange("p (j t) -> p j t", t=4), in_=house_banks[b, half, u][:].rearrange("p (t j) -> p j t", t=4))
-            for c0 in range(0, BANK, piece):
+                out=staged[:, BANK * u:BANK * (u + 1)].rearrange("p (j t) -> p j t", t=4),
+                in_=house_banks[0, 1, u][:].rearrange("p (t j) -> p j t", t=4))
+
+        def gated_unit_on_gpsimd(u, staged):
+            for c0 in (0, BANK // 2):
+                cols = slice(c0, c0 + BANK // 2)
                 nc.gpsimd.tensor_tensor(
-                    dst[:, c0:c0 + piece], house[:, c0:c0 + piece],
-                    gate[b, half][:, BANK * u + c0:BANK * u + c0 + piece], ALU.mult)
+                    h_rounded[0, 1, u][:, cols], staged[:, BANK * u:BANK * (u + 1)][:, cols], plain_gate[u][:, cols], ALU.mult)
 
         def quantise_h(b, half, after=None):
             codes, scales = held("h%d%d_codes" % (b, half), HALF, U32, after), held("h%d%d_scales" % (b, half), HALF, U8)
@@ -279,8 +288,8 @@ def tile_list_haggling_features_kernel(
             j0 = HALF * half
             bank = next_bank(which)
             res = held(slot_name("res", RESULT_SLOTS), BANK, F32)
-            repeated = b == 1 or (t, half) == REPEATED_SLICE
-            if repeated:
+            n = 0 if b == 1 else KEPT_ENTRIES.get((t, half), HALF)
+            if n == 0:
                 seller_pass(bank[:], w2_plain if b == 1 else w2q[0], t, j0, HALF, True, False)
             for a in range(2):
                 m0 = GROUP * a + P * t
@@ -288,13 +297,15 @@ def tile_list_haggling_features_kernel(
                 nc.tensor.matmul_mx(
                     out=bank[:], lhsT=w4_codes[b][:, m0:m0 + P].bitcast(FP8X4),
                     lhsT_scale=w4_planes[b][8 + 4 * a:P, P * t:P * (t + 1)],
-                    rhs=codes[:].bitcast(FP8X4), rhs_scale=scales[:],
-                    start=(a == 0 and not repeated), stop=(a == 1))
-            if repeated:
-                nc.scalar.activation(res[:], bank[:], ACT.Tanh)
-            else:
-                nc.vector.tensor_tensor(res[:], bank[:], columns(kept[half], t), ALU.add)
-                nc.scalar.activation(res[:], res[:], ACT.Tanh)
+                    rhs=codes[:].bitcast(FP8X4), rhs_scale=scales[:], start=(a == 0 and n > 0), stop=(a == 1))
+                if a == 0 and 0 < n < HALF:
+                    seller_pass(bank[:, n:HALF], w2q[0], t, j0 + n, HALF - n, False, False)
+            if n:
+                nc.vector.tensor_tensor(res[:, 0:n], bank[:, 0:n], columns(kept[half], t)[:, 0:n], ALU.add)
+            if n < HALF:
+                nc.scalar.activation(res[:, n:HALF], bank[:, n:HALF], ACT.Tanh)
+            if n:
+                nc.scalar.activation(res[:, 0:n], res[:, 0:n], ACT.Tanh)
             col = gains[b][:, t:t + 1]
             if gain_engine is nc.scalar:
                 nc.scalar.activation(res[:], res[:], ACT.Copy, scale=col)
@@ -386,18 +397,19 @@ def tile_list_haggling_features_kernel(
         r00 = round_on_gpsimd(rounded_tile("r00", "r20"), w3_raw00)
         house_w[0, 0] = gather_half("house_w0", house_tab0, U16, house_list, 0)
         w3q[0, 0] = quantise("w3_00", r00, None)
-        kept_logits(1, "r20")
+        house_w[0, 1] = gather_half("house_w0", house_tab0, U16, house_list, 1, "r20")
+        kept_logits(1, "house_tab0")
         gate_from_banks(1, "w3_raw00")
-        house_w[0, 1] = gather_half("house_w0", house_tab0, U16, house_list, 1)
         r10 = round_on_gpsimd(rounded_tile("r10"), w3_raw10)
         house_w[1, 0] = gather_half("house_w1", house_tab1, U16, house_list, 0)
         w3q[1, 0] = quantise("w3_10", r10)
-        house_w[1, 1] = gather_half("house_w1", house_tab1, U16, house_list, 1, "r10")
+        house_w[1, 1] = gather_half("house_w1", house_tab1, U16, house_list, 1, "w3_raw10")
         for u in range(4):
             house_pass(0, 0, u, 0, first_banks[u])
         for u in range(4):
             house_pass(0, 1, u, 0, second_banks[u])
-        r01 = round_shared(rounded_tile("r01"), w3_raw01, 256)
+        gate_in_h_order(held("early_gate", 2 * BANK, F32, None)[:], 0)
+        r01 = round_shared(rounded_tile("r01", "r10"), w3_raw01, 256)
         for u in range(4):
             house_pass(0, 0, u, 1)
         h_tile(0, 0, (0, 1))
@@ -417,11 +429,16 @@ def tile_list_haggling_features_kernel(
         w3q[1, 1] = quantise("w3_11", r11)
         w4_codes[0] = reorder("w4_codes0", w4_raw0, I32, 2 * GROUP, 4, nc.vector)
         quantise_h(0, 0, "r21")
-        gate_in_h_order(1, "w3_last1")
-        staged = held("staged", 4 * HALF, F32, "r20")
-        h_tile(0, 1, (0, 1, 2, 3))
+        late = held("late", 5 * BANK, F32, "w3_last1")
+        staged = late[:, 2 * BANK:5 * BANK]
+        for u in range(2):
+            stage_unit(u, staged)
+        gate_in_h_order(late[:, 0:2 * BANK], 2)
+        for u in range(2, 3):
+            stage_unit(u, staged)
+        h_tile(0, 1, (0, 1, 2, 3), "w3_raw01")
         for u in range(3):
-            gated_unit_off_vector(0, 1, u, staged, 256)
+            gated_unit_on_gpsimd(u, staged)
         h_tile(1, 0, (0, 1, 2, 3))
         for u in range(4):
             house_pass(1, 0, u, 1)
@@ -440,7 +457,7 @@ def tile_list_haggling_features_kernel(
         quantise_h(1, 1)
         quantise_h(0, 1)
         for t in range(4):
-            output_tile(0, t, 0, nc.gpsimd, first_banks[t])
+            output_tile(0, t, 0, nc.gpsimd if t < 3 else nc.vector, first_banks[t])
         for t in range(4):
             output_tile(0, t, 1, nc.vector, second_banks[t])
         for t in range(4):

@@ -20,7 +20,6 @@ P = 128
 BANK = 512
 GROUP = 512
 HALF = S // 2
-QUARTER = S // 4
 UNIT = S // 8
 BANKS = 8
 RESULT_SLOTS = 12
@@ -196,8 +195,8 @@ def tile_list_haggling_features_kernel(
         def gate_from_logits(half, after=None):
             gate[0, half] = held("gate0%d" % half, 4 * HALF, F32, after)
             nc.scalar.activation(
-                gate[0, half][:].rearrange("p (s j e) -> p s j e", s=2, e=2),
-                logits[half][:].rearrange("p (s e j) -> p s j e", s=2, e=2), ACT.Sigmoid)
+                gate[0, half][:].rearrange("p (c i t) -> p c t i", i=4, t=4),
+                logits[half][:].rearrange("p (t c i) -> p c t i", i=4, t=4), ACT.Sigmoid)
 
         def gate_in_h_order(tile, first_unit):
             for u in range(2):
@@ -211,17 +210,16 @@ def tile_list_haggling_features_kernel(
 
         def gate_from_banks(half, after=None):
             gate[1, half] = held("gate1%d" % half, 4 * HALF, F32, after)
-            for c0 in (0, QUARTER):
-                for s in range(2):
-                    bank = next_bank()
-                    j0 = HALF * half + c0
-                    for e in range(2):
-                        buyer_pass(bank[:, QUARTER * e:QUARTER * (e + 1)], 1, 2 * s + e, j0, QUARTER, e == 0, False)
-                    for e in range(2):
-                        seller_pass(bank[:, QUARTER * e:QUARTER * (e + 1)], w2q[1], 2 * s + e, j0, QUARTER, False, e == 1)
-                    nc.scalar.activation(
-                        gate[1, half][:].rearrange("p (s j e) -> p s j e", s=2, e=2)[:, s, c0:c0 + QUARTER, :],
-                        bank[:].rearrange("p (e j) -> p j e", e=2), ACT.Sigmoid)
+            for u in range(4):
+                bank = next_bank()
+                j0 = HALF * half + UNIT * u
+                for t in range(4):
+                    buyer_pass(bank[:, UNIT * t:UNIT * (t + 1)], 1, t, j0, UNIT, t == 0, False)
+                for t in range(4):
+                    seller_pass(bank[:, UNIT * t:UNIT * (t + 1)], w2q[1], t, j0, UNIT, False, t == 3)
+                nc.scalar.activation(
+                    gate[1, half][:, BANK * u:BANK * (u + 1)].rearrange("p (j t) -> p j t", t=4),
+                    bank[:].rearrange("p (t j) -> p j t", t=4), ACT.Sigmoid)
 
         def restore_order(plain, ordered, engine, pieces):
             for m0 in range(0, P, P // pieces):
@@ -255,13 +253,11 @@ def tile_list_haggling_features_kernel(
         h_tiles = {}
 
         def gated_unit(b, half, u):
-            if (b, half) == (0, 1):
-                factor = plain_gate[u].rearrange("p (j s e) -> p j s e", s=2, e=2)
-            else:
-                factor = gate[b, half][:].rearrange("p (s j e) -> p j s e", s=2, e=2)[:, UNIT * u:UNIT * (u + 1)]
+            factor = plain_gate[u] if (b, half) == (0, 1) else gate[b, half][:, BANK * u:BANK * (u + 1)]
             nc.vector.tensor_tensor(
-                h_rounded[b, half, u].rearrange("p (j s e) -> p j s e", s=2, e=2),
-                house_banks[b, half, u][:].rearrange("p (s e j) -> p j s e", s=2, e=2), factor, ALU.mult)
+                h_rounded[b, half, u].rearrange("p (j t) -> p j t", t=4),
+                house_banks[b, half, u][:].rearrange("p (t j) -> p j t", t=4),
+                factor.rearrange("p (j t) -> p j t", t=4), ALU.mult)
 
         def stage_unit(u, staged):
             nc.scalar.copy(
@@ -396,20 +392,20 @@ def tile_list_haggling_features_kernel(
         gate_from_logits(0, "w2_raw1")
         r00 = round_on_gpsimd(rounded_tile("r00", "r20"), w3_raw00)
         house_w[0, 0] = gather_half("house_w0", house_tab0, U16, house_list, 0)
-        w3q[0, 0] = quantise("w3_00", r00, None)
-        house_w[0, 1] = gather_half("house_w0", house_tab0, U16, house_list, 1, "r20")
-        kept_logits(1, "house_tab0")
+        house_w[0, 1] = gather_half("house_w0", house_tab0, U16, house_list, 1)
+        w3q[0, 0] = quantise("w3_00", r00, "house_tab0")
+        kept_logits(1, "r20")
         gate_from_banks(1, "w3_raw00")
         r10 = round_on_gpsimd(rounded_tile("r10"), w3_raw10)
         house_w[1, 0] = gather_half("house_w1", house_tab1, U16, house_list, 0)
         w3q[1, 0] = quantise("w3_10", r10)
-        house_w[1, 1] = gather_half("house_w1", house_tab1, U16, house_list, 1, "w3_raw10")
+        house_w[1, 1] = gather_half("house_w1", house_tab1, U16, house_list, 1, "r10")
         for u in range(4):
             house_pass(0, 0, u, 0, first_banks[u])
         for u in range(4):
             house_pass(0, 1, u, 0, second_banks[u])
         gate_in_h_order(held("early_gate", 2 * BANK, F32, None)[:], 0)
-        r01 = round_shared(rounded_tile("r01", "r10"), w3_raw01, 256)
+        r01 = round_shared(rounded_tile("r01", None), w3_raw01, 256)
         for u in range(4):
             house_pass(0, 0, u, 1)
         h_tile(0, 0, (0, 1))

@@ -20,6 +20,7 @@ P = 128
 BANK = 512
 GROUP = 512
 HALF = S // 2
+QUARTER = S // 4
 UNIT = S // 8
 BANKS = 8
 RESULT_SLOTS = 12
@@ -62,10 +63,10 @@ def tile_list_haggling_features_kernel(
             rows = scales.rearrange("a s t -> (a s) t")
             nc.sync.dma_start(out=tile[0:P:P // rows.shape[0], :], in_=rows.bitcast(I32))
 
-        def place_rows(plane, picked, first, step):
+        def place_rows(plane, picked, first, step, queue):
             for i in range(4):
                 src = picked[:].bitcast(I32)[first + step * i:first + 16 * step:4 * step, :]
-                nc.sync.dma_start(out=plane[i:P:32, :], in_=src)
+                queue.dma_start(out=plane[i:P:32, :], in_=src)
 
         def load_w4_planes(tile):
             for quad in (0, 2, 1, 3):
@@ -195,8 +196,8 @@ def tile_list_haggling_features_kernel(
         def gate_from_logits(half, after=None):
             gate[0, half] = held("gate0%d" % half, 4 * HALF, F32, after)
             nc.scalar.activation(
-                gate[0, half][:].rearrange("p (c i t) -> p c t i", i=4, t=4),
-                logits[half][:].rearrange("p (t c i) -> p c t i", i=4, t=4), ACT.Sigmoid)
+                gate[0, half][:].rearrange("p (s j e) -> p s j e", s=2, e=2),
+                logits[half][:].rearrange("p (s e j) -> p s j e", s=2, e=2), ACT.Sigmoid)
 
         def gate_in_h_order(tile, first_unit):
             for u in range(2):
@@ -210,16 +211,17 @@ def tile_list_haggling_features_kernel(
 
         def gate_from_banks(half, after=None):
             gate[1, half] = held("gate1%d" % half, 4 * HALF, F32, after)
-            for u in range(4):
-                bank = next_bank()
-                j0 = HALF * half + UNIT * u
-                for t in range(4):
-                    buyer_pass(bank[:, UNIT * t:UNIT * (t + 1)], 1, t, j0, UNIT, t == 0, False)
-                for t in range(4):
-                    seller_pass(bank[:, UNIT * t:UNIT * (t + 1)], w2q[1], t, j0, UNIT, False, t == 3)
-                nc.scalar.activation(
-                    gate[1, half][:, BANK * u:BANK * (u + 1)].rearrange("p (j t) -> p j t", t=4),
-                    bank[:].rearrange("p (t j) -> p j t", t=4), ACT.Sigmoid)
+            for c0 in (0, QUARTER):
+                for s in range(2):
+                    bank = next_bank()
+                    j0 = HALF * half + c0
+                    for e in range(2):
+                        buyer_pass(bank[:, QUARTER * e:QUARTER * (e + 1)], 1, 2 * s + e, j0, QUARTER, e == 0, False)
+                    for e in range(2):
+                        seller_pass(bank[:, QUARTER * e:QUARTER * (e + 1)], w2q[1], 2 * s + e, j0, QUARTER, False, e == 1)
+                    nc.scalar.activation(
+                        gate[1, half][:].rearrange("p (s j e) -> p s j e", s=2, e=2)[:, s, c0:c0 + QUARTER, :],
+                        bank[:].rearrange("p (e j) -> p j e", e=2), ACT.Sigmoid)
 
         def restore_order(plain, ordered, engine, pieces):
             for m0 in range(0, P, P // pieces):
@@ -253,11 +255,13 @@ def tile_list_haggling_features_kernel(
         h_tiles = {}
 
         def gated_unit(b, half, u):
-            factor = plain_gate[u] if (b, half) == (0, 1) else gate[b, half][:, BANK * u:BANK * (u + 1)]
+            if (b, half) == (0, 1):
+                factor = plain_gate[u].rearrange("p (j s e) -> p j s e", s=2, e=2)
+            else:
+                factor = gate[b, half][:].rearrange("p (s j e) -> p j s e", s=2, e=2)[:, UNIT * u:UNIT * (u + 1)]
             nc.vector.tensor_tensor(
-                h_rounded[b, half, u].rearrange("p (j t) -> p j t", t=4),
-                house_banks[b, half, u][:].rearrange("p (t j) -> p j t", t=4),
-                factor.rearrange("p (j t) -> p j t", t=4), ALU.mult)
+                h_rounded[b, half, u].rearrange("p (j s e) -> p j s e", s=2, e=2),
+                house_banks[b, half, u][:].rearrange("p (s e j) -> p j s e", s=2, e=2), factor, ALU.mult)
 
         def stage_unit(u, staged):
             nc.scalar.copy(
@@ -339,8 +343,8 @@ def tile_list_haggling_features_kernel(
         seller_tab = load_words("seller_tab", tab2_words[0].rearrange("p t i -> p (t i)"))
         w1_codes = reorder("w1_codes", w1_raw, U16, H, 8, nc.vector)
         w1_ordered = reorder_on_gpsimd("w1_ordered", w1_rows, U8, H, 16, 512)
-        house_pair = zeroed("house_planes", 2 * S // 4, nc.gpsimd, "w1_rows")
-        w4_rows = zeroed("w4_rows", N // 4, nc.gpsimd, "w1_raw")
+        house_pair = zeroed("house_planes", 2 * S // 4, nc.vector)
+        w4_rows = zeroed("w4_rows", N // 4, nc.vector)
         house_planes = [house_pair[:, S // 4 * a:S // 4 * (a + 1)] for a in range(2)]
         house_plane = [plane.bitcast(U8) for plane in house_planes]
         pair_picked = held("pair_picked", 2 * S, U8)
@@ -348,15 +352,15 @@ def tile_list_haggling_features_kernel(
         gather_into(pair_picked[:, S:2 * S], buyer_rows, U8, buyer_list[:])
         house_picked = held("house_picked", S, U8)
         gather_into(house_picked[:], house_rows, U8, house_list[:])
-        place_rows(pair_planes, pair_picked, 0, 8)
+        place_rows(pair_planes, pair_picked, 0, 8, nc.sync)
         buyer_tab = load_words("buyer_tab", tab_words[0].rearrange("p t i -> p (t i)"))
-        place_rows(w1_planes, w1_ordered, 0, 8)
+        place_rows(w1_planes, w1_ordered, 0, 8, nc.gpsimd)
         w3_raw00 = load_weight("w3_raw00", w3, 0, 0)
         house_tab0 = load_words("house_tab0", tab3_words[0])
-        place_rows(house_planes[0], house_picked, 0, 4)
+        place_rows(house_planes[0], house_picked, 0, 4, nc.sync)
         w3_raw10 = load_weight("w3_raw10", w3, 1, 0)
         house_tab1 = load_words("house_tab1", tab3_words[1])
-        place_rows(house_planes[1], house_picked, 64, 4)
+        place_rows(house_planes[1], house_picked, 64, 4, nc.sync)
         w3_raw01 = load_weight("w3_raw01", w3, 0, GROUP)
         w3_last = [load_weight("w3_last%d" % e, w3, 1, GROUP + GROUP // 2 * e, GROUP // 2) for e in range(2)]
         w4_raw0 = load_w4(0)
@@ -453,7 +457,7 @@ def tile_list_haggling_features_kernel(
         quantise_h(1, 1)
         quantise_h(0, 1)
         for t in range(4):
-            output_tile(0, t, 0, nc.gpsimd if t < 3 else nc.vector, first_banks[t])
+            output_tile(0, t, 0, nc.vector, first_banks[t])
         for t in range(4):
             output_tile(0, t, 1, nc.vector, second_banks[t])
         for t in range(4):

from contextlib import ExitStack

import concourse.mybir as mybir

K, K3, H, N, T, T3, S = 512, 1024, 1024, 1024, 2048, 4096, 1024
FLOPS = 2 * S * (K * H + K * H + K3 * H + H * N)

F32 = mybir.dt.float32
BF16 = mybir.dt.bfloat16
I32 = mybir.dt.int32
U32 = mybir.dt.uint32
U16 = mybir.dt.uint16
U8 = mybir.dt.uint8
FP8X4 = mybir.dt.float8_e4m3fn_x4
FP4X4 = mybir.dt.float4_e2m1fn_x4
ACT = mybir.ActivationFunctionType
ALU = mybir.AluOpType

P = 128
BANK = 512
GROUP = 512
HALF = S // 2
QUARTER = S // 4
UNIT = S // 8
BANKS = 8
RESULT_SLOTS = 12
KEPT_ENTRIES = {(2, 1): 256, (3, 1): 0}


def tile_list_haggling_features_kernel(
    tc, tab_words, tab_scales, tab2_words, tab2_scales, tab3_words, tab3_scales,
    offs, offs2, offs3, w1_words, w1_scales, w2, w3, w4_words, w4_scales, gain, out,
):
    nc = tc.nc
    with ExitStack() as ctx:
        keep = ctx.enter_context(tc.tile_pool(name="keep", bufs=1))
        psum = ctx.enter_context(tc.psum_pool(name="psum", bufs=1))

        def held(name, cols, dtype, after=None):
            return keep.tile([P, cols], dtype, name=name, tag=after or name, align_bytes=64)

        turns = {}

        def slot_name(name, slots):
            turns[name] = turns.get(name, -1) + 1
            return "%s%d" % (name, turns[name] % slots)

        def next_bank(which=None):
            name = slot_name("bank", BANKS) if which is None else "bank%d" % which
            return psum.tile([P, BANK], F32, name=name)

        def zeroed(name, cols, engine, after=None):
            tile = held(name, cols, I32, after)
            engine.memset(tile[:], 0)
            return tile

        def load_list(name, entries):
            tile = keep.tile([P, S // 16], U16, name=name)
            nc.sync.dma_start(tile[:], entries)
            return tile

        def load_rows(tile, scales):
            rows = scales.rearrange("a s t -> (a s) t")
            nc.sync.dma_start(out=tile[0:P:P // rows.shape[0], :], in_=rows.bitcast(I32))

        def place_rows(plane, picked, first, step, queue):
            for i in range(4):
                src = picked[:].bitcast(I32)[first + step * i:first + 16 * step:4 * step, :]
                queue.dma_start(out=plane[i:P:32, :], in_=src)

        def load_w4_planes(tile):
            for quad in (0, 2, 1, 3):
                src = w4_scales[:, 4 * quad:4 * quad + 4, :]
                nc.sync.dma_start(out=tile[32 * quad + 8:32 * quad + 16, :], in_=src.bitcast(I32))

        def load_weight(name, w, a, c0, cols=GROUP, after=None):
            raw = held(name, 4 * cols, F32, after)
            rows = w[512 * a:512 * (a + 1), c0:c0 + cols]
            view = raw[:].rearrange("p (j c) -> p j c", j=4)
            nc.sync.dma_start(out=view, in_=rows.rearrange("(p j) c -> p j c", j=4))
            return view

        def load_words(name, words):
            table = held(name, T, I32)
            nc.sync.dma_start(out=table[:], in_=words.bitcast(I32))
            return table

        def load_w4(b, after=None):
            raw = held("w4_raw%d" % b, 2 * GROUP, I32, after)
            words = w4_words[:, :, GROUP * b:GROUP * (b + 1), :]
            nc.sync.dma_start(
                out=raw[:].rearrange("p (a c) -> p a c", a=2), in_=words.rearrange("a p c i -> p a (c i)").bitcast(I32))
            return raw

        def gather_into(dst, window, dtype, entries):
            nc.vector.tensor_copy(dst, window[:].bitcast(dtype).indirect(entries))

        def gather_half(name, window, dtype, lst, half, after=None):
            picked = held("%s%d" % (name, half), HALF, dtype, after)
            gather_into(picked[:], window, dtype, lst[:, HALF * half // 16:HALF * (half + 1) // 16])
            return picked

        def rounded_tile(name, after=None):
            return held(name, 4 * GROUP, BF16, after)

        def round_columns(rounded, raw, m0, engine):
            count = raw.shape[2] // 4
            dst = rounded[:].rearrange("p (t m j) -> p m j t", t=4, j=4)[:, m0:m0 + count, :, :]
            src = raw.rearrange("p j (m t) -> p m j t", t=4)
            if engine is nc.scalar:
                nc.scalar.copy(out=dst, in_=src)
            elif engine is nc.vector:
                nc.vector.tensor_copy(out=dst, in_=src)
            else:
                nc.gpsimd.tensor_scalar(
                    dst.rearrange("p m j t -> p m t j"), src.rearrange("p m j t -> p m t j"), 1.0, 0.0, ALU.mult, ALU.add)

        def round_group(name, raw, engine, after=None):
            rounded = rounded_tile(name, after)
            round_columns(rounded, raw, 0, engine)
            return rounded

        def quantise(name, rounded, after=None, scales=None):
            codes = held(name + "_codes", GROUP, U32, after)
            if scales is None:
                scales = held(name + "_scales", GROUP, U8)
            nc.vector.quantize_mx(out=codes[:].bitcast(FP8X4), scales=scales[:], in_=rounded[:])
            return codes, scales

        def round_on_gpsimd(rounded, raw, m0=0):
            for e in range(raw.shape[2] // P):
                round_columns(rounded, raw[:, :, P * e:P * (e + 1)], m0 + 32 * e, nc.gpsimd)
            return rounded

        def reorder(name, raw, dtype, cols, run, engine, after=None):
            ordered = held(name, cols, dtype, after)
            engine.tensor_copy(
                out=ordered[:].rearrange("p (b t c i) -> p b c t i", t=4, c=P // run, i=run),
                in_=raw[:].bitcast(dtype).rearrange("p (b c i t) -> p b c t i", t=4, c=P // run, i=run))
            return ordered

        def reorder_on_gpsimd(name, raw, dtype, cols, run, piece, after=None):
            ordered = held(name, cols, dtype, after)
            for b in range(cols // GROUP):
                dst = ordered[:].rearrange("p (b t c i) -> p b c t i", t=4, c=P // run, i=run)[:, b]
                src = raw[:].bitcast(dtype).rearrange("p (b c i t) -> p b c t i", t=4, c=P // run, i=run)[:, b]
                step = piece // (4 * run)
                for c0 in range(0, P // run, step):
                    nc.gpsimd.tensor_copy(out=dst[:, c0:c0 + step], in_=src[:, c0:c0 + step])
            return ordered

        w2q, w3q, seller_w, buyer_w, house_w, gate, kept, logits, hq, h_rounded = {}, {}, {}, {}, {}, {}, {}, {}, {}, {}

        def columns(tile, t):
            return tile[:, HALF * t:HALF * (t + 1)]

        def seller_pass(dst, weight, t, j0, n, start, stop):
            codes, scales = weight
            half, c0 = divmod(j0, HALF)
            nc.tensor.matmul_mx(
                out=dst, lhsT=codes[:, P * t:P * (t + 1)].bitcast(FP8X4), lhsT_scale=scales[:, P * t:P * (t + 1)],
                rhs=seller_w[half][:, c0:c0 + n].bitcast(FP8X4), rhs_scale=seller_plane[:, j0:j0 + n],
                start=start, stop=stop)

        def buyer_pass(dst, b, t, j0, n, start, stop):
            half, c0 = divmod(j0, HALF)
            m0 = GROUP * b + P * t
            nc.tensor.matmul_mx(
                out=dst, lhsT=w1_codes[:, m0:m0 + P].bitcast(FP4X4), lhsT_scale=w1_plane[:, m0:m0 + P],
                rhs=buyer_w[half][:, c0:c0 + n].bitcast(FP8X4), rhs_scale=buyer_plane[:, j0:j0 + n],
                start=start, stop=stop)

        def keep_seller(half, after=None):
            kept[half] = held("kept%d" % half, 4 * HALF, F32, after)
            for t in range(4):
                n = KEPT_ENTRIES.get((t, half), HALF)
                if n:
                    bank = next_bank()
                    seller_pass(bank[:, 0:n], w2q[0], t, HALF * half, n, True, True)
                    nc.scalar.copy(out=columns(kept[half], t)[:, 0:n], in_=bank[:, 0:n])

        def kept_logits(half, after=None):
            logits[half] = held("logits%d" % half, 4 * HALF, F32, after)
            for t in range(4):
                bank = next_bank()
                dst = columns(logits[half], t)
                n = KEPT_ENTRIES.get((t, half), HALF)
                buyer_pass(bank[:], 0, t, HALF * half, HALF, True, n == HALF)
                if n < HALF:
                    seller_pass(bank[:, n:HALF], w2q[0], t, HALF * half + n, HALF - n, False, True)
                if n:
                    nc.vector.tensor_tensor(dst[:, 0:n], bank[:, 0:n], columns(kept[half], t)[:, 0:n], ALU.add)
                if n < HALF:
                    nc.scalar.copy(out=dst[:, n:HALF], in_=bank[:, n:HALF])

        def gate_from_logits(half, after=None):
            gate[0, half] = held("gate0%d" % half, 4 * HALF, F32, after)
            nc.scalar.activation(
                gate[0, half][:].rearrange("p (s j e) -> p s j e", s=2, e=2),
                logits[half][:].rearrange("p (s e j) -> p s j e", s=2, e=2), ACT.Sigmoid)

        def gate_in_h_order(tile, first_unit):
            for u in range(2):
                plain_gate[first_unit + u] = tile[:, BANK * u:BANK * (u + 1)]
            c0 = first_unit * UNIT // 4
            nc.scalar.activation(
                tile.rearrange("p (c i t) -> p c t i", i=4, t=4),
                logits[1][:].rearrange("p (t c i) -> p c t i", i=4, t=4)[:, c0:c0 + UNIT // 2], ACT.Sigmoid)

        plain_gate = {}

        def gate_from_banks(half, after=None):
            gate[1, half] = held("gate1%d" % half, 4 * HALF, F32, after)
            for c0 in (0, QUARTER):
                for s in range(2):
                    bank = next_bank()
                    j0 = HALF * half + c0
                    for e in range(2):
                        buyer_pass(bank[:, QUARTER * e:QUARTER * (e + 1)], 1, 2 * s + e, j0, QUARTER, e == 0, False)
                    for e in range(2):
                        seller_pass(bank[:, QUARTER * e:QUARTER * (e + 1)], w2q[1], 2 * s + e, j0, QUARTER, False, e == 1)
                    nc.scalar.activation(
                        gate[1, half][:].rearrange("p (s j e) -> p s j e", s=2, e=2)[:, s, c0:c0 + QUARTER, :],
                        bank[:].rearrange("p (e j) -> p j e", e=2), ACT.Sigmoid)

        def restore_order(plain, ordered, engine, pieces):
            for m0 in range(0, P, P // pieces):
                engine.tensor_copy(
                    out=plain.rearrange("p (m t) -> p m t", t=4)[:, m0:m0 + P // pieces],
                    in_=ordered.rearrange("p (t m) -> p m t", t=4)[:, m0:m0 + P // pieces])
            return plain

        house_banks = {}

        def house_pass(b, half, u, a, which=None):
            if a == 0:
                house_banks[b, half, u] = next_bank(which)
            bank = house_banks[b, half, u]
            j0 = HALF * half + UNIT * u
            codes, scales = w3q[a, b]
            for t in range(4):
                nc.tensor.matmul_mx(
                    out=bank[:, UNIT * t:UNIT * (t + 1)],
                    lhsT=codes[:, P * t:P * (t + 1)].bitcast(FP8X4), lhsT_scale=scales[:, P * t:P * (t + 1)],
                    rhs=house_w[a, half][:, UNIT * u:UNIT * (u + 1)].bitcast(FP4X4),
                    rhs_scale=house_plane[a][:, j0:j0 + UNIT],
                    start=(a == 0 and t == 0), stop=(a == 1 and t == 3))

        def h_tile(b, half, units, after=None):
            tile = held("h%d%d%d" % (b, half, units[0]), BANK * len(units), BF16, after)
            h_tiles.setdefault((b, half), []).append((units, tile))
            for i, u in enumerate(units):
                h_rounded[b, half, u] = tile[:, BANK * i:BANK * (i + 1)]

        h_tiles = {}

        def gated_unit(b, half, u):
            if (b, half) == (0, 1):
                factor = plain_gate[u].rearrange("p (j s e) -> p j s e", s=2, e=2)
            else:
                factor = gate[b, half][:].rearrange("p (s j e) -> p j s e", s=2, e=2)[:, UNIT * u:UNIT * (u + 1)]
            nc.vector.tensor_tensor(
                h_rounded[b, half, u].rearrange("p (j s e) -> p j s e", s=2, e=2),
                house_banks[b, half, u][:].rearrange("p (s e j) -> p j s e", s=2, e=2), factor, ALU.mult)

        def stage_unit(u, staged):
            nc.scalar.copy(
                out=staged[:, BANK * u:BANK * (u + 1)].rearrange("p (j t) -> p j t", t=4),
                in_=house_banks[0, 1, u][:].rearrange("p (t j) -> p j t", t=4))

        def gated_unit_on_gpsimd(u, staged):
            for c0 in (0, BANK // 2):
                cols = slice(c0, c0 + BANK // 2)
                nc.gpsimd.tensor_tensor(
                    h_rounded[0, 1, u][:, cols], staged[:, BANK * u:BANK * (u + 1)][:, cols], plain_gate[u][:, cols], ALU.mult)

        def quantise_h(b, half, after=None):
            codes, scales = held("h%d%d_codes" % (b, half), HALF, U32, after), held("h%d%d_scales" % (b, half), HALF, U8)
            for units, tile in h_tiles[b, half]:
                entries = slice(UNIT * units[0], UNIT * (units[-1] + 1))
                nc.vector.quantize_mx(out=codes[:, entries].bitcast(FP8X4), scales=scales[:, entries], in_=tile[:])
            hq[b, half] = codes, scales

        out_rows = [out[0:GROUP, :].rearrange("(p t) j -> p t j", t=4), out[GROUP:N, :].rearrange("(t p) j -> p t j", t=4)]
        w4_codes, w4_planes = {}, {}

        def output_tile(b, t, half, gain_engine, which):
            j0 = HALF * half
            bank = next_bank(which)
            res = held(slot_name("res", RESULT_SLOTS), BANK, F32)
            n = 0 if b == 1 else KEPT_ENTRIES.get((t, half), HALF)
            if n == 0:
                seller_pass(bank[:], w2_plain if b == 1 else w2q[0], t, j0, HALF, True, False)
            for a in range(2):
                m0 = GROUP * a + P * t
                codes, scales = hq[a, half]
                nc.tensor.matmul_mx(
                    out=bank[:], lhsT=w4_codes[b][:, m0:m0 + P].bitcast(FP8X4),
                    lhsT_scale=w4_planes[b][8 + 4 * a:P, P * t:P * (t + 1)],
                    rhs=codes[:].bitcast(FP8X4), rhs_scale=scales[:], start=(a == 0 and n > 0), stop=(a == 1))
                if a == 0 and 0 < n < HALF:
                    seller_pass(bank[:, n:HALF], w2q[0], t, j0 + n, HALF - n, False, False)
            if n:
                nc.vector.tensor_tensor(res[:, 0:n], bank[:, 0:n], columns(kept[half], t)[:, 0:n], ALU.add)
            if n < HALF:
                nc.scalar.activation(res[:, n:HALF], bank[:, n:HALF], ACT.Tanh)
            if n:
                nc.scalar.activation(res[:, 0:n], res[:, 0:n], ACT.Tanh)
            col = gains[b][:, t:t + 1]
            if gain_engine is nc.scalar:
                nc.scalar.activation(res[:], res[:], ACT.Copy, scale=col)
            else:
                gain_engine.tensor_scalar(res[:], res[:], col, 0.0, ALU.mult, ALU.add)
            nc.sync.dma_start(out=out_rows[b][:, t, j0:j0 + HALF], in_=res[:])

        seller_rows = zeroed("seller_rows", T // 4, nc.vector)
        buyer_rows = zeroed("buyer_rows", T // 4, nc.vector)
        w1_rows = zeroed("w1_rows", H // 4, nc.vector)
        house_rows = zeroed("house_rows", T3 // 4, nc.vector)

        warm = held("warm", 8, F32)
        nc.vector.memset(warm[:], 0.0)
        nc.scalar.activation(warm[:, 1:2], warm[:, 0:1], ACT.Sigmoid)

        pair_planes = zeroed("pair_planes", 2 * S // 4, nc.vector)
        w1_planes = zeroed("w1_plane", H // 4, nc.vector)
        w21_scales = zeroed("w21_scales", GROUP // 4, nc.vector)
        seller_plane = pair_planes[:].bitcast(U8)[:, 0:S]
        buyer_plane = pair_planes[:].bitcast(U8)[:, S:2 * S]
        w1_plane = w1_planes[:].bitcast(U8)

        seller_list = load_list("seller_list", offs2)
        w1_raw = held("w1_raw", H // 2, I32)
        nc.sync.dma_start(out=w1_raw[:], in_=w1_words[0].bitcast(I32))
        load_rows(seller_rows, tab2_scales)
        buyer_list = load_list("buyer_list", offs)
        load_rows(buyer_rows, tab_scales)
        load_rows(w1_rows, w1_scales)
        w2_raw = [load_weight("w2_raw0", w2, 0, 0)]
        house_list = load_list("house_list", offs3)
        load_rows(house_rows, tab3_scales)
        w2_raw.append(load_weight("w2_raw1", w2, 0, GROUP))
        seller_tab = load_words("seller_tab", tab2_words[0].rearrange("p t i -> p (t i)"))
        w1_codes = reorder("w1_codes", w1_raw, U16, H, 8, nc.vector)
        w1_ordered = reorder_on_gpsimd("w1_ordered", w1_rows, U8, H, 16, 512)
        house_pair = zeroed("house_planes", 2 * S // 4, nc.vector)
        w4_rows = zeroed("w4_rows", N // 4, nc.vector)
        house_planes = [house_pair[:, S // 4 * a:S // 4 * (a + 1)] for a in range(2)]
        house_plane = [plane.bitcast(U8) for plane in house_planes]
        pair_picked = held("pair_picked", 2 * S, U8)
        gather_into(pair_picked[:, 0:S], seller_rows, U8, seller_list[:])
        gather_into(pair_picked[:, S:2 * S], buyer_rows, U8, buyer_list[:])
        house_picked = held("house_picked", S, U8)
        gather_into(house_picked[:], house_rows, U8, house_list[:])
        place_rows(pair_planes, pair_picked, 0, 8, nc.sync)
        buyer_tab = load_words("buyer_tab", tab_words[0].rearrange("p t i -> p (t i)"))
        place_rows(w1_planes, w1_ordered, 0, 8, nc.gpsimd)
        w3_raw00 = load_weight("w3_raw00", w3, 0, 0)
        house_tab0 = load_words("house_tab0", tab3_words[0])
        place_rows(house_planes[0], house_picked, 0, 4, nc.sync)
        w3_raw10 = load_weight("w3_raw10", w3, 1, 0)
        house_tab1 = load_words("house_tab1", tab3_words[1])
        place_rows(house_planes[1], house_picked, 64, 4, nc.sync)
        w3_raw01 = load_weight("w3_raw01", w3, 0, GROUP)
        w3_last = [load_weight("w3_last%d" % e, w3, 1, GROUP + GROUP // 2 * e, GROUP // 2) for e in range(2)]
        w4_raw0 = load_w4(0)
        w4_codes[1] = load_w4(1)
        load_w4_planes(w4_rows)
        gains = [held("gains%d" % b, 8, F32) for b in range(2)]
        with nc.allow_non_contiguous_dma(reason="one gain a partition and slice"):
            nc.sync.dma_start(out=gains[1][:, 0:4], in_=gain[GROUP:N].rearrange("(t p) -> p t", t=4))
        nc.sync.dma_start(out=gains[0][:, 0:4], in_=gain[0:GROUP].rearrange("(p t) -> p t", t=4))
        w4_planes[1] = w4_rows[:].bitcast(U8)[:, GROUP:N]

        first_banks, second_banks = (7, 0, 1, 2), (3, 4, 5, 6)

        def round_shared(rounded, raw, gpsimd_cols, m0=0):
            round_on_gpsimd(rounded, raw[:, :, 0:gpsimd_cols], m0)
            round_columns(rounded, raw[:, :, gpsimd_cols:raw.shape[2]], m0 + gpsimd_cols // 4, nc.scalar)
            return rounded

        r20 = round_group("r20", w2_raw[0], nc.scalar)
        r21 = round_shared(rounded_tile("r21"), w2_raw[1], 128)
        w2q[0] = quantise("w2_0", r20, "house_rows")
        w2q[1] = quantise("w2_1", r21, None, w21_scales[:].bitcast(U8))
        for half in range(2):
            seller_w[half] = gather_half("seller_w", seller_tab, U32, seller_list, half)
        for half in range(2):
            keep_seller(half)
        w2_plain = (restore_order(held("w2_plain", GROUP, U32)[:], w2q[1][0][:], nc.gpsimd, 1),
                    restore_order(held("w2_plain_scales", GROUP, U8)[:], w2q[1][1], nc.gpsimd, 1))
        for half in range(2):
            buyer_w[half] = gather_half("buyer_w", buyer_tab, U32, buyer_list, half)
        kept_logits(0, "w2_raw0")
        gate_from_banks(0, "seller_tab")
        gate_from_logits(0, "w2_raw1")
        r00 = round_on_gpsimd(rounded_tile("r00", "r20"), w3_raw00)
        house_w[0, 0] = gather_half("house_w0", house_tab0, U16, house_list, 0)
        house_w[0, 1] = gather_half("house_w0", house_tab0, U16, house_list, 1)
        w3q[0, 0] = quantise("w3_00", r00, "house_tab0")
        kept_logits(1, "r20")
        gate_from_banks(1, "w3_raw00")
        r10 = round_on_gpsimd(rounded_tile("r10"), w3_raw10)
        house_w[1, 0] = gather_half("house_w1", house_tab1, U16, house_list, 0)
        w3q[1, 0] = quantise("w3_10", r10)
        house_w[1, 1] = gather_half("house_w1", house_tab1, U16, house_list, 1, "r10")
        for u in range(4):
            house_pass(0, 0, u, 0, first_banks[u])
        for u in range(4):
            house_pass(0, 1, u, 0, second_banks[u])
        gate_in_h_order(held("early_gate", 2 * BANK, F32, None)[:], 0)
        r01 = round_shared(rounded_tile("r01", None), w3_raw01, 256)
        for u in range(4):
            house_pass(0, 0, u, 1)
        h_tile(0, 0, (0, 1))
        for u in range(2):
            gated_unit(0, 0, u)
        w3q[0, 1] = quantise("w3_01", r01)
        h_tile(0, 0, (2, 3), "w3_raw01")
        for u in range(2, 4):
            gated_unit(0, 0, u)
        for u in range(4):
            house_pass(0, 1, u, 1)
        r11 = rounded_tile("r11", "r21")
        round_columns(r11, w3_last[0], 0, nc.scalar)
        round_columns(r11, w3_last[1], 64, nc.scalar)
        for u in range(4):
            house_pass(1, 0, u, 0, first_banks[u])
        w3q[1, 1] = quantise("w3_11", r11)
        w4_codes[0] = reorder("w4_codes0", w4_raw0, I32, 2 * GROUP, 4, nc.vector)
        quantise_h(0, 0, "r21")
        late = held("late", 5 * BANK, F32, "w3_last1")
        staged = late[:, 2 * BANK:5 * BANK]
        for u in range(2):
            stage_unit(u, staged)
        gate_in_h_order(late[:, 0:2 * BANK], 2)
        for u in range(2, 3):
            stage_unit(u, staged)
        h_tile(0, 1, (0, 1, 2, 3), "w3_raw01")
        for u in range(3):
            gated_unit_on_gpsimd(u, staged)
        h_tile(1, 0, (0, 1, 2, 3))
        for u in range(4):
            house_pass(1, 0, u, 1)
            gated_unit(1, 0, u)
        quantise_h(1, 0)
        for u in range(3, 4):
            gated_unit(0, 1, u)
        w4_planes[0] = reorder("w4_plane0", w4_rows[:, 0:GROUP // 4], U8, GROUP, 16, nc.vector, "h100")
        for u in range(4):
            house_pass(1, 1, u, 0, second_banks[u])
            house_pass(1, 1, u, 1)
        h_tile(1, 1, (0, 1, 2, 3))
        for u in range(4):
            gated_unit(1, 1, u)
            output_tile(1, u, 0, nc.scalar if u < 2 else nc.gpsimd, first_banks[u])
        quantise_h(1, 1)
        quantise_h(0, 1)
        for t in range(4):
            output_tile(0, t, 0, nc.vector, first_banks[t])
        for t in range(4):
            output_tile(0, t, 1, nc.vector, second_banks[t])
        for t in range(4):
            output_tile(1, t, 1, nc.vector, first_banks[t])
